import numpy as np
import ml_dtypes


def mxq(x, axis, fmt="e4m3"):
    dtype, down = {"e4m3": (ml_dtypes.float8_e4m3fn, 7), "e5m2": (ml_dtypes.float8_e5m2, 14)}[fmt]
    v = np.moveaxis(np.asarray(x, np.float32).astype(ml_dtypes.bfloat16).astype(np.float64), axis, -1)
    blocks = v.reshape(v.shape[:-1] + (-1, 32))
    amax = np.abs(blocks).max(-1, keepdims=True)
    byte = np.maximum(np.where(amax > 0, np.frexp(amax)[1] - 1 + 127, 0) - down, 1)
    scale = np.exp2(byte - 127.0)
    codes = (blocks / scale).astype(np.float32).astype(dtype).astype(np.float64)
    return np.moveaxis((codes * scale).reshape(v.shape), -1, axis)


WIDE = False


def mx_kscale(k):
    if not WIDE:
        return np.ones(k)
    levels = np.array([10, -10, 5, -5, 0])
    if k % 512:
        return np.exp2(np.random.permutation(np.resize(levels, k // 32))).repeat(32)
    a = np.empty((k // 512, 16))
    for p in range(k // 512):
        a[p, :8] = np.random.permutation(np.resize(levels, 8))
        for g in range(8):
            far = levels[np.abs(levels - a[p, g]) >= 10]
            a[p, g + 8] = far[np.random.randint(len(far))]
    return np.exp2(a.ravel()).repeat(32)


def f64(x):
    return np.asarray(x).astype(np.float64)


def striped(idx):
    return np.tile(idx.reshape(-1, 16).T, (8, 1)).astype(np.uint16)


def unstriped(offs):
    return offs[:16].T.reshape(-1).astype(np.int64)


E2M1 = np.array([0.0, 0.5, 1.0, 1.5, 2.0, 3.0, 4.0, 6.0, -0.0, -0.5, -1.0, -1.5, -2.0, -3.0, -4.0, -6.0])


def pack_weight(w, fmt):
    k, n = w.shape
    w = f64(np.asarray(w, np.float32).astype(ml_dtypes.bfloat16)).reshape(k // 32, 32, n)
    amax = np.abs(w).max(1)
    if fmt == "e4m3":
        byte = np.frexp(amax)[1] - 1 + 127 - 7
    else:
        mant, ex = np.frexp(amax / 6.0)
        byte = np.where(mant > 0.5, ex, ex - 1) + 127
    byte = np.clip(np.where(amax > 0, byte, 1), 1, 254)
    scaled = (w * np.exp2(127.0 - byte)[:, None, :]).reshape(k, n).astype(np.float32)
    by_word = np.ascontiguousarray(scaled.reshape(k // 512, 128, 4, n).transpose(0, 1, 3, 2))
    if fmt == "e4m3":
        words = by_word.astype(ml_dtypes.float8_e4m3fn).view(np.uint8)
    else:
        c = by_word.astype(ml_dtypes.float4_e2m1fn).view(np.uint8) & 0xF
        words = (c[..., 0::2] | (c[..., 1::2] << 4)).reshape(k // 512, 128, 2 * n)
    return np.ascontiguousarray(words), np.ascontiguousarray(byte.astype(np.uint8).reshape(k // 512, 16, n))


def unpack_weight(words, scales, fmt):
    g, _, n = scales.shape
    words = np.ascontiguousarray(words).reshape(g, 128, n, -1)
    if fmt == "e4m3":
        vals = words.view(ml_dtypes.float8_e4m3fn).astype(np.float64)
    else:
        nib = np.empty((g, 128, n, 4), np.uint8)
        nib[..., 0::2] = words & 0xF
        nib[..., 1::2] = words >> 4
        vals = E2M1[nib]
    vals = vals * np.repeat(np.exp2(scales.astype(np.float64) - 127.0), 8, axis=1)[..., None]
    return vals.transpose(0, 1, 3, 2).reshape(g * 512, n)


def gelu(v):
    return 0.5 * v * (1.0 + np.tanh(np.sqrt(2.0 / np.pi) * (v + 0.044715 * v**3)))


def bf(x):
    return np.asarray(x, np.float32).astype(ml_dtypes.bfloat16)

def planes(Y):
    n, m = Y.shape
    b = f64(bf(Y)).reshape(n // 32, 32, m)
    amax = np.abs(b).max(1)
    byte = np.clip(np.where(amax > 0, np.frexp(amax)[1] - 1 + 127 - 7, 1), 1, 254)
    codes = (b * np.exp2(127.0 - byte)[:, None, :]).reshape(n, m).astype(np.float32).astype(ml_dtypes.float8_e4m3fn).view(np.uint8)
    words = codes.reshape(n // 512, 128, 4, m).transpose(0, 1, 3, 2)
    return np.ascontiguousarray(words), np.ascontiguousarray(byte.astype(np.uint8).reshape(n // 512, 16, m))


K, T, S, H, N = 1536, 2048, 1024, 512, 1024

def setup_inputs():
    n = np.random.standard_normal
    s = mx_kscale(K)[:, None]
    u = mx_kscale(H)[:, None]
    d = {}
    d["tab_words"], d["tab_scales"] = pack_weight(n((K, T)) * s, "e4m3")
    d["offs"] = striped(np.random.permutation(T)[:S])
    d["w1"] = (n((K, H)) / np.sqrt(K) / s * u.T).astype(np.float32)
    d["b1"] = ((0.5 + 0.3 * n(H)) * u[:, 0]).astype(np.float32)
    d["gT"] = (0.9 * np.exp(0.5 * n((H, T))) * u).astype(np.float32)
    d["w4_words"], d["w4_scales"] = pack_weight(1.5 * n((H, N)) / np.sqrt(H) / u, "e2m1")
    d["wc"] = (2.0 * n((H, N)) / np.sqrt(H) / u * np.exp(0.8 * n(N))).astype(np.float32)
    return d

def reference(tab_words, tab_scales, offs, w1, b1, gT, w4_words, w4_scales, wc):
    v = unpack_weight(tab_words, tab_scales, "e4m3")[:, unstriped(offs)]
    g = f64(gT)[:, unstriped(offs)]
    w4 = unpack_weight(w4_words, w4_scales, "e2m1")
    dem = np.maximum((mxq(f64(w1), 0, "e4m3").T @ v) + f64(b1)[:, None], 0.0)
    hq = mxq(np.minimum(dem, g), 0, "e4m3")
    route = w4.T @ hq
    cost = mxq(f64(wc), 0, "e4m3").T @ hq
    y = cost * (1.0 / (1.0 + np.exp(-route)))
    words, scales = planes(y)
    return y, words, scales

@@ -1,0 +1,240 @@
+from contextlib import ExitStack
+
+import concourse.mybir as mybir
+
+K, T, S, H, N = 1536, 2048, 1024, 512, 1024
+FLOPS = 2 * K * H * S + 2 * 2 * H * N * S
+
+F32 = mybir.dt.float32
+BF16 = mybir.dt.bfloat16
+I32 = mybir.dt.int32
+U32 = mybir.dt.uint32
+U16 = mybir.dt.uint16
+U8 = mybir.dt.uint8
+FP8X4 = mybir.dt.float8_e4m3fn_x4
+FP4X4 = mybir.dt.float4_e2m1fn_x4
+ACT = mybir.ActivationFunctionType
+ALU = mybir.AluOpType
+
+P = 128
+PACK = 4
+K_PASS = P * PACK
+PASSES = K // K_PASS
+GROUPS = N // K_PASS
+BANK = 512
+CHUNK = 256
+CHUNKS = S // CHUNK
+RUN = 2
+
+
+def tile_list_order_lane_cost_kernel(
+    tc, tab_words, tab_scales, offs, w1, b1, gT, w4_words, w4_scales, wc, out_0, out_1, out_2
+):
+    nc = tc.nc
+    with ExitStack() as ctx:
+        keep = ctx.enter_context(tc.tile_pool(name="keep", bufs=1))
+        ring = ctx.enter_context(tc.tile_pool(name="ring", bufs=1))
+        psum = ctx.enter_context(tc.psum_pool(name="psum", bufs=4))
+
+        offsets = keep.tile([P, S // 16], U16, name="offsets")
+        bias = keep.tile([P, PACK], F32, name="bias")
+        table = [keep.tile([P, T], U32, name="table%d" % a) for a in range(PASSES)]
+        table_sc = keep.tile([P, T], U8, name="table_sc")
+        picked = [keep.tile([P, S], U32, name="picked%d" % a, align_bytes=64) for a in range(PASSES)]
+        picked_sc = keep.tile([P, S], U8, name="picked_sc", align_bytes=64)
+        stock = [keep.tile([P, T], F32, name="stock%d" % t) for t in range(PACK)]
+        stock_picked = keep.tile([P, PACK, S], F32, name="stock_picked")
+        w4_raw = keep.tile([P, 2 * N], U8, name="w4_raw")
+        w4_sc_raw = keep.tile([P, N], U8, name="w4_sc_raw")
+        w4_codes = keep.tile([P, 2 * N], U8, name="w4_codes", align_bytes=64)
+        w4_sc = keep.tile([P, N], U8, name="w4_sc", align_bytes=64)
+        h_codes = keep.tile([P, S], U32, name="h_codes", align_bytes=64)
+        h_sc = keep.tile([P, S], U8, name="h_sc", align_bytes=64)
+        y_codes = [keep.tile([P, S], U32, name="y_codes%d" % g, align_bytes=64) for g in range(GROUPS)]
+        y_sc = keep.tile([P, GROUPS * S], U8, name="y_sc", align_bytes=64)
+        warm = keep.tile([P, 8], F32, name="warm")
+
+        nc.gpsimd.memset(table_sc[:].bitcast(I32), 0)
+        nc.gpsimd.memset(w4_sc_raw[:].bitcast(I32), 0)
+        nc.vector.memset(warm[:, 0:4], 0.0)
+        nc.scalar.activation(out=warm[:, 4:8], in_=warm[:, 0:4], func=ACT.Sigmoid)
+
+        def load_table(a):
+            src = tab_words[a].rearrange("p n i -> p (n i)").bitcast(I32)
+            nc.sync.dma_start(out=table[a][:].bitcast(I32), in_=src)
+
+        def gather_table(a):
+            nc.vector.tensor_copy(out=picked[a][:], in_=table[a][:].indirect(offsets[:]))
+
+        def load_stock(t):
+            nc.sync.dma_start(out=stock[t][:], in_=gT.rearrange("(p t) c -> t p c", t=PACK)[t])
+
+        def gather_stock(t):
+            nc.vector.tensor_copy(out=stock_picked[:, t, :], in_=stock[t][:].indirect(offsets[:]))
+
+        def load_weight(rows):
+            raw = ring.tile([P, PACK, K_PASS], F32, name="raw", bufs=3)
+            nc.sync.dma_start(out=raw[:], in_=rows.rearrange("(p j) c -> p j c", j=PACK))
+            return raw
+
+        def quantise_weight(raw, name):
+            rounded = ring.tile([P, PACK * K_PASS], BF16, name="w_rounded", bufs=2, align_bytes=64)
+            nc.scalar.copy(
+                out=rounded[:].rearrange("p (t m j) -> p m j t", t=PACK, j=PACK),
+                in_=raw[:].rearrange("p j (m t) -> p m j t", t=PACK),
+            )
+            codes = keep.tile([P, K_PASS], U32, name=name + "_codes", align_bytes=64)
+            scales = keep.tile([P, K_PASS], U8, name=name + "_sc", align_bytes=64)
+            nc.vector.quantize_mx(out=codes[:].bitcast(FP8X4), scales=scales[:], in_=rounded[:])
+            return codes, scales
+
+        acc = [[psum.tile([P, BANK], F32, name=tag) for t in range(PACK)] for tag in ("route", "cost")]
+
+        def first_product(a, weight):
+            codes, scales = weight
+            for half in range(S // BANK):
+                cols = slice(half * BANK, (half + 1) * BANK)
+                for t in range(PACK):
+                    m = slice(t * P, (t + 1) * P)
+                    nc.tensor.matmul_mx(
+                        out=acc[half][t][:],
+                        lhsT=codes[:, m].bitcast(FP8X4),
+                        lhsT_scale=scales[:, m],
+                        rhs=picked[a][:, cols].bitcast(FP8X4),
+                        rhs_scale=picked_sc[4 * a :, cols],
+                        start=(a == 0),
+                        stop=(a == PASSES - 1),
+                    )
+
+        def w1_rows(a):
+            return w1[a * K_PASS : (a + 1) * K_PASS, :]
+
+        load_table(0)
+        nc.sync.dma_start(offsets[:], offs)
+        load_table(1)
+        for q in range(4):
+            nc.sync.dma_start(
+                out=table_sc[32 * q : 32 * q + 4 * PASSES, :].bitcast(I32),
+                in_=tab_scales[:, 4 * q : 4 * q + 4, :].bitcast(I32),
+            )
+        gather_table(0)
+        gather_table(1)
+        nc.vector.tensor_copy(out=picked_sc[:], in_=table_sc[:].indirect(offsets[:]))
+        raw = load_weight(w1_rows(0))
+        first_product(0, quantise_weight(raw, "w1_0"))
+        load_table(2)
+        gather_table(2)
+
+        nc.sync.dma_start(out=w4_raw[:].bitcast(I32), in_=w4_words[0].bitcast(I32))
+        for q in range(4):
+            nc.sync.dma_start(
+                out=w4_sc_raw[32 * q : 32 * q + 4, :].bitcast(I32),
+                in_=w4_scales[0, 4 * q : 4 * q + 4, :].bitcast(I32),
+            )
+        nc.sync.dma_start(out=bias[:], in_=b1.rearrange("(p t) -> p t", t=PACK))
+        nc.vector.tensor_copy(
+            out=w4_codes[:].rearrange("p (g t m b) -> p g t m b", g=GROUPS, t=PACK, b=2),
+            in_=w4_raw[:].rearrange("p (g m t b) -> p g t m b", g=GROUPS, t=PACK, b=2),
+        )
+        nc.vector.tensor_copy(
+            out=w4_sc[:].rearrange("p (g t m) -> p g t m", g=GROUPS, t=PACK),
+            in_=w4_sc_raw[:].rearrange("p (g m t) -> p g t m", g=GROUPS, t=PACK),
+        )
+
+        raw = load_weight(w1_rows(1))
+        first_product(1, quantise_weight(raw, "w1_1"))
+        load_stock(0)
+        gather_stock(0)
+        raw = load_weight(w1_rows(2))
+        first_product(2, quantise_weight(raw, "w1_2"))
+        demand = [keep.tile([P, PACK, BANK], F32, name="demand%d" % half) for half in range(S // BANK)]
+        for half in range(S // BANK):
+            for t in range(PACK):
+                nc.scalar.activation(
+                    out=demand[half][:, t, :], in_=acc[half][t][:], func=ACT.Relu, bias=bias[:, t : t + 1]
+                )
+        for t in range(1, PACK):
+            load_stock(t)
+            gather_stock(t)
+        wc_raw = [load_weight(wc[:, g * K_PASS : (g + 1) * K_PASS]) for g in range(GROUPS)]
+
+        def pairs(planes):
+            return planes.rearrange("p t (c i) -> p c t i", i=RUN)
+
+        def woven(tile):
+            return tile[:].rearrange("p (c i t) -> p c t i", i=RUN, t=PACK)
+
+        def shipments(c):
+            cols = slice(c * CHUNK, (c + 1) * CHUNK)
+            half, c0 = divmod(c * CHUNK, BANK)
+            rounded = ring.tile([P, PACK * CHUNK], BF16, name="h_rounded", bufs=4, align_bytes=64)
+            nc.vector.tensor_tensor(
+                out=woven(rounded),
+                in0=pairs(demand[half][:, :, c0 : c0 + CHUNK]),
+                in1=pairs(stock_picked[:, :, cols]),
+                op=ALU.min,
+            )
+            nc.vector.quantize_mx(out=h_codes[:, cols].bitcast(FP8X4), scales=h_sc[:, cols], in_=rounded[:])
+
+        def lanes(g, c, weight):
+            wc_codes, wc_sc = weight
+            cols = slice(c * CHUNK, (c + 1) * CHUNK)
+            y = ring.tile([P, PACK, CHUNK], F32, name="y", bufs=5)
+            for t0 in range(0, PACK, 2):
+                route = psum.tile([P, 2, CHUNK], F32, name="route")
+                cost = psum.tile([P, 2, CHUNK], F32, name="cost")
+                for e in range(2):
+                    s = (g * PACK + t0 + e) * P
+                    nc.tensor.matmul_mx(
+                        out=route[:, e, :],
+                        lhsT=w4_codes[:, 2 * s : 2 * (s + P)].bitcast(FP4X4),
+                        lhsT_scale=w4_sc[:, s : s + P],
+                        rhs=h_codes[:, cols].bitcast(FP8X4),
+                        rhs_scale=h_sc[:, cols],
+                        start=True,
+                        stop=True,
+                    )
+                for e in range(2):
+                    m = slice((t0 + e) * P, (t0 + e + 1) * P)
+                    nc.tensor.matmul_mx(
+                        out=cost[:, e, :],
+                        lhsT=wc_codes[:, m].bitcast(FP8X4),
+                        lhsT_scale=wc_sc[:, m],
+                        rhs=h_codes[:, cols].bitcast(FP8X4),
+                        rhs_scale=h_sc[:, cols],
+                        start=True,
+                        stop=True,
+                    )
+                share = ring.tile([P, 2, CHUNK], F32, name="share", bufs=12)
+                nc.scalar.activation(out=share[:], in_=route[:], func=ACT.Sigmoid)
+                nc.vector.tensor_tensor(out=y[:, t0 : t0 + 2, :], in0=cost[:], in1=share[:], op=ALU.mult)
+            rows = out_0[g * K_PASS : (g + 1) * K_PASS, cols]
+            nc.sync.dma_start(out=rows.rearrange("(p t) c -> p t c", t=PACK), in_=y[:])
+            rounded = ring.tile([P, PACK * CHUNK], BF16, name="y_rounded", bufs=4, align_bytes=64)
+            if g == GROUPS - 1 and c >= CHUNKS - 1:
+                nc.vector.tensor_copy(out=woven(rounded), in_=pairs(y[:]))
+            else:
+                nc.scalar.copy(out=woven(rounded), in_=pairs(y[:]))
+            sc_cols = slice(g * S + c * CHUNK, g * S + (c + 1) * CHUNK)
+            nc.vector.quantize_mx(out=y_codes[g][:, cols].bitcast(FP8X4), scales=y_sc[:, sc_cols], in_=rounded[:])
+            words = out_1[g].rearrange("p m t -> p (m t)").bitcast(I32)
+            nc.sync.dma_start(out=words[:, cols], in_=y_codes[g][:, cols].bitcast(I32))
+
+        shipments(0)
+        shipments(1)
+        weight = quantise_weight(wc_raw[0], "wc_0")
+        lanes(0, 0, weight)
+        shipments(2)
+        lanes(0, 1, weight)
+        shipments(3)
+        last_weight = quantise_weight(wc_raw[1], "wc_1")
+        lanes(0, 2, weight)
+        lanes(0, 3, weight)
+        for c in range(CHUNKS):
+            lanes(1, c, last_weight)
+        for q in range(4):
+            queue = nc.scalar if q % 2 else nc.sync
+            queue.dma_start(
+                out=out_2[:, 4 * q : 4 * q + 4, :].bitcast(I32).rearrange("g r m -> r g m"),
+                in_=y_sc[32 * q : 32 * q + 4, :].bitcast(I32).rearrange("r (g m) -> r g m", g=GROUPS),
+            )

@@ -55,7 +55,6 @@ def tile_list_order_lane_cost_kernel(
         warm = keep.tile([P, 8], F32, name="warm")
 
         nc.gpsimd.memset(table_sc[:].bitcast(I32), 0)
-        nc.gpsimd.memset(w4_sc_raw[:].bitcast(I32), 0)
         nc.vector.memset(warm[:, 0:4], 0.0)
         nc.scalar.activation(out=warm[:, 4:8], in_=warm[:, 0:4], func=ACT.Sigmoid)
 
@@ -109,6 +108,7 @@ def tile_list_order_lane_cost_kernel(
         def w1_rows(a):
             return w1[a * K_PASS : (a + 1) * K_PASS, :]
 
+        nc.sync.dma_start(out=w4_raw[:].bitcast(I32), in_=w4_words[0].bitcast(I32))
         load_table(0)
         nc.sync.dma_start(offsets[:], offs)
         load_table(1)
@@ -117,6 +117,10 @@ def tile_list_order_lane_cost_kernel(
                 out=table_sc[32 * q : 32 * q + 4 * PASSES, :].bitcast(I32),
                 in_=tab_scales[:, 4 * q : 4 * q + 4, :].bitcast(I32),
             )
+        nc.vector.tensor_copy(
+            out=w4_codes[:].bitcast(U16).rearrange("p (g t m) -> p g t m", g=GROUPS, t=PACK),
+            in_=w4_raw[:].bitcast(U16).rearrange("p (g m t) -> p g t m", g=GROUPS, t=PACK),
+        )
         gather_table(0)
         gather_table(1)
         nc.vector.tensor_copy(out=picked_sc[:], in_=table_sc[:].indirect(offsets[:]))
@@ -125,17 +129,13 @@ def tile_list_order_lane_cost_kernel(
         load_table(2)
         gather_table(2)
 
-        nc.sync.dma_start(out=w4_raw[:].bitcast(I32), in_=w4_words[0].bitcast(I32))
+        nc.gpsimd.memset(w4_sc_raw[:].bitcast(I32), 0)
         for q in range(4):
             nc.sync.dma_start(
                 out=w4_sc_raw[32 * q : 32 * q + 4, :].bitcast(I32),
                 in_=w4_scales[0, 4 * q : 4 * q + 4, :].bitcast(I32),
             )
         nc.sync.dma_start(out=bias[:], in_=b1.rearrange("(p t) -> p t", t=PACK))
-        nc.vector.tensor_copy(
-            out=w4_codes[:].rearrange("p (g t m b) -> p g t m b", g=GROUPS, t=PACK, b=2),
-            in_=w4_raw[:].rearrange("p (g m t b) -> p g t m b", g=GROUPS, t=PACK, b=2),
-        )
         nc.vector.tensor_copy(
             out=w4_sc[:].rearrange("p (g t m) -> p g t m", g=GROUPS, t=PACK),
             in_=w4_sc_raw[:].rearrange("p (g m t) -> p g t m", g=GROUPS, t=PACK),
@@ -161,15 +161,15 @@ def tile_list_order_lane_cost_kernel(
         def pairs(planes):
             return planes.rearrange("p t (c i) -> p c t i", i=RUN)
 
-        def woven(tile):
-            return tile[:].rearrange("p (c i t) -> p c t i", i=RUN, t=PACK)
+        def woven(run):
+            return run.rearrange("p (c i t) -> p c t i", i=RUN, t=PACK)
 
         def shipments(c):
             cols = slice(c * CHUNK, (c + 1) * CHUNK)
             half, c0 = divmod(c * CHUNK, BANK)
             rounded = ring.tile([P, PACK * CHUNK], BF16, name="h_rounded", bufs=4, align_bytes=64)
             nc.vector.tensor_tensor(
-                out=woven(rounded),
+                out=woven(rounded[:]),
                 in0=pairs(demand[half][:, :, c0 : c0 + CHUNK]),
                 in1=pairs(stock_picked[:, :, cols]),
                 op=ALU.min,
@@ -208,13 +208,19 @@ def tile_list_order_lane_cost_kernel(
                 share = ring.tile([P, 2, CHUNK], F32, name="share", bufs=12)
                 nc.scalar.activation(out=share[:], in_=route[:], func=ACT.Sigmoid)
                 nc.vector.tensor_tensor(out=y[:, t0 : t0 + 2, :], in0=cost[:], in1=share[:], op=ALU.mult)
-            rows = out_0[g * K_PASS : (g + 1) * K_PASS, cols]
-            nc.sync.dma_start(out=rows.rearrange("(p t) c -> p t c", t=PACK), in_=y[:])
+                rows = out_0[g * K_PASS : (g + 1) * K_PASS, cols].rearrange("(p t) c -> p t c", t=PACK)
+                nc.sync.dma_start(out=rows[:, t0 : t0 + 2, :], in_=y[:, t0 : t0 + 2, :])
             rounded = ring.tile([P, PACK * CHUNK], BF16, name="y_rounded", bufs=4, align_bytes=64)
-            if g == GROUPS - 1 and c >= CHUNKS - 1:
-                nc.vector.tensor_copy(out=woven(rounded), in_=pairs(y[:]))
-            else:
-                nc.scalar.copy(out=woven(rounded), in_=pairs(y[:]))
+            mid = CHUNK // 2
+            nc.scalar.copy(out=woven(rounded[:, : PACK * mid]), in_=pairs(y[:, :, :mid]))
+            nc.gpsimd.tensor_scalar(
+                out=woven(rounded[:, PACK * mid :]),
+                in0=pairs(y[:, :, mid:]),
+                scalar1=1.0,
+                scalar2=0.0,
+                op0=ALU.mult,
+                op1=ALU.subtract,
+            )
             sc_cols = slice(g * S + c * CHUNK, g * S + (c + 1) * CHUNK)
             nc.vector.quantize_mx(out=y_codes[g][:, cols].bitcast(FP8X4), scales=y_sc[:, sc_cols], in_=rounded[:])
             words = out_1[g].rearrange("p m t -> p (m t)").bitcast(I32)

@@ -21,10 +21,20 @@ PACK = 4
 K_PASS = P * PACK
 PASSES = K // K_PASS
 GROUPS = N // K_PASS
+QUADS = 4
+QUAD_ROWS = 4
 BANK = 512
-CHUNK = 256
+HALVES = S // BANK
+CHUNK = BANK // 2
 CHUNKS = S // CHUNK
 RUN = 2
+SCALAR_SHARE = CHUNK // 2
+
+RAW_BUFS = 3
+SHARE_BUFS = 12
+Y_BUFS = 5
+WEIGHT_ROUNDED_BUFS = 2
+CHUNK_ROUNDED_BUFS = 4
 
 
 def tile_list_order_lane_cost_kernel(
@@ -34,7 +44,7 @@ def tile_list_order_lane_cost_kernel(
     with ExitStack() as ctx:
         keep = ctx.enter_context(tc.tile_pool(name="keep", bufs=1))
         ring = ctx.enter_context(tc.tile_pool(name="ring", bufs=1))
-        psum = ctx.enter_context(tc.psum_pool(name="psum", bufs=4))
+        psum = ctx.enter_context(tc.psum_pool(name="psum", bufs=PACK))
 
         offsets = keep.tile([P, S // 16], U16, name="offsets")
         bias = keep.tile([P, PACK], F32, name="bias")
@@ -52,11 +62,6 @@ def tile_list_order_lane_cost_kernel(
         h_sc = keep.tile([P, S], U8, name="h_sc", align_bytes=64)
         y_codes = [keep.tile([P, S], U32, name="y_codes%d" % g, align_bytes=64) for g in range(GROUPS)]
         y_sc = keep.tile([P, GROUPS * S], U8, name="y_sc", align_bytes=64)
-        warm = keep.tile([P, 8], F32, name="warm")
-
-        nc.gpsimd.memset(table_sc[:].bitcast(I32), 0)
-        nc.vector.memset(warm[:, 0:4], 0.0)
-        nc.scalar.activation(out=warm[:, 4:8], in_=warm[:, 0:4], func=ACT.Sigmoid)
 
         def load_table(a):
             src = tab_words[a].rearrange("p n i -> p (n i)").bitcast(I32)
@@ -65,19 +70,15 @@ def tile_list_order_lane_cost_kernel(
         def gather_table(a):
             nc.vector.tensor_copy(out=picked[a][:], in_=table[a][:].indirect(offsets[:]))
 
-        def load_stock(t):
-            nc.sync.dma_start(out=stock[t][:], in_=gT.rearrange("(p t) c -> t p c", t=PACK)[t])
-
-        def gather_stock(t):
-            nc.vector.tensor_copy(out=stock_picked[:, t, :], in_=stock[t][:].indirect(offsets[:]))
-
         def load_weight(rows):
-            raw = ring.tile([P, PACK, K_PASS], F32, name="raw", bufs=3)
+            raw = ring.tile([P, PACK, K_PASS], F32, name="raw", bufs=RAW_BUFS)
             nc.sync.dma_start(out=raw[:], in_=rows.rearrange("(p j) c -> p j c", j=PACK))
             return raw
 
         def quantise_weight(raw, name):
-            rounded = ring.tile([P, PACK * K_PASS], BF16, name="w_rounded", bufs=2, align_bytes=64)
+            rounded = ring.tile(
+                [P, PACK * K_PASS], BF16, name="w_rounded", bufs=WEIGHT_ROUNDED_BUFS, align_bytes=64
+            )
             nc.scalar.copy(
                 out=rounded[:].rearrange("p (t m j) -> p m j t", t=PACK, j=PACK),
                 in_=raw[:].rearrange("p j (m t) -> p m j t", t=PACK),
@@ -89,33 +90,33 @@ def tile_list_order_lane_cost_kernel(
 
         acc = [[psum.tile([P, BANK], F32, name=tag) for t in range(PACK)] for tag in ("route", "cost")]
 
-        def first_product(a, weight):
-            codes, scales = weight
-            for half in range(S // BANK):
+        def first_product(a):
+            raw = load_weight(w1[a * K_PASS : (a + 1) * K_PASS, :])
+            codes, scales = quantise_weight(raw, "w1_%d" % a)
+            for half in range(HALVES):
                 cols = slice(half * BANK, (half + 1) * BANK)
                 for t in range(PACK):
-                    m = slice(t * P, (t + 1) * P)
+                    places = slice(t * P, (t + 1) * P)
                     nc.tensor.matmul_mx(
                         out=acc[half][t][:],
-                        lhsT=codes[:, m].bitcast(FP8X4),
-                        lhsT_scale=scales[:, m],
+                        lhsT=codes[:, places].bitcast(FP8X4),
+                        lhsT_scale=scales[:, places],
                         rhs=picked[a][:, cols].bitcast(FP8X4),
-                        rhs_scale=picked_sc[4 * a :, cols],
+                        rhs_scale=picked_sc[QUAD_ROWS * a :, cols],
                         start=(a == 0),
                         stop=(a == PASSES - 1),
                     )
 
-        def w1_rows(a):
-            return w1[a * K_PASS : (a + 1) * K_PASS, :]
+        nc.gpsimd.memset(table_sc[:].bitcast(I32), 0)
 
         nc.sync.dma_start(out=w4_raw[:].bitcast(I32), in_=w4_words[0].bitcast(I32))
         load_table(0)
         nc.sync.dma_start(offsets[:], offs)
         load_table(1)
-        for q in range(4):
+        for q in range(QUADS):
             nc.sync.dma_start(
-                out=table_sc[32 * q : 32 * q + 4 * PASSES, :].bitcast(I32),
-                in_=tab_scales[:, 4 * q : 4 * q + 4, :].bitcast(I32),
+                out=table_sc[32 * q : 32 * q + QUAD_ROWS * PASSES, :].bitcast(I32),
+                in_=tab_scales[:, QUAD_ROWS * q : QUAD_ROWS * (q + 1), :].bitcast(I32),
             )
         nc.vector.tensor_copy(
             out=w4_codes[:].bitcast(U16).rearrange("p (g t m) -> p g t m", g=GROUPS, t=PACK),
@@ -124,16 +125,15 @@ def tile_list_order_lane_cost_kernel(
         gather_table(0)
         gather_table(1)
         nc.vector.tensor_copy(out=picked_sc[:], in_=table_sc[:].indirect(offsets[:]))
-        raw = load_weight(w1_rows(0))
-        first_product(0, quantise_weight(raw, "w1_0"))
+        first_product(0)
         load_table(2)
         gather_table(2)
 
         nc.gpsimd.memset(w4_sc_raw[:].bitcast(I32), 0)
-        for q in range(4):
+        for q in range(QUADS):
             nc.sync.dma_start(
-                out=w4_sc_raw[32 * q : 32 * q + 4, :].bitcast(I32),
-                in_=w4_scales[0, 4 * q : 4 * q + 4, :].bitcast(I32),
+                out=w4_sc_raw[32 * q : 32 * q + QUAD_ROWS, :].bitcast(I32),
+                in_=w4_scales[0, QUAD_ROWS * q : QUAD_ROWS * (q + 1), :].bitcast(I32),
             )
         nc.sync.dma_start(out=bias[:], in_=b1.rearrange("(p t) -> p t", t=PACK))
         nc.vector.tensor_copy(
@@ -141,85 +141,76 @@ def tile_list_order_lane_cost_kernel(
             in_=w4_sc_raw[:].rearrange("p (g m t) -> p g t m", g=GROUPS, t=PACK),
         )
 
-        raw = load_weight(w1_rows(1))
-        first_product(1, quantise_weight(raw, "w1_1"))
-        load_stock(0)
-        gather_stock(0)
-        raw = load_weight(w1_rows(2))
-        first_product(2, quantise_weight(raw, "w1_2"))
-        demand = [keep.tile([P, PACK, BANK], F32, name="demand%d" % half) for half in range(S // BANK)]
-        for half in range(S // BANK):
+        for a in range(1, PASSES):
+            first_product(a)
+        demand = [keep.tile([P, PACK, BANK], F32, name="demand%d" % half) for half in range(HALVES)]
+        for half in range(HALVES):
             for t in range(PACK):
                 nc.scalar.activation(
                     out=demand[half][:, t, :], in_=acc[half][t][:], func=ACT.Relu, bias=bias[:, t : t + 1]
                 )
-        for t in range(1, PACK):
-            load_stock(t)
-            gather_stock(t)
+        for t in range(PACK):
+            nc.sync.dma_start(out=stock[t][:], in_=gT.rearrange("(p t) c -> t p c", t=PACK)[t])
+            nc.vector.tensor_copy(out=stock_picked[:, t, :], in_=stock[t][:].indirect(offsets[:]))
         wc_raw = [load_weight(wc[:, g * K_PASS : (g + 1) * K_PASS]) for g in range(GROUPS)]
 
-        def pairs(planes):
+        def by_runs(planes):
             return planes.rearrange("p t (c i) -> p c t i", i=RUN)
 
-        def woven(run):
-            return run.rearrange("p (c i t) -> p c t i", i=RUN, t=PACK)
+        def woven_by_runs(rounded):
+            return rounded.rearrange("p (c i t) -> p c t i", i=RUN, t=PACK)
 
         def shipments(c):
             cols = slice(c * CHUNK, (c + 1) * CHUNK)
             half, c0 = divmod(c * CHUNK, BANK)
-            rounded = ring.tile([P, PACK * CHUNK], BF16, name="h_rounded", bufs=4, align_bytes=64)
+            rounded = ring.tile([P, PACK * CHUNK], BF16, name="h_rounded", bufs=CHUNK_ROUNDED_BUFS, align_bytes=64)
             nc.vector.tensor_tensor(
-                out=woven(rounded[:]),
-                in0=pairs(demand[half][:, :, c0 : c0 + CHUNK]),
-                in1=pairs(stock_picked[:, :, cols]),
+                out=woven_by_runs(rounded[:]),
+                in0=by_runs(demand[half][:, :, c0 : c0 + CHUNK]),
+                in1=by_runs(stock_picked[:, :, cols]),
                 op=ALU.min,
             )
             nc.vector.quantize_mx(out=h_codes[:, cols].bitcast(FP8X4), scales=h_sc[:, cols], in_=rounded[:])
 
+        def second_product(bank, codes, scales, cols):
+            nc.tensor.matmul_mx(
+                out=bank,
+                lhsT=codes,
+                lhsT_scale=scales,
+                rhs=h_codes[:, cols].bitcast(FP8X4),
+                rhs_scale=h_sc[:, cols],
+                start=True,
+                stop=True,
+            )
+
         def lanes(g, c, weight):
             wc_codes, wc_sc = weight
             cols = slice(c * CHUNK, (c + 1) * CHUNK)
-            y = ring.tile([P, PACK, CHUNK], F32, name="y", bufs=5)
+            rows = out_0[g * K_PASS : (g + 1) * K_PASS, cols].rearrange("(p t) c -> p t c", t=PACK)
+            y = ring.tile([P, PACK, CHUNK], F32, name="y", bufs=Y_BUFS)
             for t0 in range(0, PACK, 2):
                 route = psum.tile([P, 2, CHUNK], F32, name="route")
                 cost = psum.tile([P, 2, CHUNK], F32, name="cost")
                 for e in range(2):
-                    s = (g * PACK + t0 + e) * P
-                    nc.tensor.matmul_mx(
-                        out=route[:, e, :],
-                        lhsT=w4_codes[:, 2 * s : 2 * (s + P)].bitcast(FP4X4),
-                        lhsT_scale=w4_sc[:, s : s + P],
-                        rhs=h_codes[:, cols].bitcast(FP8X4),
-                        rhs_scale=h_sc[:, cols],
-                        start=True,
-                        stop=True,
-                    )
+                    first = g * K_PASS + (t0 + e) * P
+                    codes = w4_codes[:, 2 * first : 2 * (first + P)].bitcast(FP4X4)
+                    second_product(route[:, e, :], codes, w4_sc[:, first : first + P], cols)
                 for e in range(2):
-                    m = slice((t0 + e) * P, (t0 + e + 1) * P)
-                    nc.tensor.matmul_mx(
-                        out=cost[:, e, :],
-                        lhsT=wc_codes[:, m].bitcast(FP8X4),
-                        lhsT_scale=wc_sc[:, m],
-                        rhs=h_codes[:, cols].bitcast(FP8X4),
-                        rhs_scale=h_sc[:, cols],
-                        start=True,
-                        stop=True,
-                    )
-                share = ring.tile([P, 2, CHUNK], F32, name="share", bufs=12)
+                    places = slice((t0 + e) * P, (t0 + e + 1) * P)
+                    second_product(cost[:, e, :], wc_codes[:, places].bitcast(FP8X4), wc_sc[:, places], cols)
+                share = ring.tile([P, 2, CHUNK], F32, name="share", bufs=SHARE_BUFS)
                 nc.scalar.activation(out=share[:], in_=route[:], func=ACT.Sigmoid)
                 nc.vector.tensor_tensor(out=y[:, t0 : t0 + 2, :], in0=cost[:], in1=share[:], op=ALU.mult)
-                rows = out_0[g * K_PASS : (g + 1) * K_PASS, cols].rearrange("(p t) c -> p t c", t=PACK)
                 nc.sync.dma_start(out=rows[:, t0 : t0 + 2, :], in_=y[:, t0 : t0 + 2, :])
-            rounded = ring.tile([P, PACK * CHUNK], BF16, name="y_rounded", bufs=4, align_bytes=64)
-            mid = CHUNK // 2
-            nc.scalar.copy(out=woven(rounded[:, : PACK * mid]), in_=pairs(y[:, :, :mid]))
+            rounded = ring.tile([P, PACK * CHUNK], BF16, name="y_rounded", bufs=CHUNK_ROUNDED_BUFS, align_bytes=64)
+            nc.scalar.copy(out=woven_by_runs(rounded[:, : PACK * SCALAR_SHARE]), in_=by_runs(y[:, :, :SCALAR_SHARE]))
             nc.gpsimd.tensor_scalar(
-                out=woven(rounded[:, PACK * mid :]),
-                in0=pairs(y[:, :, mid:]),
+                out=rounded[:, PACK * SCALAR_SHARE :].rearrange("p (c t) -> p c t", t=PACK),
+                in0=y[:, :, SCALAR_SHARE:].rearrange("p t c -> p c t"),
                 scalar1=1.0,
-                scalar2=0.0,
+                scalar2=-0.0,
                 op0=ALU.mult,
-                op1=ALU.subtract,
+                op1=ALU.add,
             )
             sc_cols = slice(g * S + c * CHUNK, g * S + (c + 1) * CHUNK)
             nc.vector.quantize_mx(out=y_codes[g][:, cols].bitcast(FP8X4), scales=y_sc[:, sc_cols], in_=rounded[:])
@@ -228,19 +219,20 @@ def tile_list_order_lane_cost_kernel(
 
         shipments(0)
         shipments(1)
-        weight = quantise_weight(wc_raw[0], "wc_0")
-        lanes(0, 0, weight)
+        first_weight = quantise_weight(wc_raw[0], "wc_0")
+        lanes(0, 0, first_weight)
         shipments(2)
-        lanes(0, 1, weight)
+        lanes(0, 1, first_weight)
         shipments(3)
         last_weight = quantise_weight(wc_raw[1], "wc_1")
-        lanes(0, 2, weight)
-        lanes(0, 3, weight)
+        for c in range(2, CHUNKS):
+            lanes(0, c, first_weight)
         for c in range(CHUNKS):
             lanes(1, c, last_weight)
-        for q in range(4):
+
+        for q in range(QUADS):
             queue = nc.scalar if q % 2 else nc.sync
             queue.dma_start(
-                out=out_2[:, 4 * q : 4 * q + 4, :].bitcast(I32).rearrange("g r m -> r g m"),
-                in_=y_sc[32 * q : 32 * q + 4, :].bitcast(I32).rearrange("r (g m) -> r g m", g=GROUPS),
+                out=out_2[:, QUAD_ROWS * q : QUAD_ROWS * (q + 1), :].bitcast(I32).rearrange("g r m -> r g m"),
+                in_=y_sc[32 * q : 32 * q + QUAD_ROWS, :].bitcast(I32).rearrange("r (g m) -> r g m", g=GROUPS),
             )

@@ -28,13 +28,13 @@ HALVES = S // BANK
 CHUNK = BANK // 2
 CHUNKS = S // CHUNK
 RUN = 2
-SCALAR_SHARE = CHUNK // 2
+SCALAR_EIGHTHS = 2
 
-RAW_BUFS = 3
-SHARE_BUFS = 12
-Y_BUFS = 5
+RAW_BUFS = 4
+SHARE_BUFS = 8
+Y_BUFS = 3
 WEIGHT_ROUNDED_BUFS = 2
-CHUNK_ROUNDED_BUFS = 4
+CHUNK_ROUNDED_BUFS = 3
 
 
 def tile_list_order_lane_cost_kernel(
@@ -53,7 +53,8 @@ def tile_list_order_lane_cost_kernel(
         picked = [keep.tile([P, S], U32, name="picked%d" % a, align_bytes=64) for a in range(PASSES)]
         picked_sc = keep.tile([P, S], U8, name="picked_sc", align_bytes=64)
         stock = [keep.tile([P, T], F32, name="stock%d" % t) for t in range(PACK)]
-        stock_picked = keep.tile([P, PACK, S], F32, name="stock_picked")
+        stock_picked = [keep.tile([P, PACK, BANK], F32, name="stock_picked%d" % half) for half in range(HALVES)]
+        warm = keep.tile([P, 2], F32, name="warm")
         w4_raw = keep.tile([P, 2 * N], U8, name="w4_raw")
         w4_sc_raw = keep.tile([P, N], U8, name="w4_sc_raw")
         w4_codes = keep.tile([P, 2 * N], U8, name="w4_codes", align_bytes=64)
@@ -70,19 +71,30 @@ def tile_list_order_lane_cost_kernel(
         def gather_table(a):
             nc.vector.tensor_copy(out=picked[a][:], in_=table[a][:].indirect(offsets[:]))
 
-        def load_weight(rows):
-            raw = ring.tile([P, PACK, K_PASS], F32, name="raw", bufs=RAW_BUFS)
-            nc.sync.dma_start(out=raw[:], in_=rows.rearrange("(p j) c -> p j c", j=PACK))
-            return raw
+        def load_weight(rows, pieces):
+            width = K_PASS // pieces
+            raws = []
+            for i in range(pieces):
+                raw = ring.tile([P, PACK, width], F32, name="raw", bufs=RAW_BUFS)
+                src = rows[:, i * width : (i + 1) * width]
+                nc.sync.dma_start(out=raw[:], in_=src.rearrange("(p j) c -> p j c", j=PACK))
+                raws.append(raw)
+            return raws
 
-        def quantise_weight(raw, name):
+        def quantise_weight(raws, name, shared=False):
             rounded = ring.tile(
                 [P, PACK * K_PASS], BF16, name="w_rounded", bufs=WEIGHT_ROUNDED_BUFS, align_bytes=64
             )
-            nc.scalar.copy(
-                out=rounded[:].rearrange("p (t m j) -> p m j t", t=PACK, j=PACK),
-                in_=raw[:].rearrange("p j (m t) -> p m j t", t=PACK),
-            )
+            dealt = rounded[:].rearrange("p (t m j) -> p m j t", t=PACK, j=PACK)
+            share_m = P // len(raws)
+            for i, raw in enumerate(raws):
+                out = dealt[:, i * share_m : (i + 1) * share_m, :, :]
+                src = raw[:].rearrange("p j (m t) -> p m j t", t=PACK)
+                if shared:
+                    nc.scalar.copy(out=out[:, : P // 2], in_=src[:, : P // 2])
+                    nc.vector.tensor_copy(out=out[:, P // 2 :], in_=src[:, P // 2 :])
+                else:
+                    nc.scalar.copy(out=out, in_=src)
             codes = keep.tile([P, K_PASS], U32, name=name + "_codes", align_bytes=64)
             scales = keep.tile([P, K_PASS], U8, name=name + "_sc", align_bytes=64)
             nc.vector.quantize_mx(out=codes[:].bitcast(FP8X4), scales=scales[:], in_=rounded[:])
@@ -91,8 +103,8 @@ def tile_list_order_lane_cost_kernel(
         acc = [[psum.tile([P, BANK], F32, name=tag) for t in range(PACK)] for tag in ("route", "cost")]
 
         def first_product(a):
-            raw = load_weight(w1[a * K_PASS : (a + 1) * K_PASS, :])
-            codes, scales = quantise_weight(raw, "w1_%d" % a)
+            raw = load_weight(w1[a * K_PASS : (a + 1) * K_PASS, :], 1)
+            codes, scales = quantise_weight(raw, "w1_%d" % a, shared=(a == PASSES - 1))
             for half in range(HALVES):
                 cols = slice(half * BANK, (half + 1) * BANK)
                 for t in range(PACK):
@@ -108,6 +120,9 @@ def tile_list_order_lane_cost_kernel(
                     )
 
         nc.gpsimd.memset(table_sc[:].bitcast(I32), 0)
+
+        nc.gpsimd.memset(warm[:, 0:1], 0.0)
+        nc.scalar.activation(out=warm[:, 1:2], in_=warm[:, 0:1], func=ACT.Sigmoid)
 
         nc.sync.dma_start(out=w4_raw[:].bitcast(I32), in_=w4_words[0].bitcast(I32))
         load_table(0)
@@ -141,18 +156,28 @@ def tile_list_order_lane_cost_kernel(
             in_=w4_sc_raw[:].rearrange("p (g m t) -> p g t m", g=GROUPS, t=PACK),
         )
 
-        for a in range(1, PASSES):
-            first_product(a)
+        def gather_stock(t, half):
+            entries = offsets[:, half * BANK // 16 : (half + 1) * BANK // 16]
+            nc.vector.tensor_copy(out=stock_picked[half][:, t, :], in_=stock[t][:].indirect(entries))
+
+        def load_stock(t):
+            nc.sync.dma_start(out=stock[t][:], in_=gT.rearrange("(p t) c -> t p c", t=PACK)[t])
+            if t < PACK - 1:
+                for half in range(HALVES):
+                    gather_stock(t, half)
+
+        first_product(1)
+        load_stock(0)
+        first_product(2)
         demand = [keep.tile([P, PACK, BANK], F32, name="demand%d" % half) for half in range(HALVES)]
         for half in range(HALVES):
             for t in range(PACK):
                 nc.scalar.activation(
                     out=demand[half][:, t, :], in_=acc[half][t][:], func=ACT.Relu, bias=bias[:, t : t + 1]
                 )
-        for t in range(PACK):
-            nc.sync.dma_start(out=stock[t][:], in_=gT.rearrange("(p t) c -> t p c", t=PACK)[t])
-            nc.vector.tensor_copy(out=stock_picked[:, t, :], in_=stock[t][:].indirect(offsets[:]))
-        wc_raw = [load_weight(wc[:, g * K_PASS : (g + 1) * K_PASS]) for g in range(GROUPS)]
+        for t in range(1, PACK):
+            load_stock(t)
+        wc_raw = [load_weight(wc[:, g * K_PASS : (g + 1) * K_PASS], 2) for g in range(GROUPS)]
 
         def by_runs(planes):
             return planes.rearrange("p t (c i) -> p c t i", i=RUN)
@@ -167,7 +192,7 @@ def tile_list_order_lane_cost_kernel(
             nc.vector.tensor_tensor(
                 out=woven_by_runs(rounded[:]),
                 in0=by_runs(demand[half][:, :, c0 : c0 + CHUNK]),
-                in1=by_runs(stock_picked[:, :, cols]),
+                in1=by_runs(stock_picked[half][:, :, c0 : c0 + CHUNK]),
                 op=ALU.min,
             )
             nc.vector.quantize_mx(out=h_codes[:, cols].bitcast(FP8X4), scales=h_sc[:, cols], in_=rounded[:])
@@ -183,52 +208,56 @@ def tile_list_order_lane_cost_kernel(
                 stop=True,
             )
 
-        def lanes(g, c, weight):
+        def lanes(g, c0, width, weight):
             wc_codes, wc_sc = weight
-            cols = slice(c * CHUNK, (c + 1) * CHUNK)
+            cols = slice(c0, c0 + width)
+            per_bank = BANK // width
             rows = out_0[g * K_PASS : (g + 1) * K_PASS, cols].rearrange("(p t) c -> p t c", t=PACK)
-            y = ring.tile([P, PACK, CHUNK], F32, name="y", bufs=Y_BUFS)
-            for t0 in range(0, PACK, 2):
-                route = psum.tile([P, 2, CHUNK], F32, name="route")
-                cost = psum.tile([P, 2, CHUNK], F32, name="cost")
-                for e in range(2):
+            y = ring.tile([P, PACK, width], F32, name="y%d" % width, bufs=Y_BUFS if width == BANK else 2)
+            for t0 in range(0, PACK, per_bank):
+                route = psum.tile([P, per_bank, width], F32, name="route")
+                cost = psum.tile([P, per_bank, width], F32, name="cost")
+                for e in range(per_bank):
                     first = g * K_PASS + (t0 + e) * P
                     codes = w4_codes[:, 2 * first : 2 * (first + P)].bitcast(FP4X4)
                     second_product(route[:, e, :], codes, w4_sc[:, first : first + P], cols)
-                for e in range(2):
+                for e in range(per_bank):
                     places = slice((t0 + e) * P, (t0 + e + 1) * P)
                     second_product(cost[:, e, :], wc_codes[:, places].bitcast(FP8X4), wc_sc[:, places], cols)
-                share = ring.tile([P, 2, CHUNK], F32, name="share", bufs=SHARE_BUFS)
+                share = ring.tile([P, per_bank, width], F32, name="share", bufs=SHARE_BUFS)
                 nc.scalar.activation(out=share[:], in_=route[:], func=ACT.Sigmoid)
-                nc.vector.tensor_tensor(out=y[:, t0 : t0 + 2, :], in0=cost[:], in1=share[:], op=ALU.mult)
-                nc.sync.dma_start(out=rows[:, t0 : t0 + 2, :], in_=y[:, t0 : t0 + 2, :])
-            rounded = ring.tile([P, PACK * CHUNK], BF16, name="y_rounded", bufs=CHUNK_ROUNDED_BUFS, align_bytes=64)
-            nc.scalar.copy(out=woven_by_runs(rounded[:, : PACK * SCALAR_SHARE]), in_=by_runs(y[:, :, :SCALAR_SHARE]))
+                planes = slice(t0, t0 + per_bank)
+                nc.vector.tensor_tensor(out=y[:, planes, :], in0=cost[:], in1=share[:], op=ALU.mult)
+                nc.sync.dma_start(out=rows[:, planes, :], in_=y[:, planes, :])
+            split = width * SCALAR_EIGHTHS // 8
+            rounded = ring.tile([P, PACK * width], BF16, name="y_rounded", bufs=2, align_bytes=64)
+            nc.scalar.copy(out=woven_by_runs(rounded[:, : PACK * split]), in_=by_runs(y[:, :, :split]))
             nc.gpsimd.tensor_scalar(
-                out=rounded[:, PACK * SCALAR_SHARE :].rearrange("p (c t) -> p c t", t=PACK),
-                in0=y[:, :, SCALAR_SHARE:].rearrange("p t c -> p c t"),
+                out=rounded[:, PACK * split :].rearrange("p (c t) -> p c t", t=PACK),
+                in0=y[:, :, split:].rearrange("p t c -> p c t"),
                 scalar1=1.0,
                 scalar2=-0.0,
                 op0=ALU.mult,
                 op1=ALU.add,
             )
-            sc_cols = slice(g * S + c * CHUNK, g * S + (c + 1) * CHUNK)
+            sc_cols = slice(g * S + c0, g * S + c0 + width)
             nc.vector.quantize_mx(out=y_codes[g][:, cols].bitcast(FP8X4), scales=y_sc[:, sc_cols], in_=rounded[:])
             words = out_1[g].rearrange("p m t -> p (m t)").bitcast(I32)
             nc.sync.dma_start(out=words[:, cols], in_=y_codes[g][:, cols].bitcast(I32))
 
+        gather_stock(PACK - 1, 0)
         shipments(0)
         shipments(1)
         first_weight = quantise_weight(wc_raw[0], "wc_0")
-        lanes(0, 0, first_weight)
+        lanes(0, 0, BANK, first_weight)
+        gather_stock(PACK - 1, 1)
         shipments(2)
-        lanes(0, 1, first_weight)
         shipments(3)
+        lanes(0, BANK, BANK, first_weight)
         last_weight = quantise_weight(wc_raw[1], "wc_1")
-        for c in range(2, CHUNKS):
-            lanes(0, c, first_weight)
-        for c in range(CHUNKS):
-            lanes(1, c, last_weight)
+        lanes(1, 0, BANK, last_weight)
+        lanes(1, BANK, CHUNK, last_weight)
+        lanes(1, BANK + CHUNK, CHUNK, last_weight)
 
         for q in range(QUADS):
             queue = nc.scalar if q % 2 else nc.sync

@@ -28,9 +28,9 @@ HALVES = S // BANK
 CHUNK = BANK // 2
 CHUNKS = S // CHUNK
 RUN = 2
-SCALAR_EIGHTHS = 2
+SCALAR_EIGHTHS = 5
 
-RAW_BUFS = 4
+RAW_BUFS = 3
 SHARE_BUFS = 8
 Y_BUFS = 3
 WEIGHT_ROUNDED_BUFS = 2
@@ -53,7 +53,9 @@ def tile_list_order_lane_cost_kernel(
         picked = [keep.tile([P, S], U32, name="picked%d" % a, align_bytes=64) for a in range(PASSES)]
         picked_sc = keep.tile([P, S], U8, name="picked_sc", align_bytes=64)
         stock = [keep.tile([P, T], F32, name="stock%d" % t) for t in range(PACK)]
-        stock_picked = [keep.tile([P, PACK, BANK], F32, name="stock_picked%d" % half) for half in range(HALVES)]
+        picked_first = keep.tile([P, PACK, BANK], F32, name="picked_first")
+        picked_second = keep.tile([P, PACK + 1, BANK], F32, name="picked_second", align_bytes=64)
+        stock_picked = [picked_first[:], picked_second[:, :PACK, :]]
         warm = keep.tile([P, 2], F32, name="warm")
         w4_raw = keep.tile([P, 2 * N], U8, name="w4_raw")
         w4_sc_raw = keep.tile([P, N], U8, name="w4_sc_raw")
@@ -73,38 +75,40 @@ def tile_list_order_lane_cost_kernel(
 
         def load_weight(rows, pieces):
             width = K_PASS // pieces
-            raws = []
+            raw = ring.tile([P, pieces, PACK, width], F32, name="raw", bufs=RAW_BUFS)
             for i in range(pieces):
-                raw = ring.tile([P, PACK, width], F32, name="raw", bufs=RAW_BUFS)
                 src = rows[:, i * width : (i + 1) * width]
-                nc.sync.dma_start(out=raw[:], in_=src.rearrange("(p j) c -> p j c", j=PACK))
-                raws.append(raw)
-            return raws
+                nc.sync.dma_start(out=raw[:, i], in_=src.rearrange("(p j) c -> p j c", j=PACK))
+            return [raw[:, i] for i in range(pieces)]
 
-        def quantise_weight(raws, name, shared=False):
-            rounded = ring.tile(
-                [P, PACK * K_PASS], BF16, name="w_rounded", bufs=WEIGHT_ROUNDED_BUFS, align_bytes=64
-            )
-            dealt = rounded[:].rearrange("p (t m j) -> p m j t", t=PACK, j=PACK)
+        def round_weight(raws, shared=False, rounded=None):
+            if rounded is None:
+                rounded = ring.tile(
+                    [P, PACK * K_PASS], BF16, name="w_rounded", bufs=WEIGHT_ROUNDED_BUFS, align_bytes=64
+                )[:]
+            dealt = rounded.rearrange("p (t m j) -> p m j t", t=PACK, j=PACK)
             share_m = P // len(raws)
             for i, raw in enumerate(raws):
                 out = dealt[:, i * share_m : (i + 1) * share_m, :, :]
-                src = raw[:].rearrange("p j (m t) -> p m j t", t=PACK)
+                src = raw.rearrange("p j (m t) -> p m j t", t=PACK)
                 if shared:
                     nc.scalar.copy(out=out[:, : P // 2], in_=src[:, : P // 2])
                     nc.vector.tensor_copy(out=out[:, P // 2 :], in_=src[:, P // 2 :])
                 else:
                     nc.scalar.copy(out=out, in_=src)
+            return rounded
+
+        def quantise_weight(rounded, name):
             codes = keep.tile([P, K_PASS], U32, name=name + "_codes", align_bytes=64)
             scales = keep.tile([P, K_PASS], U8, name=name + "_sc", align_bytes=64)
-            nc.vector.quantize_mx(out=codes[:].bitcast(FP8X4), scales=scales[:], in_=rounded[:])
+            nc.vector.quantize_mx(out=codes[:].bitcast(FP8X4), scales=scales[:], in_=rounded)
             return codes, scales
 
-        acc = [[psum.tile([P, BANK], F32, name=tag) for t in range(PACK)] for tag in ("route", "cost")]
+        acc = [[psum.tile([P, BANK], F32, name=tag) for t in range(PACK)] for tag in ("low", "high")]
 
         def first_product(a):
             raw = load_weight(w1[a * K_PASS : (a + 1) * K_PASS, :], 1)
-            codes, scales = quantise_weight(raw, "w1_%d" % a, shared=(a == PASSES - 1))
+            codes, scales = quantise_weight(round_weight(raw), "w1_%d" % a)
             for half in range(HALVES):
                 cols = slice(half * BANK, (half + 1) * BANK)
                 for t in range(PACK):
@@ -156,15 +160,16 @@ def tile_list_order_lane_cost_kernel(
             in_=w4_sc_raw[:].rearrange("p (g m t) -> p g t m", g=GROUPS, t=PACK),
         )
 
-        def gather_stock(t, half):
-            entries = offsets[:, half * BANK // 16 : (half + 1) * BANK // 16]
-            nc.vector.tensor_copy(out=stock_picked[half][:, t, :], in_=stock[t][:].indirect(entries))
+        def gather_stock(t, first, width):
+            half, c0 = divmod(first, BANK)
+            entries = offsets[:, first // 16 : (first + width) // 16]
+            nc.vector.tensor_copy(out=stock_picked[half][:, t, c0 : c0 + width], in_=stock[t][:].indirect(entries))
 
         def load_stock(t):
             nc.sync.dma_start(out=stock[t][:], in_=gT.rearrange("(p t) c -> t p c", t=PACK)[t])
             if t < PACK - 1:
                 for half in range(HALVES):
-                    gather_stock(t, half)
+                    gather_stock(t, half * BANK, BANK)
 
         first_product(1)
         load_stock(0)
@@ -185,10 +190,13 @@ def tile_list_order_lane_cost_kernel(
         def woven_by_runs(rounded):
             return rounded.rearrange("p (c i t) -> p c t i", i=RUN, t=PACK)
 
-        def shipments(c):
+        def slot(number, shape, dtype):
+            return ring.tile(shape, dtype, name="slot%d" % number, bufs=1, align_bytes=64)
+
+        def shipments(c, number):
             cols = slice(c * CHUNK, (c + 1) * CHUNK)
             half, c0 = divmod(c * CHUNK, BANK)
-            rounded = ring.tile([P, PACK * CHUNK], BF16, name="h_rounded", bufs=CHUNK_ROUNDED_BUFS, align_bytes=64)
+            rounded = slot(number, [P, PACK * CHUNK], BF16)
             nc.vector.tensor_tensor(
                 out=woven_by_runs(rounded[:]),
                 in0=by_runs(demand[half][:, :, c0 : c0 + CHUNK]),
@@ -208,56 +216,83 @@ def tile_list_order_lane_cost_kernel(
                 stop=True,
             )
 
-        def lanes(g, c0, width, weight):
+        def share_of(g, c0, width, t0, number):
+            per_bank = BANK // width
+            route = psum.tile([P, per_bank, width], F32, name="low")
+            for e in range(per_bank):
+                first = g * K_PASS + (t0 + e) * P
+                codes = w4_codes[:, 2 * first : 2 * (first + P)].bitcast(FP4X4)
+                second_product(route[:, e, :], codes, w4_sc[:, first : first + P], slice(c0, c0 + width))
+            share = slot(number, [P, per_bank, width], F32)
+            nc.scalar.activation(out=share[:], in_=route[:], func=ACT.Sigmoid)
+            return share
+
+        def shares(g, c0, width, numbers):
+            return [share_of(g, c0, width, t0, number) for t0, number in zip(range(0, PACK, BANK // width), numbers)]
+
+        def lanes(g, c0, width, weight, share_tiles):
             wc_codes, wc_sc = weight
             cols = slice(c0, c0 + width)
             per_bank = BANK // width
             rows = out_0[g * K_PASS : (g + 1) * K_PASS, cols].rearrange("(p t) c -> p t c", t=PACK)
             y = ring.tile([P, PACK, width], F32, name="y%d" % width, bufs=Y_BUFS if width == BANK else 2)
-            for t0 in range(0, PACK, per_bank):
-                route = psum.tile([P, per_bank, width], F32, name="route")
-                cost = psum.tile([P, per_bank, width], F32, name="cost")
-                for e in range(per_bank):
-                    first = g * K_PASS + (t0 + e) * P
-                    codes = w4_codes[:, 2 * first : 2 * (first + P)].bitcast(FP4X4)
-                    second_product(route[:, e, :], codes, w4_sc[:, first : first + P], cols)
+            for t0, share in zip(range(0, PACK, per_bank), share_tiles):
+                if isinstance(share, int):
+                    share = share_of(g, c0, width, t0, share)
+                cost = psum.tile([P, per_bank, width], F32, name="high")
                 for e in range(per_bank):
                     places = slice((t0 + e) * P, (t0 + e + 1) * P)
                     second_product(cost[:, e, :], wc_codes[:, places].bitcast(FP8X4), wc_sc[:, places], cols)
-                share = ring.tile([P, per_bank, width], F32, name="share", bufs=SHARE_BUFS)
-                nc.scalar.activation(out=share[:], in_=route[:], func=ACT.Sigmoid)
                 planes = slice(t0, t0 + per_bank)
-                nc.vector.tensor_tensor(out=y[:, planes, :], in0=cost[:], in1=share[:], op=ALU.mult)
+                nc.vector.tensor_tensor(out=y[:, planes, :], in0=share[:], in1=cost[:], op=ALU.mult)
                 nc.sync.dma_start(out=rows[:, planes, :], in_=y[:, planes, :])
-            split = width * SCALAR_EIGHTHS // 8
-            rounded = ring.tile([P, PACK * width], BF16, name="y_rounded", bufs=2, align_bytes=64)
+            return y
+
+        def round_lanes(width, y, eighths):
+            split = width * eighths // 8
+            rounded = ring.tile([P, PACK * width], BF16, name="y_rounded", bufs=3, align_bytes=64)
             nc.scalar.copy(out=woven_by_runs(rounded[:, : PACK * split]), in_=by_runs(y[:, :, :split]))
-            nc.gpsimd.tensor_scalar(
-                out=rounded[:, PACK * split :].rearrange("p (c t) -> p c t", t=PACK),
-                in0=y[:, :, split:].rearrange("p t c -> p c t"),
-                scalar1=1.0,
-                scalar2=-0.0,
-                op0=ALU.mult,
-                op1=ALU.add,
-            )
+            if split < width:
+                nc.vector.tensor_copy(out=woven_by_runs(rounded[:, PACK * split :]), in_=by_runs(y[:, :, split:]))
+            return rounded
+
+        def planes_of(g, c0, width, rounded):
+            cols = slice(c0, c0 + width)
             sc_cols = slice(g * S + c0, g * S + c0 + width)
             nc.vector.quantize_mx(out=y_codes[g][:, cols].bitcast(FP8X4), scales=y_sc[:, sc_cols], in_=rounded[:])
             words = out_1[g].rearrange("p m t -> p (m t)").bitcast(I32)
             nc.sync.dma_start(out=words[:, cols], in_=y_codes[g][:, cols].bitcast(I32))
 
-        gather_stock(PACK - 1, 0)
-        shipments(0)
-        shipments(1)
-        first_weight = quantise_weight(wc_raw[0], "wc_0")
-        lanes(0, 0, BANK, first_weight)
-        gather_stock(PACK - 1, 1)
-        shipments(2)
-        shipments(3)
-        lanes(0, BANK, BANK, first_weight)
-        last_weight = quantise_weight(wc_raw[1], "wc_1")
-        lanes(1, 0, BANK, last_weight)
-        lanes(1, BANK, CHUNK, last_weight)
-        lanes(1, BANK + CHUNK, CHUNK, last_weight)
+        gather_stock(PACK - 1, 0, CHUNK)
+        gather_stock(PACK - 1, CHUNK, CHUNK)
+        shipments(0, 8)
+        shipments(1, 9)
+        spare = picked_second[:, PACK - 1 :, :].rearrange("p s c -> p (s c)").bitcast(BF16)
+        first_weight = quantise_weight(round_weight(wc_raw[0], rounded=spare), "wc_0")
+        last_rounded = round_weight(wc_raw[1])
+        first = shares(0, 0, BANK, range(PACK))
+        early = shares(1, 0, BANK, range(PACK, 2 * PACK))
+        gather_stock(PACK - 1, BANK, BANK)
+        shipments(2, 8)
+        shipments(3, 9)
+        last_weight = quantise_weight(last_rounded, "wc_1")
+        late = shares(0, BANK, BANK, (10, 11, 8, 9))
+        y_0 = lanes(0, 0, BANK, first_weight, first)
+        last = [shares(1, BANK + c * CHUNK, CHUNK, (2 * c, 2 * c + 1)) for c in range(2)]
+        rounded_0 = round_lanes(BANK, y_0, 5)
+        y_1 = lanes(1, 0, BANK, last_weight, early)
+        planes_of(0, 0, BANK, rounded_0)
+        rounded_1 = round_lanes(BANK, y_1, 6)
+        y_2 = lanes(0, BANK, BANK, first_weight, late)
+        planes_of(1, 0, BANK, rounded_1)
+        rounded_2 = round_lanes(BANK, y_2, 7)
+        y_3 = lanes(1, BANK, CHUNK, last_weight, last[0])
+        rounded_3 = round_lanes(CHUNK, y_3, 6)
+        y_4 = lanes(1, BANK + CHUNK, CHUNK, last_weight, last[1])
+        planes_of(0, BANK, BANK, rounded_2)
+        rounded_4 = round_lanes(CHUNK, y_4, 4)
+        planes_of(1, BANK, CHUNK, rounded_3)
+        planes_of(1, BANK + CHUNK, CHUNK, rounded_4)
 
         for q in range(QUADS):
             queue = nc.scalar if q % 2 else nc.sync

@@ -23,18 +23,20 @@ PASSES = K // K_PASS
 GROUPS = N // K_PASS
 QUADS = 4
 QUAD_ROWS = 4
+LIST_ROWS = 16
 BANK = 512
 HALVES = S // BANK
 CHUNK = BANK // 2
-CHUNKS = S // CHUNK
 RUN = 2
-SCALAR_EIGHTHS = 5
+WC_PIECES = 2
+
+SCALAR_EIGHTHS = (8, 8, 6, 6, 5, 4)
 
 RAW_BUFS = 3
-SHARE_BUFS = 8
-Y_BUFS = 3
 WEIGHT_ROUNDED_BUFS = 2
-CHUNK_ROUNDED_BUFS = 3
+WIDE_STEPS = 2
+NARROW_STEPS = 4
+Y_ROUNDED_BUFS = 3
 
 
 def tile_list_order_lane_cost_kernel(
@@ -46,16 +48,16 @@ def tile_list_order_lane_cost_kernel(
         ring = ctx.enter_context(tc.tile_pool(name="ring", bufs=1))
         psum = ctx.enter_context(tc.psum_pool(name="psum", bufs=PACK))
 
-        offsets = keep.tile([P, S // 16], U16, name="offsets")
+        offsets = keep.tile([P, S // LIST_ROWS], U16, name="offsets")
         bias = keep.tile([P, PACK], F32, name="bias")
         table = [keep.tile([P, T], U32, name="table%d" % a) for a in range(PASSES)]
         table_sc = keep.tile([P, T], U8, name="table_sc")
         picked = [keep.tile([P, S], U32, name="picked%d" % a, align_bytes=64) for a in range(PASSES)]
         picked_sc = keep.tile([P, S], U8, name="picked_sc", align_bytes=64)
         stock = [keep.tile([P, T], F32, name="stock%d" % t) for t in range(PACK)]
-        picked_first = keep.tile([P, PACK, BANK], F32, name="picked_first")
-        picked_second = keep.tile([P, PACK + 1, BANK], F32, name="picked_second", align_bytes=64)
-        stock_picked = [picked_first[:], picked_second[:, :PACK, :]]
+        stock_picked = [
+            keep.tile([P, PACK, BANK], F32, name="stock_picked%d" % half, align_bytes=64) for half in range(HALVES)
+        ]
         warm = keep.tile([P, 2], F32, name="warm")
         w4_raw = keep.tile([P, 2 * N], U8, name="w4_raw")
         w4_sc_raw = keep.tile([P, N], U8, name="w4_sc_raw")
@@ -81,21 +83,17 @@ def tile_list_order_lane_cost_kernel(
                 nc.sync.dma_start(out=raw[:, i], in_=src.rearrange("(p j) c -> p j c", j=PACK))
             return [raw[:, i] for i in range(pieces)]
 
-        def round_weight(raws, shared=False, rounded=None):
-            if rounded is None:
-                rounded = ring.tile(
-                    [P, PACK * K_PASS], BF16, name="w_rounded", bufs=WEIGHT_ROUNDED_BUFS, align_bytes=64
-                )[:]
+        def rounded_weight_tile():
+            return ring.tile([P, PACK * K_PASS], BF16, name="w_rounded", bufs=WEIGHT_ROUNDED_BUFS, align_bytes=64)[:]
+
+        def round_weight(pieces, rounded):
             dealt = rounded.rearrange("p (t m j) -> p m j t", t=PACK, j=PACK)
-            share_m = P // len(raws)
-            for i, raw in enumerate(raws):
-                out = dealt[:, i * share_m : (i + 1) * share_m, :, :]
-                src = raw.rearrange("p j (m t) -> p m j t", t=PACK)
-                if shared:
-                    nc.scalar.copy(out=out[:, : P // 2], in_=src[:, : P // 2])
-                    nc.vector.tensor_copy(out=out[:, P // 2 :], in_=src[:, P // 2 :])
-                else:
-                    nc.scalar.copy(out=out, in_=src)
+            m_piece = P // len(pieces)
+            for i, raw in enumerate(pieces):
+                nc.scalar.copy(
+                    out=dealt[:, i * m_piece : (i + 1) * m_piece, :, :],
+                    in_=raw.rearrange("p j (m t) -> p m j t", t=PACK),
+                )
             return rounded
 
         def quantise_weight(rounded, name):
@@ -104,11 +102,12 @@ def tile_list_order_lane_cost_kernel(
             nc.vector.quantize_mx(out=codes[:].bitcast(FP8X4), scales=scales[:], in_=rounded)
             return codes, scales
 
-        acc = [[psum.tile([P, BANK], F32, name=tag) for t in range(PACK)] for tag in ("low", "high")]
+        acc = [[psum.tile([P, BANK], F32, name=tag) for t in range(PACK)] for tag in ("route", "cost")]
 
         def first_product(a):
-            raw = load_weight(w1[a * K_PASS : (a + 1) * K_PASS, :], 1)
-            codes, scales = quantise_weight(round_weight(raw), "w1_%d" % a)
+            pieces = load_weight(w1[a * K_PASS : (a + 1) * K_PASS, :], 1)
+            rounded = round_weight(pieces, rounded_weight_tile())
+            codes, scales = quantise_weight(rounded, "w1_%d" % a)
             for half in range(HALVES):
                 cols = slice(half * BANK, (half + 1) * BANK)
                 for t in range(PACK):
@@ -125,7 +124,7 @@ def tile_list_order_lane_cost_kernel(
 
         nc.gpsimd.memset(table_sc[:].bitcast(I32), 0)
 
-        nc.gpsimd.memset(warm[:, 0:1], 0.0)
+        nc.vector.memset(warm[:, 0:1], 0.0)
         nc.scalar.activation(out=warm[:, 1:2], in_=warm[:, 0:1], func=ACT.Sigmoid)
 
         nc.sync.dma_start(out=w4_raw[:].bitcast(I32), in_=w4_words[0].bitcast(I32))
@@ -160,29 +159,27 @@ def tile_list_order_lane_cost_kernel(
             in_=w4_sc_raw[:].rearrange("p (g m t) -> p g t m", g=GROUPS, t=PACK),
         )
 
-        def gather_stock(t, first, width):
-            half, c0 = divmod(first, BANK)
-            entries = offsets[:, first // 16 : (first + width) // 16]
-            nc.vector.tensor_copy(out=stock_picked[half][:, t, c0 : c0 + width], in_=stock[t][:].indirect(entries))
-
-        def load_stock(t):
-            nc.sync.dma_start(out=stock[t][:], in_=gT.rearrange("(p t) c -> t p c", t=PACK)[t])
-            if t < PACK - 1:
-                for half in range(HALVES):
-                    gather_stock(t, half * BANK, BANK)
-
-        first_product(1)
-        load_stock(0)
-        first_product(2)
+        for a in range(1, PASSES):
+            first_product(a)
         demand = [keep.tile([P, PACK, BANK], F32, name="demand%d" % half) for half in range(HALVES)]
         for half in range(HALVES):
             for t in range(PACK):
                 nc.scalar.activation(
                     out=demand[half][:, t, :], in_=acc[half][t][:], func=ACT.Relu, bias=bias[:, t : t + 1]
                 )
-        for t in range(1, PACK):
-            load_stock(t)
-        wc_raw = [load_weight(wc[:, g * K_PASS : (g + 1) * K_PASS], 2) for g in range(GROUPS)]
+
+        def gather_stock(t, first, width):
+            half, c0 = divmod(first, BANK)
+            entries = offsets[:, first // LIST_ROWS : (first + width) // LIST_ROWS]
+            nc.vector.tensor_copy(out=stock_picked[half][:, t, c0 : c0 + width], in_=stock[t][:].indirect(entries))
+
+        for t in range(PACK):
+            nc.sync.dma_start(out=stock[t][:], in_=gT.rearrange("(p t) c -> t p c", t=PACK)[t])
+            if t < PACK - 1:
+                gather_stock(t, 0, BANK)
+            if t < PACK - 2:
+                gather_stock(t, BANK, BANK)
+        wc_pieces = [load_weight(wc[:, g * K_PASS : (g + 1) * K_PASS], WC_PIECES) for g in range(GROUPS)]
 
         def by_runs(planes):
             return planes.rearrange("p t (c i) -> p c t i", i=RUN)
@@ -190,13 +187,13 @@ def tile_list_order_lane_cost_kernel(
         def woven_by_runs(rounded):
             return rounded.rearrange("p (c i t) -> p c t i", i=RUN, t=PACK)
 
-        def slot(number, shape, dtype):
-            return ring.tile(shape, dtype, name="slot%d" % number, bufs=1, align_bytes=64)
+        def cell(number, shape, dtype):
+            return ring.tile(shape, dtype, name="cell%d" % number, bufs=1, align_bytes=64)
 
         def shipments(c, number):
             cols = slice(c * CHUNK, (c + 1) * CHUNK)
             half, c0 = divmod(c * CHUNK, BANK)
-            rounded = slot(number, [P, PACK * CHUNK], BF16)
+            rounded = cell(number, [P, PACK * CHUNK], BF16)
             nc.vector.tensor_tensor(
                 out=woven_by_runs(rounded[:]),
                 in0=by_runs(demand[half][:, :, c0 : c0 + CHUNK]),
@@ -216,30 +213,33 @@ def tile_list_order_lane_cost_kernel(
                 stop=True,
             )
 
-        def share_of(g, c0, width, t0, number):
+        steps = [(g, 0, BANK) for g in range(GROUPS)]
+        steps += [(g, c0, CHUNK) for c0 in range(BANK, S, CHUNK) for g in range(GROUPS)]
+
+        def shares(step, numbers):
+            g, c0, width = steps[step]
             per_bank = BANK // width
-            route = psum.tile([P, per_bank, width], F32, name="low")
-            for e in range(per_bank):
-                first = g * K_PASS + (t0 + e) * P
-                codes = w4_codes[:, 2 * first : 2 * (first + P)].bitcast(FP4X4)
-                second_product(route[:, e, :], codes, w4_sc[:, first : first + P], slice(c0, c0 + width))
-            share = slot(number, [P, per_bank, width], F32)
-            nc.scalar.activation(out=share[:], in_=route[:], func=ACT.Sigmoid)
-            return share
+            tiles = []
+            for t0, number in zip(range(0, PACK, per_bank), numbers):
+                route = psum.tile([P, per_bank, width], F32, name="route")
+                for e in range(per_bank):
+                    first = g * K_PASS + (t0 + e) * P
+                    codes = w4_codes[:, 2 * first : 2 * (first + P)].bitcast(FP4X4)
+                    second_product(route[:, e, :], codes, w4_sc[:, first : first + P], slice(c0, c0 + width))
+                share = cell(number, [P, per_bank, width], F32)
+                nc.scalar.activation(out=share[:], in_=route[:], func=ACT.Sigmoid)
+                tiles.append(share)
+            return tiles
 
-        def shares(g, c0, width, numbers):
-            return [share_of(g, c0, width, t0, number) for t0, number in zip(range(0, PACK, BANK // width), numbers)]
-
-        def lanes(g, c0, width, weight, share_tiles):
+        def lanes(step, weight, share_tiles):
+            g, c0, width = steps[step]
             wc_codes, wc_sc = weight
             cols = slice(c0, c0 + width)
             per_bank = BANK // width
             rows = out_0[g * K_PASS : (g + 1) * K_PASS, cols].rearrange("(p t) c -> p t c", t=PACK)
-            y = ring.tile([P, PACK, width], F32, name="y%d" % width, bufs=Y_BUFS if width == BANK else 2)
+            y = ring.tile([P, PACK, width], F32, name="y%d" % width, bufs=WIDE_STEPS if width == BANK else NARROW_STEPS)
             for t0, share in zip(range(0, PACK, per_bank), share_tiles):
-                if isinstance(share, int):
-                    share = share_of(g, c0, width, t0, share)
-                cost = psum.tile([P, per_bank, width], F32, name="high")
+                cost = psum.tile([P, per_bank, width], F32, name="cost")
                 for e in range(per_bank):
                     places = slice((t0 + e) * P, (t0 + e + 1) * P)
                     second_product(cost[:, e, :], wc_codes[:, places].bitcast(FP8X4), wc_sc[:, places], cols)
@@ -248,15 +248,17 @@ def tile_list_order_lane_cost_kernel(
                 nc.sync.dma_start(out=rows[:, planes, :], in_=y[:, planes, :])
             return y
 
-        def round_lanes(width, y, eighths):
-            split = width * eighths // 8
-            rounded = ring.tile([P, PACK * width], BF16, name="y_rounded", bufs=3, align_bytes=64)
+        def round_lanes(step, y):
+            width = steps[step][2]
+            split = width * SCALAR_EIGHTHS[step] // 8
+            rounded = ring.tile([P, PACK * width], BF16, name="y_rounded", bufs=Y_ROUNDED_BUFS, align_bytes=64)
             nc.scalar.copy(out=woven_by_runs(rounded[:, : PACK * split]), in_=by_runs(y[:, :, :split]))
             if split < width:
                 nc.vector.tensor_copy(out=woven_by_runs(rounded[:, PACK * split :]), in_=by_runs(y[:, :, split:]))
             return rounded
 
-        def planes_of(g, c0, width, rounded):
+        def quantise_lanes(step, rounded):
+            g, c0, width = steps[step]
             cols = slice(c0, c0 + width)
             sc_cols = slice(g * S + c0, g * S + c0 + width)
             nc.vector.quantize_mx(out=y_codes[g][:, cols].bitcast(FP8X4), scales=y_sc[:, sc_cols], in_=rounded[:])
@@ -267,32 +269,30 @@ def tile_list_order_lane_cost_kernel(
         gather_stock(PACK - 1, CHUNK, CHUNK)
         shipments(0, 8)
         shipments(1, 9)
-        spare = picked_second[:, PACK - 1 :, :].rearrange("p s c -> p (s c)").bitcast(BF16)
-        first_weight = quantise_weight(round_weight(wc_raw[0], rounded=spare), "wc_0")
-        last_rounded = round_weight(wc_raw[1])
-        first = shares(0, 0, BANK, range(PACK))
-        early = shares(1, 0, BANK, range(PACK, 2 * PACK))
+        lent = stock_picked[1][:, PACK - 2 :, :].rearrange("p t c -> p (t c)").bitcast(BF16)
+        weights = [quantise_weight(round_weight(wc_pieces[0], lent), "wc_0")]
+        last_rounded = round_weight(wc_pieces[1], rounded_weight_tile())
+        share_tiles = [shares(0, range(0, 4)), shares(1, range(4, 8))]
+        gather_stock(PACK - 2, BANK, BANK)
         gather_stock(PACK - 1, BANK, BANK)
         shipments(2, 8)
-        shipments(3, 9)
-        last_weight = quantise_weight(last_rounded, "wc_1")
-        late = shares(0, BANK, BANK, (10, 11, 8, 9))
-        y_0 = lanes(0, 0, BANK, first_weight, first)
-        last = [shares(1, BANK + c * CHUNK, CHUNK, (2 * c, 2 * c + 1)) for c in range(2)]
-        rounded_0 = round_lanes(BANK, y_0, 5)
-        y_1 = lanes(1, 0, BANK, last_weight, early)
-        planes_of(0, 0, BANK, rounded_0)
-        rounded_1 = round_lanes(BANK, y_1, 6)
-        y_2 = lanes(0, BANK, BANK, first_weight, late)
-        planes_of(1, 0, BANK, rounded_1)
-        rounded_2 = round_lanes(BANK, y_2, 7)
-        y_3 = lanes(1, BANK, CHUNK, last_weight, last[0])
-        rounded_3 = round_lanes(CHUNK, y_3, 6)
-        y_4 = lanes(1, BANK + CHUNK, CHUNK, last_weight, last[1])
-        planes_of(0, BANK, BANK, rounded_2)
-        rounded_4 = round_lanes(CHUNK, y_4, 4)
-        planes_of(1, BANK, CHUNK, rounded_3)
-        planes_of(1, BANK + CHUNK, CHUNK, rounded_4)
+        weights.append(quantise_weight(last_rounded, "wc_1"))
+        share_tiles += [shares(2, (10, 11)), shares(3, (9, 8))]
+        y = lanes(0, weights[0], share_tiles[0])
+        shipments(3, 3)
+        share_tiles += [shares(4, (0, 1)), shares(5, (2, 3))]
+
+        rounded_y = [round_lanes(0, y)]
+        y = lanes(1, weights[1], share_tiles[1])
+        quantise_lanes(0, rounded_y[0])
+        rounded_y.append(round_lanes(1, y))
+        for step in range(WIDE_STEPS, len(steps)):
+            y = lanes(step, weights[steps[step][0]], share_tiles[step])
+            if step > WIDE_STEPS:
+                quantise_lanes(step - 2, rounded_y[step - 2])
+            rounded_y.append(round_lanes(step, y))
+        for step in range(len(steps) - 2, len(steps)):
+            quantise_lanes(step, rounded_y[step])
 
         for q in range(QUADS):
             queue = nc.scalar if q % 2 else nc.sync

@@ -30,7 +30,7 @@ CHUNK = BANK // 2
 RUN = 2
 WC_PIECES = 2
 
-SCALAR_EIGHTHS = (8, 8, 6, 6, 5, 4)
+SPLIT = 384
 
 RAW_BUFS = 3
 WEIGHT_ROUNDED_BUFS = 2
@@ -55,9 +55,7 @@ def tile_list_order_lane_cost_kernel(
         picked = [keep.tile([P, S], U32, name="picked%d" % a, align_bytes=64) for a in range(PASSES)]
         picked_sc = keep.tile([P, S], U8, name="picked_sc", align_bytes=64)
         stock = [keep.tile([P, T], F32, name="stock%d" % t) for t in range(PACK)]
-        stock_picked = [
-            keep.tile([P, PACK, BANK], F32, name="stock_picked%d" % half, align_bytes=64) for half in range(HALVES)
-        ]
+        stock_picked = keep.tile([P, PACK, S], F32, name="stock_picked", align_bytes=64)
         warm = keep.tile([P, 2], F32, name="warm")
         w4_raw = keep.tile([P, 2 * N], U8, name="w4_raw")
         w4_sc_raw = keep.tile([P, N], U8, name="w4_sc_raw")
@@ -66,7 +64,6 @@ def tile_list_order_lane_cost_kernel(
         h_codes = keep.tile([P, S], U32, name="h_codes", align_bytes=64)
         h_sc = keep.tile([P, S], U8, name="h_sc", align_bytes=64)
         y_codes = [keep.tile([P, S], U32, name="y_codes%d" % g, align_bytes=64) for g in range(GROUPS)]
-        y_sc = keep.tile([P, GROUPS * S], U8, name="y_sc", align_bytes=64)
 
         def load_table(a):
             src = tab_words[a].rearrange("p n i -> p (n i)").bitcast(I32)
@@ -106,7 +103,14 @@ def tile_list_order_lane_cost_kernel(
 
         def first_product(a):
             pieces = load_weight(w1[a * K_PASS : (a + 1) * K_PASS, :], 1)
-            rounded = round_weight(pieces, rounded_weight_tile())
+            rounded = rounded_weight_tile()
+            if a < PASSES - 1:
+                round_weight(pieces, rounded)
+            else:
+                dealt = rounded.rearrange("p (t m j) -> p m j t", t=PACK, j=PACK)
+                raw = pieces[0].rearrange("p j (m t) -> p m j t", t=PACK)
+                nc.scalar.copy(out=dealt[:, : P // 2], in_=raw[:, : P // 2])
+                nc.vector.tensor_copy(out=dealt[:, P // 2 :], in_=raw[:, P // 2 :])
             codes, scales = quantise_weight(rounded, "w1_%d" % a)
             for half in range(HALVES):
                 cols = slice(half * BANK, (half + 1) * BANK)
@@ -159,26 +163,28 @@ def tile_list_order_lane_cost_kernel(
             in_=w4_sc_raw[:].rearrange("p (g m t) -> p g t m", g=GROUPS, t=PACK),
         )
 
-        for a in range(1, PASSES):
-            first_product(a)
-        demand = [keep.tile([P, PACK, BANK], F32, name="demand%d" % half) for half in range(HALVES)]
+        def gather_stock(t, first, width):
+            entries = offsets[:, first // LIST_ROWS : (first + width) // LIST_ROWS]
+            nc.vector.tensor_copy(out=stock_picked[:, t, first : first + width], in_=stock[t][:].indirect(entries))
+
+        def load_stock(t):
+            nc.sync.dma_start(out=stock[t][:], in_=gT.rearrange("(p t) c -> t p c", t=PACK)[t])
+
+        first_product(1)
+        load_stock(0)
+        gather_stock(0, 0, S)
+        first_product(2)
+        demand = [ring.tile([P, PACK, BANK], F32, name="demand%d" % half, bufs=1) for half in range(HALVES)]
         for half in range(HALVES):
             for t in range(PACK):
                 nc.scalar.activation(
                     out=demand[half][:, t, :], in_=acc[half][t][:], func=ACT.Relu, bias=bias[:, t : t + 1]
                 )
 
-        def gather_stock(t, first, width):
-            half, c0 = divmod(first, BANK)
-            entries = offsets[:, first // LIST_ROWS : (first + width) // LIST_ROWS]
-            nc.vector.tensor_copy(out=stock_picked[half][:, t, c0 : c0 + width], in_=stock[t][:].indirect(entries))
-
-        for t in range(PACK):
-            nc.sync.dma_start(out=stock[t][:], in_=gT.rearrange("(p t) c -> t p c", t=PACK)[t])
+        for t in range(1, PACK):
+            load_stock(t)
             if t < PACK - 1:
-                gather_stock(t, 0, BANK)
-            if t < PACK - 2:
-                gather_stock(t, BANK, BANK)
+                gather_stock(t, 0, S)
         wc_pieces = [load_weight(wc[:, g * K_PASS : (g + 1) * K_PASS], WC_PIECES) for g in range(GROUPS)]
 
         def by_runs(planes):
@@ -187,20 +193,19 @@ def tile_list_order_lane_cost_kernel(
         def woven_by_runs(rounded):
             return rounded.rearrange("p (c i t) -> p c t i", i=RUN, t=PACK)
 
-        def cell(number, shape, dtype):
-            return ring.tile(shape, dtype, name="cell%d" % number, bufs=1, align_bytes=64)
-
-        def shipments(c, number):
-            cols = slice(c * CHUNK, (c + 1) * CHUNK)
-            half, c0 = divmod(c * CHUNK, BANK)
-            rounded = cell(number, [P, PACK * CHUNK], BF16)
+        def minimum(first, width, rounded):
+            half, c0 = divmod(first, BANK)
             nc.vector.tensor_tensor(
-                out=woven_by_runs(rounded[:]),
-                in0=by_runs(demand[half][:, :, c0 : c0 + CHUNK]),
-                in1=by_runs(stock_picked[half][:, :, c0 : c0 + CHUNK]),
+                out=woven_by_runs(rounded),
+                in0=by_runs(demand[half][:, :, c0 : c0 + width]),
+                in1=by_runs(stock_picked[:, :, first : first + width]),
                 op=ALU.min,
             )
-            nc.vector.quantize_mx(out=h_codes[:, cols].bitcast(FP8X4), scales=h_sc[:, cols], in_=rounded[:])
+            return rounded
+
+        def quantise_h(first, width, rounded):
+            cols = slice(first, first + width)
+            nc.vector.quantize_mx(out=h_codes[:, cols].bitcast(FP8X4), scales=h_sc[:, cols], in_=rounded)
 
         def second_product(bank, codes, scales, cols):
             nc.tensor.matmul_mx(
@@ -213,85 +218,103 @@ def tile_list_order_lane_cost_kernel(
                 stop=True,
             )
 
-        steps = [(g, 0, BANK) for g in range(GROUPS)]
-        steps += [(g, c0, CHUNK) for c0 in range(BANK, S, CHUNK) for g in range(GROUPS)]
+        steps = [(g, half) for half in range(HALVES) for g in range(GROUPS)]
 
-        def shares(step, numbers):
-            g, c0, width = steps[step]
-            per_bank = BANK // width
+        def banks_of(step):
+            if step < len(steps) - 1:
+                return [(t, 1, 0, BANK) for t in range(PACK)]
+            return [(t, 2, c0, CHUNK) for c0 in (0, CHUNK) for t in (0, 2)]
+
+        def shares(step):
+            g, half = steps[step]
+            tag = "share%d" % step if step < GROUPS else "demand%d" % (step - GROUPS)
+            share = ring.tile([P, PACK, BANK], F32, name=tag, bufs=1)
+            cells = [share[:, i, :] for i in range(PACK)]
+            if step == len(steps) - 1:
+                cells[-1] = ring.tile([P, BANK], F32, name="last_cell", bufs=1, align_bytes=64)[:]
             tiles = []
-            for t0, number in zip(range(0, PACK, per_bank), numbers):
-                route = psum.tile([P, per_bank, width], F32, name="route")
-                for e in range(per_bank):
+            for (t0, planes, c0, width), cell in zip(banks_of(step), cells):
+                route = psum.tile([P, planes, width], F32, name="route")
+                cols = slice(half * BANK + c0, half * BANK + c0 + width)
+                for e in range(planes):
                     first = g * K_PASS + (t0 + e) * P
                     codes = w4_codes[:, 2 * first : 2 * (first + P)].bitcast(FP4X4)
-                    second_product(route[:, e, :], codes, w4_sc[:, first : first + P], slice(c0, c0 + width))
-                share = cell(number, [P, per_bank, width], F32)
-                nc.scalar.activation(out=share[:], in_=route[:], func=ACT.Sigmoid)
-                tiles.append(share)
+                    second_product(route[:, e, :], codes, w4_sc[:, first : first + P], cols)
+                cell = cell.rearrange("p (e c) -> p e c", e=planes)
+                nc.scalar.activation(out=cell, in_=route[:], func=ACT.Sigmoid)
+                tiles.append(cell)
             return tiles
 
-        def lanes(step, weight, share_tiles):
-            g, c0, width = steps[step]
+        def lanes(step, weight, cells):
+            g, half = steps[step]
             wc_codes, wc_sc = weight
-            cols = slice(c0, c0 + width)
-            per_bank = BANK // width
-            rows = out_0[g * K_PASS : (g + 1) * K_PASS, cols].rearrange("(p t) c -> p t c", t=PACK)
-            y = ring.tile([P, PACK, width], F32, name="y%d" % width, bufs=WIDE_STEPS if width == BANK else NARROW_STEPS)
-            for t0, share in zip(range(0, PACK, per_bank), share_tiles):
-                cost = psum.tile([P, per_bank, width], F32, name="cost")
-                for e in range(per_bank):
+            rows = out_0[g * K_PASS : (g + 1) * K_PASS, half * BANK : (half + 1) * BANK]
+            rows = rows.rearrange("(p t) c -> p t c", t=PACK)
+            if step < RAW_BUFS:
+                y = ring.tile([P, PACK, BANK], F32, name="raw", bufs=RAW_BUFS)
+            else:
+                y = keep.tile([P, PACK, BANK], F32, name="y_last")
+            for (t0, planes, c0, width), cell in zip(banks_of(step), cells):
+                cost = psum.tile([P, planes, width], F32, name="cost")
+                cols = slice(half * BANK + c0, half * BANK + c0 + width)
+                for e in range(planes):
                     places = slice((t0 + e) * P, (t0 + e + 1) * P)
                     second_product(cost[:, e, :], wc_codes[:, places].bitcast(FP8X4), wc_sc[:, places], cols)
-                planes = slice(t0, t0 + per_bank)
-                nc.vector.tensor_tensor(out=y[:, planes, :], in0=share[:], in1=cost[:], op=ALU.mult)
-                nc.sync.dma_start(out=rows[:, planes, :], in_=y[:, planes, :])
+                last = t0 + planes
+                nc.vector.tensor_tensor(out=y[:, t0:last, c0 : c0 + width], in0=cell, in1=cost[:], op=ALU.mult)
+                if last % 2 == 0 and c0 + width == BANK:
+                    nc.sync.dma_start(out=rows[:, last - 2 : last, :], in_=y[:, last - 2 : last, :])
             return y
 
-        def round_lanes(step, y):
-            width = steps[step][2]
-            split = width * SCALAR_EIGHTHS[step] // 8
-            rounded = ring.tile([P, PACK * width], BF16, name="y_rounded", bufs=Y_ROUNDED_BUFS, align_bytes=64)
-            nc.scalar.copy(out=woven_by_runs(rounded[:, : PACK * split]), in_=by_runs(y[:, :, :split]))
-            if split < width:
-                nc.vector.tensor_copy(out=woven_by_runs(rounded[:, PACK * split :]), in_=by_runs(y[:, :, split:]))
-            return rounded
+        def round_on_gpsimd(y, rounded, c0, c1):
+            nc.gpsimd.tensor_scalar(
+                out=rounded[:, PACK * c0 : PACK * c1].rearrange("p (c t) -> p c t", t=PACK),
+                in0=y[:, :, c0:c1].rearrange("p t c -> p c t"),
+                scalar1=1.0,
+                scalar2=-0.0,
+                op0=ALU.mult,
+                op1=ALU.add,
+            )
+
+        def round_on_scalar(y, rounded, c0, c1):
+            nc.scalar.copy(out=woven_by_runs(rounded[:, PACK * c0 : PACK * c1]), in_=by_runs(y[:, :, c0:c1]))
+
+        def round_on_vector(y, rounded, c0, c1):
+            nc.vector.tensor_copy(out=woven_by_runs(rounded[:, PACK * c0 : PACK * c1]), in_=by_runs(y[:, :, c0:c1]))
 
         def quantise_lanes(step, rounded):
-            g, c0, width = steps[step]
-            cols = slice(c0, c0 + width)
-            sc_cols = slice(g * S + c0, g * S + c0 + width)
+            g, half = steps[step]
+            cols = slice(half * BANK, (half + 1) * BANK)
+            sc_cols = slice(g * S + half * BANK, g * S + (half + 1) * BANK)
             nc.vector.quantize_mx(out=y_codes[g][:, cols].bitcast(FP8X4), scales=y_sc[:, sc_cols], in_=rounded[:])
             words = out_1[g].rearrange("p m t -> p (m t)").bitcast(I32)
             nc.sync.dma_start(out=words[:, cols], in_=y_codes[g][:, cols].bitcast(I32))
 
         gather_stock(PACK - 1, 0, CHUNK)
         gather_stock(PACK - 1, CHUNK, CHUNK)
-        shipments(0, 8)
-        shipments(1, 9)
-        lent = stock_picked[1][:, PACK - 2 :, :].rearrange("p t c -> p (t c)").bitcast(BF16)
-        weights = [quantise_weight(round_weight(wc_pieces[0], lent), "wc_0")]
-        last_rounded = round_weight(wc_pieces[1], rounded_weight_tile())
-        share_tiles = [shares(0, range(0, 4)), shares(1, range(4, 8))]
-        gather_stock(PACK - 2, BANK, BANK)
+        h_rounded = keep.tile([P, PACK * (CHUNK + BANK)], BF16, name="h_rounded", align_bytes=64)
+        lent = stock_picked[:, PACK - 1, BANK:].bitcast(BF16)
+        first_chunks = [minimum(0, CHUNK, h_rounded[:, : PACK * CHUNK]), minimum(CHUNK, CHUNK, lent)]
+        quantise_h(0, CHUNK, first_chunks[0])
+        quantise_h(CHUNK, CHUNK, first_chunks[1])
         gather_stock(PACK - 1, BANK, BANK)
-        shipments(2, 8)
-        weights.append(quantise_weight(last_rounded, "wc_1"))
-        share_tiles += [shares(2, (10, 11)), shares(3, (9, 8))]
-        y = lanes(0, weights[0], share_tiles[0])
-        shipments(3, 3)
-        share_tiles += [shares(4, (0, 1)), shares(5, (2, 3))]
-
-        rounded_y = [round_lanes(0, y)]
-        y = lanes(1, weights[1], share_tiles[1])
-        quantise_lanes(0, rounded_y[0])
-        rounded_y.append(round_lanes(1, y))
-        for step in range(WIDE_STEPS, len(steps)):
-            y = lanes(step, weights[steps[step][0]], share_tiles[step])
-            if step > WIDE_STEPS:
-                quantise_lanes(step - 2, rounded_y[step - 2])
-            rounded_y.append(round_lanes(step, y))
-        for step in range(len(steps) - 2, len(steps)):
+        weights = [quantise_weight(round_weight(wc_pieces[0], rounded_weight_tile()), "wc_0")]
+        share_tiles = [shares(0)]
+        second_half = minimum(BANK, BANK, h_rounded[:, PACK * CHUNK :])
+        weights.append(quantise_weight(round_weight(wc_pieces[1], rounded_weight_tile()), "wc_1"))
+        quantise_h(BANK, BANK, second_half)
+        share_tiles += [shares(step) for step in range(1, len(steps))]
+        ys = [lanes(step, weights[steps[step][0]], share_tiles[step]) for step in range(len(steps))]
+        rounded_y = [keep.tile([P, PACK * BANK], BF16, name="y_rounded%d" % step, align_bytes=64) for step in range(len(steps))]
+        y_sc = ring.tile([P, GROUPS * S], U8, name="last_cell", bufs=1, align_bytes=64)
+        round_on_gpsimd(ys[0], rounded_y[0], 0, CHUNK)
+        round_on_gpsimd(ys[0], rounded_y[0], CHUNK, BANK)
+        for step in (1, 2):
+            round_on_gpsimd(ys[step], rounded_y[step], 0, CHUNK)
+            round_on_scalar(ys[step], rounded_y[step], CHUNK, BANK)
+        round_on_scalar(ys[3], rounded_y[3], 0, CHUNK)
+        round_on_scalar(ys[3], rounded_y[3], CHUNK, BANK)
+        for step in range(len(steps)):
             quantise_lanes(step, rounded_y[step])
 
         for q in range(QUADS):

@@ -30,7 +30,7 @@ CHUNK = BANK // 2
 RUN = 2
 WC_PIECES = 2
 
-SPLIT = 384
+SLIVER = 128
 
 RAW_BUFS = 3
 WEIGHT_ROUNDED_BUFS = 2
@@ -46,6 +46,7 @@ def tile_list_order_lane_cost_kernel(
     with ExitStack() as ctx:
         keep = ctx.enter_context(tc.tile_pool(name="keep", bufs=1))
         ring = ctx.enter_context(tc.tile_pool(name="ring", bufs=1))
+        handed = ctx.enter_context(tc.tile_pool(name="handed", bufs=1))
         psum = ctx.enter_context(tc.psum_pool(name="psum", bufs=PACK))
 
         offsets = keep.tile([P, S // LIST_ROWS], U16, name="offsets")
@@ -221,50 +222,59 @@ def tile_list_order_lane_cost_kernel(
         steps = [(g, half) for half in range(HALVES) for g in range(GROUPS)]
 
         def banks_of(step):
-            if step < len(steps) - 1:
-                return [(t, 1, 0, BANK) for t in range(PACK)]
-            return [(t, 2, c0, CHUNK) for c0 in (0, CHUNK) for t in (0, 2)]
+            return [(t, 1, 0, BANK) for t in range(PACK)]
 
-        def shares(step):
-            g, half = steps[step]
+        def share_cells(step):
             tag = "share%d" % step if step < GROUPS else "demand%d" % (step - GROUPS)
             share = ring.tile([P, PACK, BANK], F32, name=tag, bufs=1)
             cells = [share[:, i, :] for i in range(PACK)]
             if step == len(steps) - 1:
                 cells[-1] = ring.tile([P, BANK], F32, name="last_cell", bufs=1, align_bytes=64)[:]
-            tiles = []
-            for (t0, planes, c0, width), cell in zip(banks_of(step), cells):
-                route = psum.tile([P, planes, width], F32, name="route")
-                cols = slice(half * BANK + c0, half * BANK + c0 + width)
-                for e in range(planes):
-                    first = g * K_PASS + (t0 + e) * P
-                    codes = w4_codes[:, 2 * first : 2 * (first + P)].bitcast(FP4X4)
-                    second_product(route[:, e, :], codes, w4_sc[:, first : first + P], cols)
-                cell = cell.rearrange("p (e c) -> p e c", e=planes)
-                nc.scalar.activation(out=cell, in_=route[:], func=ACT.Sigmoid)
-                tiles.append(cell)
-            return tiles
+            return [cell.rearrange("p (e c) -> p e c", e=bank[1]) for cell, bank in zip(cells, banks_of(step))]
 
-        def lanes(step, weight, cells):
+        def share_bank(step, bank, cell):
+            g, half = steps[step]
+            t0, planes, c0, width = bank
+            route = psum.tile([P, planes, width], F32, name="route")
+            cols = slice(half * BANK + c0, half * BANK + c0 + width)
+            for e in range(planes):
+                first = g * K_PASS + (t0 + e) * P
+                codes = w4_codes[:, 2 * first : 2 * (first + P)].bitcast(FP4X4)
+                second_product(route[:, e, :], codes, w4_sc[:, first : first + P], cols)
+            nc.scalar.activation(out=cell, in_=route[:], func=ACT.Sigmoid)
+
+        def shares(step):
+            cells = share_cells(step)
+            for bank, cell in zip(banks_of(step), cells):
+                share_bank(step, bank, cell)
+            return cells
+
+        def cost_bank(step, weight, bank):
             g, half = steps[step]
             wc_codes, wc_sc = weight
+            t0, planes, c0, width = bank
+            cost = psum.tile([P, planes, width], F32, name="cost")
+            cols = slice(half * BANK + c0, half * BANK + c0 + width)
+            for e in range(planes):
+                places = slice((t0 + e) * P, (t0 + e + 1) * P)
+                second_product(cost[:, e, :], wc_codes[:, places].bitcast(FP8X4), wc_sc[:, places], cols)
+            return cost
+
+        def lanes_tile(step):
+            if step < RAW_BUFS:
+                return ring.tile([P, PACK, BANK], F32, name="raw", bufs=RAW_BUFS)
+            return keep.tile([P, PACK, BANK], F32, name="y_last")
+
+        def lanes_bank(step, bank, cell, cost, y):
+            g, half = steps[step]
             rows = out_0[g * K_PASS : (g + 1) * K_PASS, half * BANK : (half + 1) * BANK]
             rows = rows.rearrange("(p t) c -> p t c", t=PACK)
-            if step < RAW_BUFS:
-                y = ring.tile([P, PACK, BANK], F32, name="raw", bufs=RAW_BUFS)
-            else:
-                y = keep.tile([P, PACK, BANK], F32, name="y_last")
-            for (t0, planes, c0, width), cell in zip(banks_of(step), cells):
-                cost = psum.tile([P, planes, width], F32, name="cost")
-                cols = slice(half * BANK + c0, half * BANK + c0 + width)
-                for e in range(planes):
-                    places = slice((t0 + e) * P, (t0 + e + 1) * P)
-                    second_product(cost[:, e, :], wc_codes[:, places].bitcast(FP8X4), wc_sc[:, places], cols)
-                last = t0 + planes
-                nc.vector.tensor_tensor(out=y[:, t0:last, c0 : c0 + width], in0=cell, in1=cost[:], op=ALU.mult)
-                if last % 2 == 0 and c0 + width == BANK:
-                    nc.sync.dma_start(out=rows[:, last - 2 : last, :], in_=y[:, last - 2 : last, :])
-            return y
+            t0, planes, c0, width = bank
+            last = t0 + planes
+            nc.vector.tensor_tensor(out=y[:, t0:last, c0 : c0 + width], in0=cell, in1=cost[:], op=ALU.mult)
+            stored = 1 if step == 0 else 2
+            if last % stored == 0 and c0 + width == BANK:
+                nc.sync.dma_start(out=rows[:, last - stored : last, :], in_=y[:, last - stored : last, :])
 
         def round_on_gpsimd(y, rounded, c0, c1):
             nc.gpsimd.tensor_scalar(
@@ -292,29 +302,48 @@ def tile_list_order_lane_cost_kernel(
 
         gather_stock(PACK - 1, 0, CHUNK)
         gather_stock(PACK - 1, CHUNK, CHUNK)
-        h_rounded = keep.tile([P, PACK * (CHUNK + BANK)], BF16, name="h_rounded", align_bytes=64)
+        h_rounded = keep.tile([P, PACK * CHUNK], BF16, name="h_rounded", align_bytes=64)
+        last_weight = handed.tile([P, PACK * K_PASS], BF16, name="last_weight", align_bytes=64, offset=0)
+        last_h = handed.tile([P, PACK * BANK], BF16, name="last_h", align_bytes=64, offset=2 * PACK * K_PASS)
         lent = stock_picked[:, PACK - 1, BANK:].bitcast(BF16)
-        first_chunks = [minimum(0, CHUNK, h_rounded[:, : PACK * CHUNK]), minimum(CHUNK, CHUNK, lent)]
+        first_chunks = [minimum(0, CHUNK, h_rounded[:]), minimum(CHUNK, CHUNK, lent)]
         quantise_h(0, CHUNK, first_chunks[0])
         quantise_h(CHUNK, CHUNK, first_chunks[1])
         gather_stock(PACK - 1, BANK, BANK)
-        weights = [quantise_weight(round_weight(wc_pieces[0], rounded_weight_tile()), "wc_0")]
+        wc_rounded = [round_weight(wc_pieces[0], rounded_weight_tile()), round_weight(wc_pieces[1], last_weight[:])]
+        weights = [quantise_weight(wc_rounded[0], "wc_0")]
         share_tiles = [shares(0)]
-        second_half = minimum(BANK, BANK, h_rounded[:, PACK * CHUNK :])
-        weights.append(quantise_weight(round_weight(wc_pieces[1], rounded_weight_tile()), "wc_1"))
+        first_costs = [cost_bank(0, weights[0], bank) for bank in banks_of(0)]
+        second_half = minimum(BANK, BANK, last_h[:])
+        weights.append(quantise_weight(wc_rounded[1], "wc_1"))
         quantise_h(BANK, BANK, second_half)
-        share_tiles += [shares(step) for step in range(1, len(steps))]
-        ys = [lanes(step, weights[steps[step][0]], share_tiles[step]) for step in range(len(steps))]
-        rounded_y = [keep.tile([P, PACK * BANK], BF16, name="y_rounded%d" % step, align_bytes=64) for step in range(len(steps))]
-        y_sc = ring.tile([P, GROUPS * S], U8, name="last_cell", bufs=1, align_bytes=64)
-        round_on_gpsimd(ys[0], rounded_y[0], 0, CHUNK)
-        round_on_gpsimd(ys[0], rounded_y[0], CHUNK, BANK)
-        for step in (1, 2):
-            round_on_gpsimd(ys[step], rounded_y[step], 0, CHUNK)
-            round_on_scalar(ys[step], rounded_y[step], CHUNK, BANK)
-        round_on_scalar(ys[3], rounded_y[3], 0, CHUNK)
-        round_on_scalar(ys[3], rounded_y[3], CHUNK, BANK)
+        share_tiles.append(shares(1))
+        costs = first_costs
+        ys = []
         for step in range(len(steps)):
+            ys.append(lanes_tile(step))
+            if step + 2 < len(steps):
+                share_tiles.append(share_cells(step + 2))
+            next_costs = []
+            for i, bank in enumerate(banks_of(step)):
+                lanes_bank(step, bank, share_tiles[step][i], costs[i], ys[step])
+                if step + 1 < len(steps):
+                    next_costs.append(cost_bank(step + 1, weights[steps[step + 1][0]], banks_of(step + 1)[i]))
+                if step + 2 < len(steps):
+                    share_bank(step + 2, banks_of(step + 2)[i], share_tiles[step + 2][i])
+            costs = next_costs
+        rounded_y = [handed.tile([P, PACK * BANK], BF16, name="y_rounded0", align_bytes=64, offset=PACK * K_PASS)]
+        rounded_y += [keep.tile([P, PACK * BANK], BF16, name="y_rounded%d" % step, align_bytes=64) for step in range(1, len(steps))]
+        y_sc = ring.tile([P, GROUPS * S], U8, name="last_cell", bufs=1, align_bytes=64)
+        for step in (0, 1):
+            round_on_gpsimd(ys[step], rounded_y[step], 0, CHUNK)
+            round_on_gpsimd(ys[step], rounded_y[step], CHUNK, BANK)
+        round_on_gpsimd(ys[2], rounded_y[2], 0, SLIVER)
+        round_on_scalar(ys[2], rounded_y[2], SLIVER, BANK)
+        round_on_scalar(ys[3], rounded_y[3], 0, BANK - SLIVER)
+        quantise_lanes(0, rounded_y[0])
+        round_on_vector(ys[3], rounded_y[3], BANK - SLIVER, BANK)
+        for step in range(1, len(steps)):
             quantise_lanes(step, rounded_y[step])
 
         for q in range(QUADS):

@@ -62,7 +62,7 @@ def tile_list_order_lane_cost_kernel(
         w4_sc_raw = keep.tile([P, N], U8, name="w4_sc_raw")
         w4_codes = keep.tile([P, 2 * N], U8, name="w4_codes", align_bytes=64)
         w4_sc = keep.tile([P, N], U8, name="w4_sc", align_bytes=64)
-        h_codes = keep.tile([P, S], U32, name="h_codes", align_bytes=64)
+        h_codes = [keep.tile([P, BANK], U32, name="h_codes0", align_bytes=64)]
         h_sc = keep.tile([P, S], U8, name="h_sc", align_bytes=64)
         y_codes = [keep.tile([P, S], U32, name="y_codes%d" % g, align_bytes=64) for g in range(GROUPS)]
 
@@ -95,7 +95,7 @@ def tile_list_order_lane_cost_kernel(
             return rounded
 
         def quantise_weight(rounded, name):
-            codes = keep.tile([P, K_PASS], U32, name=name + "_codes", align_bytes=64)
+            codes = ring.tile([P, K_PASS], U32, name=name + "_codes", bufs=1, align_bytes=64)
             scales = keep.tile([P, K_PASS], U8, name=name + "_sc", align_bytes=64)
             nc.vector.quantize_mx(out=codes[:].bitcast(FP8X4), scales=scales[:], in_=rounded)
             return codes, scales
@@ -205,15 +205,16 @@ def tile_list_order_lane_cost_kernel(
             return rounded
 
         def quantise_h(first, width, rounded):
-            cols = slice(first, first + width)
-            nc.vector.quantize_mx(out=h_codes[:, cols].bitcast(FP8X4), scales=h_sc[:, cols], in_=rounded)
+            half, c0 = divmod(first, BANK)
+            codes = h_codes[half][:, c0 : c0 + width].bitcast(FP8X4)
+            nc.vector.quantize_mx(out=codes, scales=h_sc[:, first : first + width], in_=rounded)
 
         def second_product(bank, codes, scales, cols):
             nc.tensor.matmul_mx(
                 out=bank,
                 lhsT=codes,
                 lhsT_scale=scales,
-                rhs=h_codes[:, cols].bitcast(FP8X4),
+                rhs=h_codes[cols.start // BANK][:].bitcast(FP8X4),
                 rhs_scale=h_sc[:, cols],
                 start=True,
                 stop=True,
@@ -228,6 +229,9 @@ def tile_list_order_lane_cost_kernel(
             tag = "share%d" % step if step < GROUPS else "demand%d" % (step - GROUPS)
             share = ring.tile([P, PACK, BANK], F32, name=tag, bufs=1)
             cells = [share[:, i, :] for i in range(PACK)]
+            if step == 0:
+                cells[0] = ring.tile([P, BANK], F32, name="h_codes1", bufs=1, align_bytes=64)[:]
+                cells[1] = ring.tile([P, BANK], F32, name="wc_1_codes", bufs=1, align_bytes=64)[:]
             if step == len(steps) - 1:
                 cells[-1] = ring.tile([P, BANK], F32, name="last_cell", bufs=1, align_bytes=64)[:]
             return [cell.rearrange("p (e c) -> p e c", e=bank[1]) for cell, bank in zip(cells, banks_of(step))]
@@ -304,23 +308,30 @@ def tile_list_order_lane_cost_kernel(
         gather_stock(PACK - 1, CHUNK, CHUNK)
         h_rounded = keep.tile([P, PACK * CHUNK], BF16, name="h_rounded", align_bytes=64)
         last_weight = handed.tile([P, PACK * K_PASS], BF16, name="last_weight", align_bytes=64, offset=0)
+        first_weight = handed.tile([P, PACK * K_PASS], BF16, name="first_weight", align_bytes=64, offset=2 * PACK * K_PASS)
         last_h = handed.tile([P, PACK * BANK], BF16, name="last_h", align_bytes=64, offset=2 * PACK * K_PASS)
         lent = stock_picked[:, PACK - 1, BANK:].bitcast(BF16)
         first_chunks = [minimum(0, CHUNK, h_rounded[:]), minimum(CHUNK, CHUNK, lent)]
         quantise_h(0, CHUNK, first_chunks[0])
         quantise_h(CHUNK, CHUNK, first_chunks[1])
         gather_stock(PACK - 1, BANK, BANK)
-        wc_rounded = [round_weight(wc_pieces[0], rounded_weight_tile()), round_weight(wc_pieces[1], last_weight[:])]
+        wc_rounded = [round_weight(wc_pieces[0], first_weight[:]), round_weight(wc_pieces[1], last_weight[:])]
         weights = [quantise_weight(wc_rounded[0], "wc_0")]
         share_tiles = [shares(0)]
         first_costs = [cost_bank(0, weights[0], bank) for bank in banks_of(0)]
         second_half = minimum(BANK, BANK, last_h[:])
-        weights.append(quantise_weight(wc_rounded[1], "wc_1"))
-        quantise_h(BANK, BANK, second_half)
         share_tiles.append(shares(1))
-        costs = first_costs
-        ys = []
-        for step in range(len(steps)):
+        ys = [lanes_tile(0)]
+        for i, bank in enumerate(banks_of(0)):
+            lanes_bank(0, bank, share_tiles[0][i], first_costs[i], ys[0])
+            if i == 1:
+                h_codes.append(ring.tile([P, BANK], U32, name="h_codes1", bufs=1, align_bytes=64))
+                quantise_h(BANK, BANK, second_half)
+            if i == 2:
+                weights.append(quantise_weight(wc_rounded[1], "wc_1"))
+        costs = [cost_bank(1, weights[1], bank) for bank in banks_of(1)]
+        share_tiles.append(shares(2))
+        for step in range(1, len(steps)):
             ys.append(lanes_tile(step))
             if step + 2 < len(steps):
                 share_tiles.append(share_cells(step + 2))

@@ -29,14 +29,12 @@ HALVES = S // BANK
 CHUNK = BANK // 2
 RUN = 2
 WC_PIECES = 2
+ROUNDED_BYTES = 2 * PACK * BANK
 
 SLIVER = 128
 
 RAW_BUFS = 3
-WEIGHT_ROUNDED_BUFS = 2
-WIDE_STEPS = 2
-NARROW_STEPS = 4
-Y_ROUNDED_BUFS = 3
+W1_ROUNDED_BUFS = 2
 
 
 def tile_list_order_lane_cost_kernel(
@@ -46,23 +44,27 @@ def tile_list_order_lane_cost_kernel(
     with ExitStack() as ctx:
         keep = ctx.enter_context(tc.tile_pool(name="keep", bufs=1))
         ring = ctx.enter_context(tc.tile_pool(name="ring", bufs=1))
-        handed = ctx.enter_context(tc.tile_pool(name="handed", bufs=1))
+        placed = ctx.enter_context(tc.tile_pool(name="placed", bufs=1))
         psum = ctx.enter_context(tc.psum_pool(name="psum", bufs=PACK))
+
+        def handed_on(tag, shape, dtype):
+            return ring.tile(shape, dtype, name=tag, bufs=1, align_bytes=64)
 
         offsets = keep.tile([P, S // LIST_ROWS], U16, name="offsets")
         bias = keep.tile([P, PACK], F32, name="bias")
-        table = [keep.tile([P, T], U32, name="table%d" % a) for a in range(PASSES)]
+        table = [keep.tile([P, T], U32, name="table%d" % a) for a in range(PASSES - 1)]
+        table.append(handed_on("w1_0_codes", [P, T], U32))
         table_sc = keep.tile([P, T], U8, name="table_sc")
         picked = [keep.tile([P, S], U32, name="picked%d" % a, align_bytes=64) for a in range(PASSES)]
         picked_sc = keep.tile([P, S], U8, name="picked_sc", align_bytes=64)
-        stock = [keep.tile([P, T], F32, name="stock%d" % t) for t in range(PACK)]
+        stock = [handed_on("w1_1_codes", [P, T], F32)]
+        stock += [keep.tile([P, T], F32, name="stock%d" % t) for t in range(1, PACK)]
         stock_picked = keep.tile([P, PACK, S], F32, name="stock_picked", align_bytes=64)
-        warm = keep.tile([P, 2], F32, name="warm")
         w4_raw = keep.tile([P, 2 * N], U8, name="w4_raw")
         w4_sc_raw = keep.tile([P, N], U8, name="w4_sc_raw")
         w4_codes = keep.tile([P, 2 * N], U8, name="w4_codes", align_bytes=64)
         w4_sc = keep.tile([P, N], U8, name="w4_sc", align_bytes=64)
-        h_codes = [keep.tile([P, BANK], U32, name="h_codes0", align_bytes=64)]
+        h_codes = [keep.tile([P, BANK], U32, name="h_0_codes", align_bytes=64)]
         h_sc = keep.tile([P, S], U8, name="h_sc", align_bytes=64)
         y_codes = [keep.tile([P, S], U32, name="y_codes%d" % g, align_bytes=64) for g in range(GROUPS)]
 
@@ -73,6 +75,13 @@ def tile_list_order_lane_cost_kernel(
         def gather_table(a):
             nc.vector.tensor_copy(out=picked[a][:], in_=table[a][:].indirect(offsets[:]))
 
+        def load_stock(t):
+            nc.sync.dma_start(out=stock[t][:], in_=gT.rearrange("(p t) c -> t p c", t=PACK)[t])
+
+        def gather_stock(t, first, width):
+            entries = offsets[:, first // LIST_ROWS : (first + width) // LIST_ROWS]
+            nc.vector.tensor_copy(out=stock_picked[:, t, first : first + width], in_=stock[t][:].indirect(entries))
+
         def load_weight(rows, pieces):
             width = K_PASS // pieces
             raw = ring.tile([P, pieces, PACK, width], F32, name="raw", bufs=RAW_BUFS)
@@ -81,37 +90,32 @@ def tile_list_order_lane_cost_kernel(
                 nc.sync.dma_start(out=raw[:, i], in_=src.rearrange("(p j) c -> p j c", j=PACK))
             return [raw[:, i] for i in range(pieces)]
 
-        def rounded_weight_tile():
-            return ring.tile([P, PACK * K_PASS], BF16, name="w_rounded", bufs=WEIGHT_ROUNDED_BUFS, align_bytes=64)[:]
+        def undealt(raw):
+            return raw.rearrange("p j (m t) -> p m j t", t=PACK)
+
+        def dealt(rounded):
+            return rounded.rearrange("p (t m j) -> p m j t", t=PACK, j=PACK)
 
         def round_weight(pieces, rounded):
-            dealt = rounded.rearrange("p (t m j) -> p m j t", t=PACK, j=PACK)
             m_piece = P // len(pieces)
             for i, raw in enumerate(pieces):
-                nc.scalar.copy(
-                    out=dealt[:, i * m_piece : (i + 1) * m_piece, :, :],
-                    in_=raw.rearrange("p j (m t) -> p m j t", t=PACK),
-                )
+                nc.scalar.copy(out=dealt(rounded)[:, i * m_piece : (i + 1) * m_piece], in_=undealt(raw))
             return rounded
 
         def quantise_weight(rounded, name):
-            codes = ring.tile([P, K_PASS], U32, name=name + "_codes", bufs=1, align_bytes=64)
+            codes = handed_on(name + "_codes", [P, K_PASS], U32)
             scales = keep.tile([P, K_PASS], U8, name=name + "_sc", align_bytes=64)
             nc.vector.quantize_mx(out=codes[:].bitcast(FP8X4), scales=scales[:], in_=rounded)
             return codes, scales
 
+        def load_w1(a):
+            pieces = load_weight(w1[a * K_PASS : (a + 1) * K_PASS, :], 1)
+            rounded = ring.tile([P, PACK * K_PASS], BF16, name="w1_rounded", bufs=W1_ROUNDED_BUFS, align_bytes=64)
+            return pieces, rounded[:]
+
         acc = [[psum.tile([P, BANK], F32, name=tag) for t in range(PACK)] for tag in ("route", "cost")]
 
-        def first_product(a):
-            pieces = load_weight(w1[a * K_PASS : (a + 1) * K_PASS, :], 1)
-            rounded = rounded_weight_tile()
-            if a < PASSES - 1:
-                round_weight(pieces, rounded)
-            else:
-                dealt = rounded.rearrange("p (t m j) -> p m j t", t=PACK, j=PACK)
-                raw = pieces[0].rearrange("p j (m t) -> p m j t", t=PACK)
-                nc.scalar.copy(out=dealt[:, : P // 2], in_=raw[:, : P // 2])
-                nc.vector.tensor_copy(out=dealt[:, P // 2 :], in_=raw[:, P // 2 :])
+        def first_product(a, rounded):
             codes, scales = quantise_weight(rounded, "w1_%d" % a)
             for half in range(HALVES):
                 cols = slice(half * BANK, (half + 1) * BANK)
@@ -129,9 +133,6 @@ def tile_list_order_lane_cost_kernel(
 
         nc.gpsimd.memset(table_sc[:].bitcast(I32), 0)
 
-        nc.vector.memset(warm[:, 0:1], 0.0)
-        nc.scalar.activation(out=warm[:, 1:2], in_=warm[:, 0:1], func=ACT.Sigmoid)
-
         nc.sync.dma_start(out=w4_raw[:].bitcast(I32), in_=w4_words[0].bitcast(I32))
         load_table(0)
         nc.sync.dma_start(offsets[:], offs)
@@ -148,9 +149,12 @@ def tile_list_order_lane_cost_kernel(
         gather_table(0)
         gather_table(1)
         nc.vector.tensor_copy(out=picked_sc[:], in_=table_sc[:].indirect(offsets[:]))
-        first_product(0)
+
+        pieces, rounded = load_w1(0)
+        round_weight(pieces, rounded)
         load_table(2)
         gather_table(2)
+        first_product(0, rounded)
 
         nc.gpsimd.memset(w4_sc_raw[:].bitcast(I32), 0)
         for q in range(QUADS):
@@ -164,18 +168,18 @@ def tile_list_order_lane_cost_kernel(
             in_=w4_sc_raw[:].rearrange("p (g m t) -> p g t m", g=GROUPS, t=PACK),
         )
 
-        def gather_stock(t, first, width):
-            entries = offsets[:, first // LIST_ROWS : (first + width) // LIST_ROWS]
-            nc.vector.tensor_copy(out=stock_picked[:, t, first : first + width], in_=stock[t][:].indirect(entries))
-
-        def load_stock(t):
-            nc.sync.dma_start(out=stock[t][:], in_=gT.rearrange("(p t) c -> t p c", t=PACK)[t])
-
-        first_product(1)
+        pieces, rounded = load_w1(1)
+        round_weight(pieces, rounded)
         load_stock(0)
         gather_stock(0, 0, S)
-        first_product(2)
-        demand = [ring.tile([P, PACK, BANK], F32, name="demand%d" % half, bufs=1) for half in range(HALVES)]
+        first_product(1, rounded)
+
+        pieces, rounded = load_w1(2)
+        nc.scalar.copy(out=dealt(rounded)[:, : P // 2], in_=undealt(pieces[0])[:, : P // 2])
+        nc.vector.tensor_copy(out=dealt(rounded)[:, P // 2 :], in_=undealt(pieces[0])[:, P // 2 :])
+        first_product(2, rounded)
+
+        demand = [handed_on("demand%d" % half, [P, PACK, BANK], F32) for half in range(HALVES)]
         for half in range(HALVES):
             for t in range(PACK):
                 nc.scalar.activation(
@@ -202,160 +206,157 @@ def tile_list_order_lane_cost_kernel(
                 in1=by_runs(stock_picked[:, :, first : first + width]),
                 op=ALU.min,
             )
-            return rounded
 
         def quantise_h(first, width, rounded):
             half, c0 = divmod(first, BANK)
             codes = h_codes[half][:, c0 : c0 + width].bitcast(FP8X4)
             nc.vector.quantize_mx(out=codes, scales=h_sc[:, first : first + width], in_=rounded)
 
-        def second_product(bank, codes, scales, cols):
+        steps = [(g, half) for half in range(HALVES) for g in range(GROUPS)]
+        last_step = len(steps) - 1
+
+        def second_product(tag, codes, scales, half):
+            bank = psum.tile([P, BANK], F32, name=tag)
             nc.tensor.matmul_mx(
-                out=bank,
+                out=bank[:],
                 lhsT=codes,
                 lhsT_scale=scales,
-                rhs=h_codes[cols.start // BANK][:].bitcast(FP8X4),
-                rhs_scale=h_sc[:, cols],
+                rhs=h_codes[half][:].bitcast(FP8X4),
+                rhs_scale=h_sc[:, half * BANK : (half + 1) * BANK],
                 start=True,
                 stop=True,
             )
-
-        steps = [(g, half) for half in range(HALVES) for g in range(GROUPS)]
-
-        def banks_of(step):
-            return [(t, 1, 0, BANK) for t in range(PACK)]
+            return bank
 
         def share_cells(step):
             tag = "share%d" % step if step < GROUPS else "demand%d" % (step - GROUPS)
-            share = ring.tile([P, PACK, BANK], F32, name=tag, bufs=1)
-            cells = [share[:, i, :] for i in range(PACK)]
+            share = handed_on(tag, [P, PACK, BANK], F32)
+            cells = [share[:, t, :] for t in range(PACK)]
             if step == 0:
-                cells[0] = ring.tile([P, BANK], F32, name="h_codes1", bufs=1, align_bytes=64)[:]
-                cells[1] = ring.tile([P, BANK], F32, name="wc_1_codes", bufs=1, align_bytes=64)[:]
-            if step == len(steps) - 1:
-                cells[-1] = ring.tile([P, BANK], F32, name="last_cell", bufs=1, align_bytes=64)[:]
-            return [cell.rearrange("p (e c) -> p e c", e=bank[1]) for cell, bank in zip(cells, banks_of(step))]
+                cells[0] = handed_on("h_1_codes", [P, BANK], F32)[:]
+                cells[1] = handed_on("wc_1_codes", [P, BANK], F32)[:]
+            if step == last_step:
+                cells[-1] = handed_on("y_sc", [P, BANK], F32)[:]
+            return cells
 
-        def share_bank(step, bank, cell):
+        def share_plane(step, t, cell):
             g, half = steps[step]
-            t0, planes, c0, width = bank
-            route = psum.tile([P, planes, width], F32, name="route")
-            cols = slice(half * BANK + c0, half * BANK + c0 + width)
-            for e in range(planes):
-                first = g * K_PASS + (t0 + e) * P
-                codes = w4_codes[:, 2 * first : 2 * (first + P)].bitcast(FP4X4)
-                second_product(route[:, e, :], codes, w4_sc[:, first : first + P], cols)
+            first = g * K_PASS + t * P
+            codes = w4_codes[:, 2 * first : 2 * (first + P)].bitcast(FP4X4)
+            route = second_product("route", codes, w4_sc[:, first : first + P], half)
             nc.scalar.activation(out=cell, in_=route[:], func=ACT.Sigmoid)
 
         def shares(step):
             cells = share_cells(step)
-            for bank, cell in zip(banks_of(step), cells):
-                share_bank(step, bank, cell)
+            for t in range(PACK):
+                share_plane(step, t, cells[t])
             return cells
 
-        def cost_bank(step, weight, bank):
+        def cost_plane(step, t):
             g, half = steps[step]
-            wc_codes, wc_sc = weight
-            t0, planes, c0, width = bank
-            cost = psum.tile([P, planes, width], F32, name="cost")
-            cols = slice(half * BANK + c0, half * BANK + c0 + width)
-            for e in range(planes):
-                places = slice((t0 + e) * P, (t0 + e + 1) * P)
-                second_product(cost[:, e, :], wc_codes[:, places].bitcast(FP8X4), wc_sc[:, places], cols)
-            return cost
+            codes, scales = wc_quantised[g]
+            places = slice(t * P, (t + 1) * P)
+            return second_product("cost", codes[:, places].bitcast(FP8X4), scales[:, places], half)
 
         def lanes_tile(step):
             if step < RAW_BUFS:
                 return ring.tile([P, PACK, BANK], F32, name="raw", bufs=RAW_BUFS)
             return keep.tile([P, PACK, BANK], F32, name="y_last")
 
-        def lanes_bank(step, bank, cell, cost, y):
+        def lanes_plane(step, t, cell, cost):
             g, half = steps[step]
             rows = out_0[g * K_PASS : (g + 1) * K_PASS, half * BANK : (half + 1) * BANK]
-            rows = rows.rearrange("(p t) c -> p t c", t=PACK)
-            t0, planes, c0, width = bank
-            last = t0 + planes
-            nc.vector.tensor_tensor(out=y[:, t0:last, c0 : c0 + width], in0=cell, in1=cost[:], op=ALU.mult)
-            stored = 1 if step == 0 else 2
-            if last % stored == 0 and c0 + width == BANK:
-                nc.sync.dma_start(out=rows[:, last - stored : last, :], in_=y[:, last - stored : last, :])
+            nc.vector.tensor_tensor(out=y[step][:, t, :], in0=cell, in1=cost[:], op=ALU.mult)
+            nc.sync.dma_start(out=rows.rearrange("(p t) c -> t p c", t=PACK)[t], in_=y[step][:, t, :])
 
-        def round_on_gpsimd(y, rounded, c0, c1):
+        def round_on_gpsimd(step, c0, c1):
             nc.gpsimd.tensor_scalar(
-                out=rounded[:, PACK * c0 : PACK * c1].rearrange("p (c t) -> p c t", t=PACK),
-                in0=y[:, :, c0:c1].rearrange("p t c -> p c t"),
+                out=y_rounded[step][:, PACK * c0 : PACK * c1].rearrange("p (c t) -> p c t", t=PACK),
+                in0=y[step][:, :, c0:c1].rearrange("p t c -> p c t"),
                 scalar1=1.0,
                 scalar2=-0.0,
                 op0=ALU.mult,
                 op1=ALU.add,
             )
 
-        def round_on_scalar(y, rounded, c0, c1):
-            nc.scalar.copy(out=woven_by_runs(rounded[:, PACK * c0 : PACK * c1]), in_=by_runs(y[:, :, c0:c1]))
+        def round_on_scalar(step, c0, c1):
+            out = woven_by_runs(y_rounded[step][:, PACK * c0 : PACK * c1])
+            nc.scalar.copy(out=out, in_=by_runs(y[step][:, :, c0:c1]))
 
-        def round_on_vector(y, rounded, c0, c1):
-            nc.vector.tensor_copy(out=woven_by_runs(rounded[:, PACK * c0 : PACK * c1]), in_=by_runs(y[:, :, c0:c1]))
+        def round_on_vector(step, c0, c1):
+            out = woven_by_runs(y_rounded[step][:, PACK * c0 : PACK * c1])
+            nc.vector.tensor_copy(out=out, in_=by_runs(y[step][:, :, c0:c1]))
 
-        def quantise_lanes(step, rounded):
+        def quantise_lanes(step):
             g, half = steps[step]
             cols = slice(half * BANK, (half + 1) * BANK)
             sc_cols = slice(g * S + half * BANK, g * S + (half + 1) * BANK)
-            nc.vector.quantize_mx(out=y_codes[g][:, cols].bitcast(FP8X4), scales=y_sc[:, sc_cols], in_=rounded[:])
+            codes = y_codes[g][:, cols]
+            nc.vector.quantize_mx(out=codes.bitcast(FP8X4), scales=y_sc[:, sc_cols], in_=y_rounded[step][:])
             words = out_1[g].rearrange("p m t -> p (m t)").bitcast(I32)
-            nc.sync.dma_start(out=words[:, cols], in_=y_codes[g][:, cols].bitcast(I32))
+            nc.sync.dma_start(out=words[:, cols], in_=codes.bitcast(I32))
 
-        gather_stock(PACK - 1, 0, CHUNK)
-        gather_stock(PACK - 1, CHUNK, CHUNK)
-        h_rounded = keep.tile([P, PACK * CHUNK], BF16, name="h_rounded", align_bytes=64)
-        last_weight = handed.tile([P, PACK * K_PASS], BF16, name="last_weight", align_bytes=64, offset=0)
-        first_weight = handed.tile([P, PACK * K_PASS], BF16, name="first_weight", align_bytes=64, offset=2 * PACK * K_PASS)
-        last_h = handed.tile([P, PACK * BANK], BF16, name="last_h", align_bytes=64, offset=2 * PACK * K_PASS)
-        lent = stock_picked[:, PACK - 1, BANK:].bitcast(BF16)
-        first_chunks = [minimum(0, CHUNK, h_rounded[:]), minimum(CHUNK, CHUNK, lent)]
-        quantise_h(0, CHUNK, first_chunks[0])
-        quantise_h(CHUNK, CHUNK, first_chunks[1])
+        def placed_rounded(name, offset):
+            return placed.tile([P, PACK * BANK], BF16, name=name, align_bytes=64, offset=offset)
+
+        second_chunk = keep.tile([P, PACK * CHUNK], BF16, name="second_chunk", align_bytes=64)
+        chunks = [stock_picked[:, PACK - 1, BANK:].bitcast(BF16), second_chunk[:]]
+        for c in range(len(chunks)):
+            gather_stock(PACK - 1, c * CHUNK, CHUNK)
+        for c, rounded in enumerate(chunks):
+            minimum(c * CHUNK, CHUNK, rounded)
+        for c, rounded in enumerate(chunks):
+            quantise_h(c * CHUNK, CHUNK, rounded)
         gather_stock(PACK - 1, BANK, BANK)
-        wc_rounded = [round_weight(wc_pieces[0], first_weight[:]), round_weight(wc_pieces[1], last_weight[:])]
-        weights = [quantise_weight(wc_rounded[0], "wc_0")]
-        share_tiles = [shares(0)]
-        first_costs = [cost_bank(0, weights[0], bank) for bank in banks_of(0)]
-        second_half = minimum(BANK, BANK, last_h[:])
-        share_tiles.append(shares(1))
-        ys = [lanes_tile(0)]
-        for i, bank in enumerate(banks_of(0)):
-            lanes_bank(0, bank, share_tiles[0][i], first_costs[i], ys[0])
-            if i == 1:
-                h_codes.append(ring.tile([P, BANK], U32, name="h_codes1", bufs=1, align_bytes=64))
-                quantise_h(BANK, BANK, second_half)
-            if i == 2:
-                weights.append(quantise_weight(wc_rounded[1], "wc_1"))
-        costs = [cost_bank(1, weights[1], bank) for bank in banks_of(1)]
-        share_tiles.append(shares(2))
+
+        wc_rounded = [placed_rounded("wc_0_rounded", ROUNDED_BYTES), placed_rounded("wc_1_rounded", 0)]
+        for g in range(GROUPS):
+            round_weight(wc_pieces[g], wc_rounded[g][:])
+        wc_quantised = [quantise_weight(wc_rounded[0][:], "wc_0")]
+        cells = [shares(0)]
+        costs = [cost_plane(0, t) for t in range(PACK)]
+        second_half = placed_rounded("second_half", ROUNDED_BYTES)
+        minimum(BANK, BANK, second_half[:])
+        cells.append(shares(1))
+
+        y = [lanes_tile(0)]
+        lanes_plane(0, 0, cells[0][0], costs[0])
+        lanes_plane(0, 1, cells[0][1], costs[1])
+        h_codes.append(handed_on("h_1_codes", [P, BANK], U32))
+        quantise_h(BANK, BANK, second_half[:])
+        lanes_plane(0, 2, cells[0][2], costs[2])
+        wc_quantised.append(quantise_weight(wc_rounded[1][:], "wc_1"))
+        lanes_plane(0, 3, cells[0][3], costs[3])
+        costs = [cost_plane(1, t) for t in range(PACK)]
+        cells.append(shares(2))
+
         for step in range(1, len(steps)):
-            ys.append(lanes_tile(step))
-            if step + 2 < len(steps):
-                share_tiles.append(share_cells(step + 2))
+            y.append(lanes_tile(step))
+            if step + 2 <= last_step:
+                cells.append(share_cells(step + 2))
             next_costs = []
-            for i, bank in enumerate(banks_of(step)):
-                lanes_bank(step, bank, share_tiles[step][i], costs[i], ys[step])
-                if step + 1 < len(steps):
-                    next_costs.append(cost_bank(step + 1, weights[steps[step + 1][0]], banks_of(step + 1)[i]))
-                if step + 2 < len(steps):
-                    share_bank(step + 2, banks_of(step + 2)[i], share_tiles[step + 2][i])
+            for t in range(PACK):
+                lanes_plane(step, t, cells[step][t], costs[t])
+                if step + 1 <= last_step:
+                    next_costs.append(cost_plane(step + 1, t))
+                if step + 2 <= last_step:
+                    share_plane(step + 2, t, cells[step + 2][t])
             costs = next_costs
-        rounded_y = [handed.tile([P, PACK * BANK], BF16, name="y_rounded0", align_bytes=64, offset=PACK * K_PASS)]
-        rounded_y += [keep.tile([P, PACK * BANK], BF16, name="y_rounded%d" % step, align_bytes=64) for step in range(1, len(steps))]
-        y_sc = ring.tile([P, GROUPS * S], U8, name="last_cell", bufs=1, align_bytes=64)
-        for step in (0, 1):
-            round_on_gpsimd(ys[step], rounded_y[step], 0, CHUNK)
-            round_on_gpsimd(ys[step], rounded_y[step], CHUNK, BANK)
-        round_on_gpsimd(ys[2], rounded_y[2], 0, SLIVER)
-        round_on_scalar(ys[2], rounded_y[2], SLIVER, BANK)
-        round_on_scalar(ys[3], rounded_y[3], 0, BANK - SLIVER)
-        quantise_lanes(0, rounded_y[0])
-        round_on_vector(ys[3], rounded_y[3], BANK - SLIVER, BANK)
+
+        y_rounded = [placed_rounded("y_rounded0", ROUNDED_BYTES // 2)]
         for step in range(1, len(steps)):
-            quantise_lanes(step, rounded_y[step])
+            y_rounded.append(keep.tile([P, PACK * BANK], BF16, name="y_rounded%d" % step, align_bytes=64))
+        y_sc = handed_on("y_sc", [P, GROUPS * S], U8)
+        for step in range(GROUPS):
+            for c0 in range(0, BANK, CHUNK):
+                round_on_gpsimd(step, c0, c0 + CHUNK)
+        round_on_gpsimd(last_step - 1, 0, SLIVER)
+        round_on_scalar(last_step - 1, SLIVER, BANK)
+        round_on_scalar(last_step, 0, BANK - SLIVER)
+        quantise_lanes(0)
+        round_on_vector(last_step, BANK - SLIVER, BANK)
+        for step in range(1, len(steps)):
+            quantise_lanes(step)
 
         for q in range(QUADS):
             queue = nc.scalar if q % 2 else nc.sync

@@ -133,7 +133,6 @@ def tile_list_order_lane_cost_kernel(
 
         nc.gpsimd.memset(table_sc[:].bitcast(I32), 0)
 
-        nc.sync.dma_start(out=w4_raw[:].bitcast(I32), in_=w4_words[0].bitcast(I32))
         load_table(0)
         nc.sync.dma_start(offsets[:], offs)
         load_table(1)
@@ -142,10 +141,6 @@ def tile_list_order_lane_cost_kernel(
                 out=table_sc[32 * q : 32 * q + QUAD_ROWS * PASSES, :].bitcast(I32),
                 in_=tab_scales[:, QUAD_ROWS * q : QUAD_ROWS * (q + 1), :].bitcast(I32),
             )
-        nc.vector.tensor_copy(
-            out=w4_codes[:].bitcast(U16).rearrange("p (g t m) -> p g t m", g=GROUPS, t=PACK),
-            in_=w4_raw[:].bitcast(U16).rearrange("p (g m t) -> p g t m", g=GROUPS, t=PACK),
-        )
         gather_table(0)
         gather_table(1)
         nc.vector.tensor_copy(out=picked_sc[:], in_=table_sc[:].indirect(offsets[:]))
@@ -190,6 +185,11 @@ def tile_list_order_lane_cost_kernel(
             load_stock(t)
             if t < PACK - 1:
                 gather_stock(t, 0, S)
+        nc.sync.dma_start(out=w4_raw[:].bitcast(I32), in_=w4_words[0].bitcast(I32))
+        nc.scalar.copy(
+            out=w4_codes[:].bitcast(U16).rearrange("p (g t m) -> p g m t", g=GROUPS, t=PACK),
+            in_=w4_raw[:].bitcast(U16).rearrange("p (g m t) -> p g m t", g=GROUPS, t=PACK),
+        )
         wc_pieces = [load_weight(wc[:, g * K_PASS : (g + 1) * K_PASS], WC_PIECES) for g in range(GROUPS)]
 
         def by_runs(planes):

@@ -131,6 +131,10 @@ def tile_list_order_lane_cost_kernel(
                         stop=(a == PASSES - 1),
                     )
 
+        warm = keep.tile([P, 2], F32, name="warm")
+        nc.vector.memset(warm[:, 0:1], 0.0)
+        nc.scalar.activation(out=warm[:, 1:2], in_=warm[:, 0:1], func=ACT.Sigmoid)
+
         nc.gpsimd.memset(table_sc[:].bitcast(I32), 0)
 
         load_table(0)

@@ -44,7 +44,6 @@ def tile_list_order_lane_cost_kernel(
     with ExitStack() as ctx:
         keep = ctx.enter_context(tc.tile_pool(name="keep", bufs=1))
         ring = ctx.enter_context(tc.tile_pool(name="ring", bufs=1))
-        placed = ctx.enter_context(tc.tile_pool(name="placed", bufs=1))
         psum = ctx.enter_context(tc.psum_pool(name="psum", bufs=PACK))
 
         def handed_on(tag, shape, dtype):
@@ -64,7 +63,7 @@ def tile_list_order_lane_cost_kernel(
         w4_sc_raw = keep.tile([P, N], U8, name="w4_sc_raw")
         w4_codes = keep.tile([P, 2 * N], U8, name="w4_codes", align_bytes=64)
         w4_sc = keep.tile([P, N], U8, name="w4_sc", align_bytes=64)
-        h_codes = [keep.tile([P, BANK], U32, name="h_0_codes", align_bytes=64)]
+        h_codes = [keep.tile([P, BANK], U32, name="h_%d_codes" % half, align_bytes=64) for half in range(HALVES)]
         h_sc = keep.tile([P, S], U8, name="h_sc", align_bytes=64)
         y_codes = [keep.tile([P, S], U32, name="y_codes%d" % g, align_bytes=64) for g in range(GROUPS)]
 
@@ -216,7 +215,7 @@ def tile_list_order_lane_cost_kernel(
             codes = h_codes[half][:, c0 : c0 + width].bitcast(FP8X4)
             nc.vector.quantize_mx(out=codes, scales=h_sc[:, first : first + width], in_=rounded)
 
-        steps = [(g, half) for half in range(HALVES) for g in range(GROUPS)]
+        steps = [(g, half) for g in range(GROUPS) for half in range(HALVES)]
         last_step = len(steps) - 1
 
         def second_product(tag, codes, scales, half):
@@ -233,12 +232,11 @@ def tile_list_order_lane_cost_kernel(
             return bank
 
         def share_cells(step):
-            tag = "share%d" % step if step < GROUPS else "demand%d" % (step - GROUPS)
-            share = handed_on(tag, [P, PACK, BANK], F32)
+            g, half = steps[step]
+            share = handed_on(("demand%d" if half else "share%d") % g, [P, PACK, BANK], F32)
             cells = [share[:, t, :] for t in range(PACK)]
-            if step == 0:
-                cells[0] = handed_on("h_1_codes", [P, BANK], F32)[:]
-                cells[1] = handed_on("wc_1_codes", [P, BANK], F32)[:]
+            if step == 1:
+                cells[0] = handed_on("wc_1_codes", [P, BANK], F32)[:]
             if step == last_step:
                 cells[-1] = handed_on("y_sc", [P, BANK], F32)[:]
             return cells
@@ -297,11 +295,10 @@ def tile_list_order_lane_cost_kernel(
             sc_cols = slice(g * S + half * BANK, g * S + (half + 1) * BANK)
             codes = y_codes[g][:, cols]
             nc.vector.quantize_mx(out=codes.bitcast(FP8X4), scales=y_sc[:, sc_cols], in_=y_rounded[step][:])
-            words = out_1[g].rearrange("p m t -> p (m t)").bitcast(I32)
-            nc.sync.dma_start(out=words[:, cols], in_=codes.bitcast(I32))
 
-        def placed_rounded(name, offset):
-            return placed.tile([P, PACK * BANK], BF16, name=name, align_bytes=64, offset=offset)
+        def store_words(g, cols):
+            words = out_1[g].rearrange("p m t -> p (m t)").bitcast(I32)
+            nc.sync.dma_start(out=words[:, cols], in_=y_codes[g][:, cols].bitcast(I32))
 
         second_chunk = keep.tile([P, PACK * CHUNK], BF16, name="second_chunk", align_bytes=64)
         chunks = [stock_picked[:, PACK - 1, BANK:].bitcast(BF16), second_chunk[:]]
@@ -313,54 +310,76 @@ def tile_list_order_lane_cost_kernel(
             quantise_h(c * CHUNK, CHUNK, rounded)
         gather_stock(PACK - 1, BANK, BANK)
 
-        wc_rounded = [placed_rounded("wc_0_rounded", ROUNDED_BYTES), placed_rounded("wc_1_rounded", 0)]
-        for g in range(GROUPS):
-            round_weight(wc_pieces[g], wc_rounded[g][:])
-        wc_quantised = [quantise_weight(wc_rounded[0][:], "wc_0")]
-        cells = [shares(0)]
-        costs = [cost_plane(0, t) for t in range(PACK)]
-        second_half = placed_rounded("second_half", ROUNDED_BYTES)
+        def quantiser_input(tag):
+            return handed_on(tag, [P, PACK * BANK], BF16)
+
+        wc_rounded = round_weight(wc_pieces[0], quantiser_input("wc_0_rounded")[:])
+        cells = {0: shares(0)}
+        second_half = quantiser_input("turns")
         minimum(BANK, BANK, second_half[:])
-        cells.append(shares(1))
+        wc_quantised = [quantise_weight(wc_rounded, "wc_0")]
+        costs = [cost_plane(0, t) for t in range(PACK)]
+        cells[2] = shares(2)
+        quantise_h(BANK, BANK, second_half[:])
+        cells[1] = shares(1)
+        wc_rounded = quantiser_input("turns")[:]
+        m_piece = P // WC_PIECES
+        for i, raw in enumerate(wc_pieces[1]):
+            nc.gpsimd.tensor_scalar(
+                out=wc_rounded.rearrange("p (t m j) -> p m t j", t=PACK, j=PACK)[:, i * m_piece : (i + 1) * m_piece],
+                in0=raw.rearrange("p j (m t) -> p m t j", t=PACK),
+                scalar1=1.0,
+                scalar2=-0.0,
+                op0=ALU.mult,
+                op1=ALU.add,
+            )
 
         y = [lanes_tile(0)]
-        lanes_plane(0, 0, cells[0][0], costs[0])
-        lanes_plane(0, 1, cells[0][1], costs[1])
-        h_codes.append(handed_on("h_1_codes", [P, BANK], U32))
-        quantise_h(BANK, BANK, second_half[:])
-        lanes_plane(0, 2, cells[0][2], costs[2])
-        wc_quantised.append(quantise_weight(wc_rounded[1][:], "wc_1"))
-        lanes_plane(0, 3, cells[0][3], costs[3])
-        costs = [cost_plane(1, t) for t in range(PACK)]
-        cells.append(shares(2))
+        cells[3] = share_cells(3)
+        next_costs = []
+        for t in range(PACK):
+            lanes_plane(0, t, cells[0][t], costs[t])
+            next_costs.append(cost_plane(1, t))
+            share_plane(3, t, cells[3][t])
+        costs = next_costs
 
-        for step in range(1, len(steps)):
+        y.append(lanes_tile(1))
+        lanes_plane(1, 0, cells[1][0], costs[0])
+        lanes_plane(1, 1, cells[1][1], costs[1])
+        wc_quantised.append(quantise_weight(wc_rounded, "wc_1"))
+        next_costs = [cost_plane(2, 0), cost_plane(2, 1)]
+        for t in range(2, PACK):
+            lanes_plane(1, t, cells[1][t], costs[t])
+            next_costs.append(cost_plane(2, t))
+        costs = next_costs
+
+        for step in range(2, len(steps)):
             y.append(lanes_tile(step))
-            if step + 2 <= last_step:
-                cells.append(share_cells(step + 2))
             next_costs = []
             for t in range(PACK):
                 lanes_plane(step, t, cells[step][t], costs[t])
-                if step + 1 <= last_step:
+                if step < last_step:
                     next_costs.append(cost_plane(step + 1, t))
-                if step + 2 <= last_step:
-                    share_plane(step + 2, t, cells[step + 2][t])
             costs = next_costs
 
-        y_rounded = [placed_rounded("y_rounded0", ROUNDED_BYTES // 2)]
+        y_rounded = [quantiser_input("turns")]
         for step in range(1, len(steps)):
             y_rounded.append(keep.tile([P, PACK * BANK], BF16, name="y_rounded%d" % step, align_bytes=64))
         y_sc = handed_on("y_sc", [P, GROUPS * S], U8)
-        for step in range(GROUPS):
-            for c0 in range(0, BANK, CHUNK):
-                round_on_gpsimd(step, c0, c0 + CHUNK)
-        round_on_gpsimd(last_step - 1, 0, SLIVER)
-        round_on_scalar(last_step - 1, SLIVER, BANK)
+        round_on_gpsimd(0, 0, CHUNK)
+        round_on_gpsimd(0, CHUNK, BANK)
+        round_on_gpsimd(1, 0, CHUNK)
+        round_on_gpsimd(1, CHUNK, BANK - SLIVER)
+        round_on_scalar(1, BANK - SLIVER, BANK)
+        round_on_scalar(2, 0, BANK)
         round_on_scalar(last_step, 0, BANK - SLIVER)
         quantise_lanes(0)
         round_on_vector(last_step, BANK - SLIVER, BANK)
-        for step in range(1, len(steps)):
-            quantise_lanes(step)
+        quantise_lanes(1)
+        store_words(0, slice(0, S))
+        for half in range(HALVES):
+            quantise_lanes(GROUPS + half)
+            store_words(1, slice(half * BANK, (half + 1) * BANK))
 
         for q in range(QUADS):
             queue = nc.scalar if q % 2 else nc.sync

@@ -193,7 +193,7 @@ def tile_list_order_lane_cost_kernel(
             out=w4_codes[:].bitcast(U16).rearrange("p (g t m) -> p g m t", g=GROUPS, t=PACK),
             in_=w4_raw[:].bitcast(U16).rearrange("p (g m t) -> p g m t", g=GROUPS, t=PACK),
         )
-        wc_pieces = [load_weight(wc[:, g * K_PASS : (g + 1) * K_PASS], WC_PIECES) for g in range(GROUPS)]
+        wc_pieces = [load_weight(wc[:, :K_PASS], WC_PIECES), load_weight(wc[:, K_PASS:], 1)]
 
         def by_runs(planes):
             return planes.rearrange("p t (c i) -> p c t i", i=RUN)
@@ -235,8 +235,8 @@ def tile_list_order_lane_cost_kernel(
             g, half = steps[step]
             share = handed_on(("demand%d" if half else "share%d") % g, [P, PACK, BANK], F32)
             cells = [share[:, t, :] for t in range(PACK)]
-            if step == 1:
-                cells[0] = handed_on("wc_1_codes", [P, BANK], F32)[:]
+            if step == 0:
+                cells[PACK - 2] = handed_on("wc_1_codes", [P, BANK], F32)[:]
             if step == last_step:
                 cells[-1] = handed_on("y_sc", [P, BANK], F32)[:]
             return cells
@@ -285,16 +285,14 @@ def tile_list_order_lane_cost_kernel(
             out = woven_by_runs(y_rounded[step][:, PACK * c0 : PACK * c1])
             nc.scalar.copy(out=out, in_=by_runs(y[step][:, :, c0:c1]))
 
-        def round_on_vector(step, c0, c1):
-            out = woven_by_runs(y_rounded[step][:, PACK * c0 : PACK * c1])
-            nc.vector.tensor_copy(out=out, in_=by_runs(y[step][:, :, c0:c1]))
-
-        def quantise_lanes(step):
+        def quantise_lanes(step, c0, c1):
             g, half = steps[step]
-            cols = slice(half * BANK, (half + 1) * BANK)
-            sc_cols = slice(g * S + half * BANK, g * S + (half + 1) * BANK)
-            codes = y_codes[g][:, cols]
-            nc.vector.quantize_mx(out=codes.bitcast(FP8X4), scales=y_sc[:, sc_cols], in_=y_rounded[step][:])
+            first, end = half * BANK + c0, half * BANK + c1
+            nc.vector.quantize_mx(
+                out=y_codes[g][:, first:end].bitcast(FP8X4),
+                scales=y_sc[:, g * S + first : g * S + end],
+                in_=y_rounded[step][:, PACK * c0 : PACK * c1],
+            )
 
         def store_words(g, cols):
             words = out_1[g].rearrange("p m t -> p (m t)").bitcast(I32)
@@ -310,76 +308,68 @@ def tile_list_order_lane_cost_kernel(
             quantise_h(c * CHUNK, CHUNK, rounded)
         gather_stock(PACK - 1, BANK, BANK)
 
-        def quantiser_input(tag):
-            return handed_on(tag, [P, PACK * BANK], BF16)
+        width = PACK * BANK
+        turns = keep.tile([P, width + width // 2], BF16, name="turns", align_bytes=64)
+        second_half = turns[:, width // 2 :]
+        wc_rounded = [keep.tile([P, width], BF16, name="wc_0_rounded", align_bytes=64)[:], turns[:, :width]]
 
-        wc_rounded = round_weight(wc_pieces[0], quantiser_input("wc_0_rounded")[:])
-        cells = {0: shares(0)}
-        second_half = quantiser_input("turns")
-        minimum(BANK, BANK, second_half[:])
-        wc_quantised = [quantise_weight(wc_rounded, "wc_0")]
+        round_weight(wc_pieces[0], wc_rounded[0])
+        cells = [shares(0)]
+        minimum(BANK, BANK, second_half)
+        wc_quantised = [quantise_weight(wc_rounded[0], "wc_0")]
         costs = [cost_plane(0, t) for t in range(PACK)]
-        cells[2] = shares(2)
-        quantise_h(BANK, BANK, second_half[:])
-        cells[1] = shares(1)
-        wc_rounded = quantiser_input("turns")[:]
-        m_piece = P // WC_PIECES
-        for i, raw in enumerate(wc_pieces[1]):
-            nc.gpsimd.tensor_scalar(
-                out=wc_rounded.rearrange("p (t m j) -> p m t j", t=PACK, j=PACK)[:, i * m_piece : (i + 1) * m_piece],
-                in0=raw.rearrange("p j (m t) -> p m t j", t=PACK),
-                scalar1=1.0,
-                scalar2=-0.0,
-                op0=ALU.mult,
-                op1=ALU.add,
-            )
+        quantise_h(BANK, BANK, second_half)
+        raw = wc_pieces[1][0]
+        nc.scalar.copy(out=dealt(wc_rounded[1])[:, :, :, : PACK // 2], in_=undealt(raw)[:, :, :, : PACK // 2])
+        nc.gpsimd.tensor_scalar(
+            out=wc_rounded[1].rearrange("p (t m j) -> p m t j", t=PACK, j=PACK)[:, :, PACK // 2 :],
+            in0=raw.rearrange("p j (m t) -> p m t j", t=PACK)[:, :, PACK // 2 :],
+            scalar1=1.0,
+            scalar2=-0.0,
+            op0=ALU.mult,
+            op1=ALU.add,
+        )
+        cells += [share_cells(step) for step in range(1, len(steps))]
+        early = [(2, t) for t in range(PACK // 2)] + [(1, t) for t in range(PACK)]
+        late = [(2, t) for t in range(PACK // 2, PACK)] + [(3, t) for t in range(PACK)]
+        for step, t in early:
+            share_plane(step, t, cells[step][t])
 
-        y = [lanes_tile(0)]
-        cells[3] = share_cells(3)
-        next_costs = []
-        for t in range(PACK):
-            lanes_plane(0, t, cells[0][t], costs[t])
-            next_costs.append(cost_plane(1, t))
-            share_plane(3, t, cells[3][t])
-        costs = next_costs
-
-        y.append(lanes_tile(1))
-        lanes_plane(1, 0, cells[1][0], costs[0])
-        lanes_plane(1, 1, cells[1][1], costs[1])
-        wc_quantised.append(quantise_weight(wc_rounded, "wc_1"))
-        next_costs = [cost_plane(2, 0), cost_plane(2, 1)]
-        for t in range(2, PACK):
-            lanes_plane(1, t, cells[1][t], costs[t])
-            next_costs.append(cost_plane(2, t))
-        costs = next_costs
-
-        for step in range(2, len(steps)):
+        y = []
+        for step in range(len(steps)):
             y.append(lanes_tile(step))
+            if step == 1:
+                wc_quantised.append(quantise_weight(wc_rounded[1], "wc_1"))
             next_costs = []
             for t in range(PACK):
                 lanes_plane(step, t, cells[step][t], costs[t])
-                if step < last_step:
+                if step + 1 <= last_step:
                     next_costs.append(cost_plane(step + 1, t))
+                if PACK * step + t < len(late):
+                    later, plane = late[PACK * step + t]
+                    share_plane(later, plane, cells[later][plane])
             costs = next_costs
 
-        y_rounded = [quantiser_input("turns")]
+        y_rounded = [turns[:, :width]]
         for step in range(1, len(steps)):
             y_rounded.append(keep.tile([P, PACK * BANK], BF16, name="y_rounded%d" % step, align_bytes=64))
         y_sc = handed_on("y_sc", [P, GROUPS * S], U8)
         round_on_gpsimd(0, 0, CHUNK)
         round_on_gpsimd(0, CHUNK, BANK)
         round_on_gpsimd(1, 0, CHUNK)
-        round_on_gpsimd(1, CHUNK, BANK - SLIVER)
-        round_on_scalar(1, BANK - SLIVER, BANK)
-        round_on_scalar(2, 0, BANK)
+        round_on_gpsimd(1, CHUNK, BANK)
+        round_on_gpsimd(2, 0, SLIVER)
+        round_on_scalar(2, SLIVER, BANK)
         round_on_scalar(last_step, 0, BANK - SLIVER)
-        quantise_lanes(0)
-        round_on_vector(last_step, BANK - SLIVER, BANK)
-        quantise_lanes(1)
+        round_on_scalar(last_step, BANK - SLIVER, BANK)
+        quantise_lanes(0, 0, BANK)
+        quantise_lanes(1, 0, BANK)
         store_words(0, slice(0, S))
-        for half in range(HALVES):
-            quantise_lanes(GROUPS + half)
-            store_words(1, slice(half * BANK, (half + 1) * BANK))
+        quantise_lanes(2, 0, BANK)
+        store_words(1, slice(0, BANK))
+        for c0, c1 in ((0, BANK - SLIVER), (BANK - SLIVER, BANK)):
+            quantise_lanes(last_step, c0, c1)
+            store_words(1, slice(BANK + c0, BANK + c1))
 
         for q in range(QUADS):
             queue = nc.scalar if q % 2 else nc.sync

@@ -26,15 +26,15 @@ QUAD_ROWS = 4
 LIST_ROWS = 16
 BANK = 512
 HALVES = S // BANK
-CHUNK = BANK // 2
 RUN = 2
 WC_PIECES = 2
-ROUNDED_BYTES = 2 * PACK * BANK
+WIDTH = PACK * BANK
 
-SLIVER = 128
-
-RAW_BUFS = 3
-W1_ROUNDED_BUFS = 2
+W1_ON_VECTOR = (0, 48, 80)
+WC_ON_GPSIMD = 32
+Y_ON_GPSIMD = 192
+LAST_PART = 128
+RAW_BUFS = 4
 
 
 def tile_list_order_lane_cost_kernel(
@@ -49,41 +49,40 @@ def tile_list_order_lane_cost_kernel(
         def handed_on(tag, shape, dtype):
             return ring.tile(shape, dtype, name=tag, bufs=1, align_bytes=64)
 
+        def raw_tile(shape):
+            return ring.tile(shape, F32, name="raw", bufs=RAW_BUFS)
+
         offsets = keep.tile([P, S // LIST_ROWS], U16, name="offsets")
         bias = keep.tile([P, PACK], F32, name="bias")
-        table = [keep.tile([P, T], U32, name="table%d" % a) for a in range(PASSES - 1)]
-        table.append(handed_on("w1_0_codes", [P, T], U32))
+        table = [keep.tile([P, T], U32, name="table%d" % a) for a in range(PASSES)]
         table_sc = keep.tile([P, T], U8, name="table_sc")
         picked = [keep.tile([P, S], U32, name="picked%d" % a, align_bytes=64) for a in range(PASSES)]
         picked_sc = keep.tile([P, S], U8, name="picked_sc", align_bytes=64)
-        stock = [handed_on("w1_1_codes", [P, T], F32)]
-        stock += [keep.tile([P, T], F32, name="stock%d" % t) for t in range(1, PACK)]
+        stock = [keep.tile([P, T], F32, name="stock%d" % t) for t in range(PACK)]
         stock_picked = keep.tile([P, PACK, S], F32, name="stock_picked", align_bytes=64)
         w4_raw = keep.tile([P, 2 * N], U8, name="w4_raw")
         w4_sc_raw = keep.tile([P, N], U8, name="w4_sc_raw")
         w4_codes = keep.tile([P, 2 * N], U8, name="w4_codes", align_bytes=64)
         w4_sc = keep.tile([P, N], U8, name="w4_sc", align_bytes=64)
-        h_codes = [keep.tile([P, BANK], U32, name="h_%d_codes" % half, align_bytes=64) for half in range(HALVES)]
-        h_sc = keep.tile([P, S], U8, name="h_sc", align_bytes=64)
+        w1_codes = [keep.tile([P, K_PASS], U32, name="w1_codes%d" % a, align_bytes=64) for a in range(PASSES)]
+        w1_sc = [keep.tile([P, K_PASS], U8, name="w1_sc%d" % a, align_bytes=64) for a in range(PASSES)]
+        wc_codes = [keep.tile([P, K_PASS], U32, name="wc_codes%d" % g, align_bytes=64) for g in range(GROUPS)]
+        h_codes = [keep.tile([P, BANK], U32, name="h_codes%d" % half, align_bytes=64) for half in range(HALVES)]
+        first_sc = keep.tile([P, BANK], U8, name="first_sc", align_bytes=64)
+        h_sc = [first_sc[:], keep.tile([P, BANK], U8, name="h_sc1", align_bytes=64)[:]]
+        wc_sc = [first_sc[QUAD_ROWS:, :], keep.tile([P, K_PASS], U8, name="wc_sc1", align_bytes=64)[:]]
         y_codes = [keep.tile([P, S], U32, name="y_codes%d" % g, align_bytes=64) for g in range(GROUPS)]
 
-        def load_table(a):
+        def load_words(a):
             src = tab_words[a].rearrange("p n i -> p (n i)").bitcast(I32)
             nc.sync.dma_start(out=table[a][:].bitcast(I32), in_=src)
 
-        def gather_table(a):
-            nc.vector.tensor_copy(out=picked[a][:], in_=table[a][:].indirect(offsets[:]))
-
-        def load_stock(t):
-            nc.sync.dma_start(out=stock[t][:], in_=gT.rearrange("(p t) c -> t p c", t=PACK)[t])
-
-        def gather_stock(t, first, width):
-            entries = offsets[:, first // LIST_ROWS : (first + width) // LIST_ROWS]
-            nc.vector.tensor_copy(out=stock_picked[:, t, first : first + width], in_=stock[t][:].indirect(entries))
+        def entries(first, width):
+            return offsets[:, first // LIST_ROWS : (first + width) // LIST_ROWS]
 
         def load_weight(rows, pieces):
             width = K_PASS // pieces
-            raw = ring.tile([P, pieces, PACK, width], F32, name="raw", bufs=RAW_BUFS)
+            raw = raw_tile([P, pieces, PACK, width])
             for i in range(pieces):
                 src = rows[:, i * width : (i + 1) * width]
                 nc.sync.dma_start(out=raw[:, i], in_=src.rearrange("(p j) c -> p j c", j=PACK))
@@ -95,66 +94,57 @@ def tile_list_order_lane_cost_kernel(
         def dealt(rounded):
             return rounded.rearrange("p (t m j) -> p m j t", t=PACK, j=PACK)
 
-        def round_weight(pieces, rounded):
-            m_piece = P // len(pieces)
-            for i, raw in enumerate(pieces):
-                nc.scalar.copy(out=dealt(rounded)[:, i * m_piece : (i + 1) * m_piece], in_=undealt(raw))
-            return rounded
-
-        def quantise_weight(rounded, name):
-            codes = handed_on(name + "_codes", [P, K_PASS], U32)
-            scales = keep.tile([P, K_PASS], U8, name=name + "_sc", align_bytes=64)
-            nc.vector.quantize_mx(out=codes[:].bitcast(FP8X4), scales=scales[:], in_=rounded)
-            return codes, scales
-
-        def load_w1(a):
-            pieces = load_weight(w1[a * K_PASS : (a + 1) * K_PASS, :], 1)
-            rounded = ring.tile([P, PACK * K_PASS], BF16, name="w1_rounded", bufs=W1_ROUNDED_BUFS, align_bytes=64)
-            return pieces, rounded[:]
-
-        acc = [[psum.tile([P, BANK], F32, name=tag) for t in range(PACK)] for tag in ("route", "cost")]
-
-        def first_product(a, rounded):
-            codes, scales = quantise_weight(rounded, "w1_%d" % a)
-            for half in range(HALVES):
-                cols = slice(half * BANK, (half + 1) * BANK)
-                for t in range(PACK):
-                    places = slice(t * P, (t + 1) * P)
-                    nc.tensor.matmul_mx(
-                        out=acc[half][t][:],
-                        lhsT=codes[:, places].bitcast(FP8X4),
-                        lhsT_scale=scales[:, places],
-                        rhs=picked[a][:, cols].bitcast(FP8X4),
-                        rhs_scale=picked_sc[QUAD_ROWS * a :, cols],
-                        start=(a == 0),
-                        stop=(a == PASSES - 1),
-                    )
+        def quantise(codes, scales, rounded):
+            nc.vector.quantize_mx(out=codes.bitcast(FP8X4), scales=scales, in_=rounded)
 
         warm = keep.tile([P, 2], F32, name="warm")
         nc.vector.memset(warm[:, 0:1], 0.0)
         nc.scalar.activation(out=warm[:, 1:2], in_=warm[:, 0:1], func=ACT.Sigmoid)
 
         nc.gpsimd.memset(table_sc[:].bitcast(I32), 0)
+        nc.gpsimd.memset(w4_sc_raw[:].bitcast(I32), 0)
 
-        load_table(0)
+        acc = [[psum.tile([P, BANK], F32, name=tag) for t in range(PACK)] for tag in ("route", "cost")]
+
+        def gather_words(a):
+            nc.vector.tensor_copy(out=picked[a][:], in_=table[a][:].indirect(offsets[:]))
+
+        def first_product(a):
+            raw = load_weight(w1[a * K_PASS : (a + 1) * K_PASS, :], 1)[0]
+            rounded = ring.tile([P, WIDTH], BF16, name="w1_rounded", bufs=2, align_bytes=64)
+            m = P - W1_ON_VECTOR[a]
+            nc.scalar.copy(out=dealt(rounded[:])[:, :m], in_=undealt(raw)[:, :m])
+            if m < P:
+                nc.vector.tensor_copy(out=dealt(rounded[:])[:, m:], in_=undealt(raw)[:, m:])
+            quantise(w1_codes[a][:], w1_sc[a][:], rounded[:])
+            for half in range(HALVES):
+                cols = slice(half * BANK, (half + 1) * BANK)
+                for t in range(PACK):
+                    places = slice(t * P, (t + 1) * P)
+                    nc.tensor.matmul_mx(
+                        out=acc[half][t][:],
+                        lhsT=w1_codes[a][:, places].bitcast(FP8X4),
+                        lhsT_scale=w1_sc[a][:, places],
+                        rhs=picked[a][:, cols].bitcast(FP8X4),
+                        rhs_scale=picked_sc[QUAD_ROWS * a :, cols],
+                        start=(a == 0),
+                        stop=(a == PASSES - 1),
+                    )
+
+        load_words(0)
         nc.sync.dma_start(offsets[:], offs)
-        load_table(1)
+        load_words(1)
         for q in range(QUADS):
             nc.sync.dma_start(
                 out=table_sc[32 * q : 32 * q + QUAD_ROWS * PASSES, :].bitcast(I32),
                 in_=tab_scales[:, QUAD_ROWS * q : QUAD_ROWS * (q + 1), :].bitcast(I32),
             )
-        gather_table(0)
-        gather_table(1)
+        gather_words(0)
+        gather_words(1)
         nc.vector.tensor_copy(out=picked_sc[:], in_=table_sc[:].indirect(offsets[:]))
-
-        pieces, rounded = load_w1(0)
-        round_weight(pieces, rounded)
-        load_table(2)
-        gather_table(2)
-        first_product(0, rounded)
-
-        nc.gpsimd.memset(w4_sc_raw[:].bitcast(I32), 0)
+        first_product(0)
+        load_words(2)
+        gather_words(2)
         for q in range(QUADS):
             nc.sync.dma_start(
                 out=w4_sc_raw[32 * q : 32 * q + QUAD_ROWS, :].bitcast(I32),
@@ -165,17 +155,8 @@ def tile_list_order_lane_cost_kernel(
             out=w4_sc[:].rearrange("p (g t m) -> p g t m", g=GROUPS, t=PACK),
             in_=w4_sc_raw[:].rearrange("p (g m t) -> p g t m", g=GROUPS, t=PACK),
         )
-
-        pieces, rounded = load_w1(1)
-        round_weight(pieces, rounded)
-        load_stock(0)
-        gather_stock(0, 0, S)
-        first_product(1, rounded)
-
-        pieces, rounded = load_w1(2)
-        nc.scalar.copy(out=dealt(rounded)[:, : P // 2], in_=undealt(pieces[0])[:, : P // 2])
-        nc.vector.tensor_copy(out=dealt(rounded)[:, P // 2 :], in_=undealt(pieces[0])[:, P // 2 :])
-        first_product(2, rounded)
+        first_product(1)
+        first_product(2)
 
         demand = [handed_on("demand%d" % half, [P, PACK, BANK], F32) for half in range(HALVES)]
         for half in range(HALVES):
@@ -184,16 +165,34 @@ def tile_list_order_lane_cost_kernel(
                     out=demand[half][:, t, :], in_=acc[half][t][:], func=ACT.Relu, bias=bias[:, t : t + 1]
                 )
 
-        for t in range(1, PACK):
-            load_stock(t)
-            if t < PACK - 1:
-                gather_stock(t, 0, S)
+        for t in range(PACK):
+            nc.sync.dma_start(out=stock[t][:], in_=gT.rearrange("(p t) c -> t p c", t=PACK)[t])
+            width = S if t < PACK - 1 else BANK
+            for first in range(0, S, width):
+                nc.vector.tensor_copy(
+                    out=stock_picked[:, t, first : first + width], in_=stock[t][:].indirect(entries(first, width))
+                )
+
+        lap_gpsimd = PACK * WC_ON_GPSIMD
+        lap_wc = 64
+        turns = keep.tile([P, 3 * WIDTH - lap_gpsimd - lap_wc], BF16, name="turns", align_bytes=64)
+        h_start = WIDTH - lap_gpsimd
+        wc_start = h_start + WIDTH - lap_wc
+        wc_rounded = [turns[:, wc_start:], turns[:, :WIDTH]]
+        h_first = keep.tile([P, WIDTH], BF16, name="h_first", align_bytes=64)
+        h_rounded = [h_first[:], turns[:, h_start : h_start + WIDTH]]
+
+        m_piece = P // WC_PIECES
+        pieces = load_weight(wc[:, :K_PASS], WC_PIECES)
+        for i in range(WC_PIECES):
+            nc.scalar.copy(out=dealt(wc_rounded[0])[:, i * m_piece : (i + 1) * m_piece], in_=undealt(pieces[i]))
         nc.sync.dma_start(out=w4_raw[:].bitcast(I32), in_=w4_words[0].bitcast(I32))
         nc.scalar.copy(
             out=w4_codes[:].bitcast(U16).rearrange("p (g t m) -> p g m t", g=GROUPS, t=PACK),
             in_=w4_raw[:].bitcast(U16).rearrange("p (g m t) -> p g m t", g=GROUPS, t=PACK),
         )
-        wc_pieces = [load_weight(wc[:, :K_PASS], WC_PIECES), load_weight(wc[:, K_PASS:], 1)]
+        pieces = load_weight(wc[:, K_PASS:], WC_PIECES)
+        nc.scalar.copy(out=dealt(wc_rounded[1])[:, :m_piece], in_=undealt(pieces[0]))
 
         def by_runs(planes):
             return planes.rearrange("p t (c i) -> p c t i", i=RUN)
@@ -201,19 +200,13 @@ def tile_list_order_lane_cost_kernel(
         def woven_by_runs(rounded):
             return rounded.rearrange("p (c i t) -> p c t i", i=RUN, t=PACK)
 
-        def minimum(first, width, rounded):
-            half, c0 = divmod(first, BANK)
+        def minimum(half):
             nc.vector.tensor_tensor(
-                out=woven_by_runs(rounded),
-                in0=by_runs(demand[half][:, :, c0 : c0 + width]),
-                in1=by_runs(stock_picked[:, :, first : first + width]),
+                out=woven_by_runs(h_rounded[half]),
+                in0=by_runs(demand[half][:]),
+                in1=by_runs(stock_picked[:, :, half * BANK : (half + 1) * BANK]),
                 op=ALU.min,
             )
-
-        def quantise_h(first, width, rounded):
-            half, c0 = divmod(first, BANK)
-            codes = h_codes[half][:, c0 : c0 + width].bitcast(FP8X4)
-            nc.vector.quantize_mx(out=codes, scales=h_sc[:, first : first + width], in_=rounded)
 
         steps = [(g, half) for g in range(GROUPS) for half in range(HALVES)]
         last_step = len(steps) - 1
@@ -225,51 +218,81 @@ def tile_list_order_lane_cost_kernel(
                 lhsT=codes,
                 lhsT_scale=scales,
                 rhs=h_codes[half][:].bitcast(FP8X4),
-                rhs_scale=h_sc[:, half * BANK : (half + 1) * BANK],
+                rhs_scale=h_sc[half],
                 start=True,
                 stop=True,
             )
             return bank
 
-        def share_cells(step):
-            g, half = steps[step]
-            share = handed_on(("demand%d" if half else "share%d") % g, [P, PACK, BANK], F32)
-            cells = [share[:, t, :] for t in range(PACK)]
-            if step == 0:
-                cells[PACK - 2] = handed_on("wc_1_codes", [P, BANK], F32)[:]
-            if step == last_step:
-                cells[-1] = handed_on("y_sc", [P, BANK], F32)[:]
-            return cells
-
-        def share_plane(step, t, cell):
+        def share_plane(step, t):
             g, half = steps[step]
             first = g * K_PASS + t * P
             codes = w4_codes[:, 2 * first : 2 * (first + P)].bitcast(FP4X4)
             route = second_product("route", codes, w4_sc[:, first : first + P], half)
-            nc.scalar.activation(out=cell, in_=route[:], func=ACT.Sigmoid)
-
-        def shares(step):
-            cells = share_cells(step)
-            for t in range(PACK):
-                share_plane(step, t, cells[t])
-            return cells
+            nc.scalar.activation(out=cells[step][t], in_=route[:], func=ACT.Sigmoid)
 
         def cost_plane(step, t):
             g, half = steps[step]
-            codes, scales = wc_quantised[g]
             places = slice(t * P, (t + 1) * P)
-            return second_product("cost", codes[:, places].bitcast(FP8X4), scales[:, places], half)
+            return second_product("cost", wc_codes[g][:, places].bitcast(FP8X4), wc_sc[g][:, places], half)
 
-        def lanes_tile(step):
-            if step < RAW_BUFS:
-                return ring.tile([P, PACK, BANK], F32, name="raw", bufs=RAW_BUFS)
-            return keep.tile([P, PACK, BANK], F32, name="y_last")
-
-        def lanes_plane(step, t, cell, cost):
+        def lanes_plane(step, t, cost):
             g, half = steps[step]
             rows = out_0[g * K_PASS : (g + 1) * K_PASS, half * BANK : (half + 1) * BANK]
-            nc.vector.tensor_tensor(out=y[step][:, t, :], in0=cell, in1=cost[:], op=ALU.mult)
+            nc.vector.tensor_tensor(out=y[step][:, t, :], in0=cells[step][t], in1=cost[:], op=ALU.mult)
             nc.sync.dma_start(out=rows.rearrange("(p t) c -> t p c", t=PACK)[t], in_=y[step][:, t, :])
+
+        minimum(0)
+        quantise(wc_codes[0][:], wc_sc[0], wc_rounded[0])
+        quantise(h_codes[0][:], h_sc[0], h_rounded[0])
+        minimum(1)
+
+        cells = []
+        for step in range(len(steps)):
+            g, half = steps[step]
+            share = handed_on(("demand%d" if g else "share%d") % half, [P, PACK, BANK], F32)
+            cells.append([share[:, t, :] for t in range(PACK)])
+        cells[last_step][-1] = handed_on("y_sc", [P, BANK], F32)[:]
+        y = [raw_tile([P, PACK, BANK]) for step in range(len(steps))]
+
+        costs = []
+        share_plane(0, 0)
+        for t in range(PACK):
+            if t + 1 < PACK:
+                share_plane(0, t + 1)
+            costs.append(cost_plane(0, t))
+
+        m_scalar = P - WC_ON_GPSIMD - m_piece
+        nc.scalar.copy(
+            out=dealt(wc_rounded[1])[:, m_piece : m_piece + m_scalar], in_=undealt(pieces[1])[:, :m_scalar]
+        )
+        share_plane(2, 0)
+        for step in range(len(steps)):
+            next_costs = []
+            for t in range(PACK):
+                lanes_plane(step, t, costs[t])
+                if (step, t) == (0, 0):
+                    quantise(h_codes[1][:], h_sc[1], h_rounded[1])
+                    nc.gpsimd.tensor_scalar(
+                        out=wc_rounded[1].rearrange("p (t m j) -> p m t j", t=PACK, j=PACK)[:, m_piece + m_scalar :],
+                        in0=pieces[1].rearrange("p j (m t) -> p m t j", t=PACK)[:, m_scalar:],
+                        scalar1=1.0,
+                        scalar2=-0.0,
+                        op0=ALU.mult,
+                        op1=ALU.add,
+                    )
+                if (step, t) == (0, PACK - 1):
+                    quantise(wc_codes[1][:], wc_sc[1], wc_rounded[1])
+                if step < last_step:
+                    if (step + 1, t) != (2, 0):
+                        share_plane(step + 1, t)
+                    next_costs.append(cost_plane(step + 1, t))
+            costs = next_costs
+
+        y_rounded = [turns[:, :WIDTH], turns[:, WIDTH : 2 * WIDTH]]
+        for step in range(2, len(steps)):
+            y_rounded.append(keep.tile([P, WIDTH], BF16, name="y_rounded%d" % step, align_bytes=64))
+        y_sc = handed_on("y_sc", [P, GROUPS * S], U8)
 
         def round_on_gpsimd(step, c0, c1):
             nc.gpsimd.tensor_scalar(
@@ -288,86 +311,26 @@ def tile_list_order_lane_cost_kernel(
         def quantise_lanes(step, c0, c1):
             g, half = steps[step]
             first, end = half * BANK + c0, half * BANK + c1
-            nc.vector.quantize_mx(
-                out=y_codes[g][:, first:end].bitcast(FP8X4),
-                scales=y_sc[:, g * S + first : g * S + end],
-                in_=y_rounded[step][:, PACK * c0 : PACK * c1],
+            quantise(
+                y_codes[g][:, first:end], y_sc[:, g * S + first : g * S + end], y_rounded[step][:, PACK * c0 : PACK * c1]
             )
 
         def store_words(g, cols):
             words = out_1[g].rearrange("p m t -> p (m t)").bitcast(I32)
             nc.sync.dma_start(out=words[:, cols], in_=y_codes[g][:, cols].bitcast(I32))
 
-        second_chunk = keep.tile([P, PACK * CHUNK], BF16, name="second_chunk", align_bytes=64)
-        chunks = [stock_picked[:, PACK - 1, BANK:].bitcast(BF16), second_chunk[:]]
-        for c in range(len(chunks)):
-            gather_stock(PACK - 1, c * CHUNK, CHUNK)
-        for c, rounded in enumerate(chunks):
-            minimum(c * CHUNK, CHUNK, rounded)
-        for c, rounded in enumerate(chunks):
-            quantise_h(c * CHUNK, CHUNK, rounded)
-        gather_stock(PACK - 1, BANK, BANK)
-
-        width = PACK * BANK
-        turns = keep.tile([P, width + width // 2], BF16, name="turns", align_bytes=64)
-        second_half = turns[:, width // 2 :]
-        wc_rounded = [keep.tile([P, width], BF16, name="wc_0_rounded", align_bytes=64)[:], turns[:, :width]]
-
-        round_weight(wc_pieces[0], wc_rounded[0])
-        cells = [shares(0)]
-        minimum(BANK, BANK, second_half)
-        wc_quantised = [quantise_weight(wc_rounded[0], "wc_0")]
-        costs = [cost_plane(0, t) for t in range(PACK)]
-        quantise_h(BANK, BANK, second_half)
-        raw = wc_pieces[1][0]
-        nc.scalar.copy(out=dealt(wc_rounded[1])[:, :, :, : PACK // 2], in_=undealt(raw)[:, :, :, : PACK // 2])
-        nc.gpsimd.tensor_scalar(
-            out=wc_rounded[1].rearrange("p (t m j) -> p m t j", t=PACK, j=PACK)[:, :, PACK // 2 :],
-            in0=raw.rearrange("p j (m t) -> p m t j", t=PACK)[:, :, PACK // 2 :],
-            scalar1=1.0,
-            scalar2=-0.0,
-            op0=ALU.mult,
-            op1=ALU.add,
-        )
-        cells += [share_cells(step) for step in range(1, len(steps))]
-        early = [(2, t) for t in range(PACK // 2)] + [(1, t) for t in range(PACK)]
-        late = [(2, t) for t in range(PACK // 2, PACK)] + [(3, t) for t in range(PACK)]
-        for step, t in early:
-            share_plane(step, t, cells[step][t])
-
-        y = []
-        for step in range(len(steps)):
-            y.append(lanes_tile(step))
-            if step == 1:
-                wc_quantised.append(quantise_weight(wc_rounded[1], "wc_1"))
-            next_costs = []
-            for t in range(PACK):
-                lanes_plane(step, t, cells[step][t], costs[t])
-                if step + 1 <= last_step:
-                    next_costs.append(cost_plane(step + 1, t))
-                if PACK * step + t < len(late):
-                    later, plane = late[PACK * step + t]
-                    share_plane(later, plane, cells[later][plane])
-            costs = next_costs
-
-        y_rounded = [turns[:, :width]]
-        for step in range(1, len(steps)):
-            y_rounded.append(keep.tile([P, PACK * BANK], BF16, name="y_rounded%d" % step, align_bytes=64))
-        y_sc = handed_on("y_sc", [P, GROUPS * S], U8)
-        round_on_gpsimd(0, 0, CHUNK)
-        round_on_gpsimd(0, CHUNK, BANK)
-        round_on_gpsimd(1, 0, CHUNK)
-        round_on_gpsimd(1, CHUNK, BANK)
-        round_on_gpsimd(2, 0, SLIVER)
-        round_on_scalar(2, SLIVER, BANK)
-        round_on_scalar(last_step, 0, BANK - SLIVER)
-        round_on_scalar(last_step, BANK - SLIVER, BANK)
-        quantise_lanes(0, 0, BANK)
-        quantise_lanes(1, 0, BANK)
+        for step in range(2):
+            round_on_gpsimd(step, 0, BANK // 2)
+            round_on_gpsimd(step, BANK // 2, BANK)
+        round_on_gpsimd(2, 0, Y_ON_GPSIMD)
+        round_on_scalar(2, Y_ON_GPSIMD, BANK)
+        round_on_scalar(last_step, 0, BANK - LAST_PART)
+        round_on_scalar(last_step, BANK - LAST_PART, BANK)
+        quantise(y_codes[0][:], y_sc[:, :S], turns[:, : 2 * WIDTH])
         store_words(0, slice(0, S))
         quantise_lanes(2, 0, BANK)
         store_words(1, slice(0, BANK))
-        for c0, c1 in ((0, BANK - SLIVER), (BANK - SLIVER, BANK)):
+        for c0, c1 in ((0, BANK - LAST_PART), (BANK - LAST_PART, BANK)):
             quantise_lanes(last_step, c0, c1)
             store_words(1, slice(BANK + c0, BANK + c1))
 

@@ -32,8 +32,9 @@ WIDTH = PACK * BANK
 
 W1_ON_VECTOR = (0, 48, 80)
 WC_ON_GPSIMD = 32
-Y_ON_GPSIMD = 192
-LAST_PART = 128
+Y_ON_GPSIMD = 160
+Y_ON_VECTOR = 128
+CHUNK = BANK // 2
 RAW_BUFS = 4
 
 
@@ -66,11 +67,9 @@ def tile_list_order_lane_cost_kernel(
         w4_sc = keep.tile([P, N], U8, name="w4_sc", align_bytes=64)
         w1_codes = [keep.tile([P, K_PASS], U32, name="w1_codes%d" % a, align_bytes=64) for a in range(PASSES)]
         w1_sc = [keep.tile([P, K_PASS], U8, name="w1_sc%d" % a, align_bytes=64) for a in range(PASSES)]
-        wc_codes = [keep.tile([P, K_PASS], U32, name="wc_codes%d" % g, align_bytes=64) for g in range(GROUPS)]
         h_codes = [keep.tile([P, BANK], U32, name="h_codes%d" % half, align_bytes=64) for half in range(HALVES)]
-        first_sc = keep.tile([P, BANK], U8, name="first_sc", align_bytes=64)
-        h_sc = [first_sc[:], keep.tile([P, BANK], U8, name="h_sc1", align_bytes=64)[:]]
-        wc_sc = [first_sc[QUAD_ROWS:, :], keep.tile([P, K_PASS], U8, name="wc_sc1", align_bytes=64)[:]]
+        h_sc = [keep.tile([P, BANK], U8, name="h_sc%d" % half, align_bytes=64)[:] for half in range(HALVES)]
+        wc_sc = [keep.tile([P, K_PASS], U8, name="wc_sc%d" % g, align_bytes=64)[:] for g in range(GROUPS)]
         y_codes = [keep.tile([P, S], U32, name="y_codes%d" % g, align_bytes=64) for g in range(GROUPS)]
 
         def load_words(a):
@@ -165,34 +164,39 @@ def tile_list_order_lane_cost_kernel(
                     out=demand[half][:, t, :], in_=acc[half][t][:], func=ACT.Relu, bias=bias[:, t : t + 1]
                 )
 
+        def gather_stock(t, first, width):
+            nc.vector.tensor_copy(
+                out=stock_picked[:, t, first : first + width], in_=stock[t][:].indirect(entries(first, width))
+            )
+
         for t in range(PACK):
             nc.sync.dma_start(out=stock[t][:], in_=gT.rearrange("(p t) c -> t p c", t=PACK)[t])
-            width = S if t < PACK - 1 else BANK
-            for first in range(0, S, width):
-                nc.vector.tensor_copy(
-                    out=stock_picked[:, t, first : first + width], in_=stock[t][:].indirect(entries(first, width))
-                )
+            if t < PACK - 1:
+                gather_stock(t, 0, S)
 
         lap_gpsimd = PACK * WC_ON_GPSIMD
-        lap_wc = 64
-        turns = keep.tile([P, 3 * WIDTH - lap_gpsimd - lap_wc], BF16, name="turns", align_bytes=64)
-        h_start = WIDTH - lap_gpsimd
-        wc_start = h_start + WIDTH - lap_wc
-        wc_rounded = [turns[:, wc_start:], turns[:, :WIDTH]]
-        h_first = keep.tile([P, WIDTH], BF16, name="h_first", align_bytes=64)
-        h_rounded = [h_first[:], turns[:, h_start : h_start + WIDTH]]
+        turns = keep.tile([P, 2 * WIDTH], BF16, name="turns", align_bytes=64)
+        wc_first = keep.tile([P, WIDTH], BF16, name="wc_first", align_bytes=64)
+        wc_rounded = [wc_first[:], turns[:, :WIDTH]]
+        h_middle = keep.tile([P, 2, PACK * CHUNK], BF16, name="h_middle", align_bytes=64)
+        h_last = WIDTH - lap_gpsimd
+        h_rounded = [
+            stock_picked[:, PACK - 1, BANK:].bitcast(BF16),
+            h_middle[:, 0, :],
+            h_middle[:, 1, :],
+            turns[:, h_last : h_last + PACK * CHUNK],
+        ]
 
-        m_piece = P // WC_PIECES
-        pieces = load_weight(wc[:, :K_PASS], WC_PIECES)
-        for i in range(WC_PIECES):
-            nc.scalar.copy(out=dealt(wc_rounded[0])[:, i * m_piece : (i + 1) * m_piece], in_=undealt(pieces[i]))
         nc.sync.dma_start(out=w4_raw[:].bitcast(I32), in_=w4_words[0].bitcast(I32))
         nc.scalar.copy(
             out=w4_codes[:].bitcast(U16).rearrange("p (g t m) -> p g m t", g=GROUPS, t=PACK),
             in_=w4_raw[:].bitcast(U16).rearrange("p (g m t) -> p g m t", g=GROUPS, t=PACK),
         )
-        pieces = load_weight(wc[:, K_PASS:], WC_PIECES)
-        nc.scalar.copy(out=dealt(wc_rounded[1])[:, :m_piece], in_=undealt(pieces[0]))
+        m_piece = P // WC_PIECES
+        pieces = load_weight(wc[:, :K_PASS], WC_PIECES)
+        for i in range(WC_PIECES):
+            nc.scalar.copy(out=dealt(wc_rounded[0])[:, i * m_piece : (i + 1) * m_piece], in_=undealt(pieces[i]))
+        wc_last = load_weight(wc[:, K_PASS:], 1)[0]
 
         def by_runs(planes):
             return planes.rearrange("p t (c i) -> p c t i", i=RUN)
@@ -200,13 +204,18 @@ def tile_list_order_lane_cost_kernel(
         def woven_by_runs(rounded):
             return rounded.rearrange("p (c i t) -> p c t i", i=RUN, t=PACK)
 
-        def minimum(half):
+        def minimum(c):
+            half, c0 = divmod(c * CHUNK, BANK)
             nc.vector.tensor_tensor(
-                out=woven_by_runs(h_rounded[half]),
-                in0=by_runs(demand[half][:]),
-                in1=by_runs(stock_picked[:, :, half * BANK : (half + 1) * BANK]),
+                out=woven_by_runs(h_rounded[c]),
+                in0=by_runs(demand[half][:, :, c0 : c0 + CHUNK]),
+                in1=by_runs(stock_picked[:, :, c * CHUNK : (c + 1) * CHUNK]),
                 op=ALU.min,
             )
+
+        def quantise_h(c):
+            half, c0 = divmod(c * CHUNK, BANK)
+            quantise(h_codes[half][:, c0 : c0 + CHUNK], h_sc[half][:, c0 : c0 + CHUNK], h_rounded[c])
 
         steps = [(g, half) for g in range(GROUPS) for half in range(HALVES)]
         last_step = len(steps) - 1
@@ -242,46 +251,49 @@ def tile_list_order_lane_cost_kernel(
             nc.vector.tensor_tensor(out=y[step][:, t, :], in0=cells[step][t], in1=cost[:], op=ALU.mult)
             nc.sync.dma_start(out=rows.rearrange("(p t) c -> t p c", t=PACK)[t], in_=y[step][:, t, :])
 
-        minimum(0)
+        for work in (lambda c: gather_stock(PACK - 1, c * CHUNK, CHUNK), minimum, quantise_h):
+            work(0)
+            work(1)
+        gather_stock(PACK - 1, 2 * CHUNK, CHUNK)
+        gather_stock(PACK - 1, 3 * CHUNK, CHUNK)
+        minimum(2)
+        wc_codes = [keep.tile([P, K_PASS], U32, name="wc_codes0", align_bytes=64)]
         quantise(wc_codes[0][:], wc_sc[0], wc_rounded[0])
-        quantise(h_codes[0][:], h_sc[0], h_rounded[0])
-        minimum(1)
+        minimum(3)
+        quantise_h(2)
 
         cells = []
         for step in range(len(steps)):
             g, half = steps[step]
             share = handed_on(("demand%d" if g else "share%d") % half, [P, PACK, BANK], F32)
             cells.append([share[:, t, :] for t in range(PACK)])
+        cells[0][PACK - 2] = handed_on("wc_codes1", [P, BANK], F32)[:]
         cells[last_step][-1] = handed_on("y_sc", [P, BANK], F32)[:]
         y = [raw_tile([P, PACK, BANK]) for step in range(len(steps))]
 
-        costs = []
-        share_plane(0, 0)
         for t in range(PACK):
-            if t + 1 < PACK:
-                share_plane(0, t + 1)
-            costs.append(cost_plane(0, t))
+            share_plane(0, t)
+        costs = [cost_plane(0, t) for t in range(PACK)]
 
-        m_scalar = P - WC_ON_GPSIMD - m_piece
-        nc.scalar.copy(
-            out=dealt(wc_rounded[1])[:, m_piece : m_piece + m_scalar], in_=undealt(pieces[1])[:, :m_scalar]
-        )
+        m_scalar = P - WC_ON_GPSIMD
+        nc.scalar.copy(out=dealt(wc_rounded[1])[:, :m_scalar], in_=undealt(wc_last)[:, :m_scalar])
         share_plane(2, 0)
         for step in range(len(steps)):
             next_costs = []
             for t in range(PACK):
                 lanes_plane(step, t, costs[t])
                 if (step, t) == (0, 0):
-                    quantise(h_codes[1][:], h_sc[1], h_rounded[1])
+                    quantise_h(3)
                     nc.gpsimd.tensor_scalar(
-                        out=wc_rounded[1].rearrange("p (t m j) -> p m t j", t=PACK, j=PACK)[:, m_piece + m_scalar :],
-                        in0=pieces[1].rearrange("p j (m t) -> p m t j", t=PACK)[:, m_scalar:],
+                        out=wc_rounded[1].rearrange("p (t m j) -> p m t j", t=PACK, j=PACK)[:, m_scalar:],
+                        in0=wc_last.rearrange("p j (m t) -> p m t j", t=PACK)[:, m_scalar:],
                         scalar1=1.0,
                         scalar2=-0.0,
                         op0=ALU.mult,
                         op1=ALU.add,
                     )
                 if (step, t) == (0, PACK - 1):
+                    wc_codes.append(handed_on("wc_codes1", [P, K_PASS], U32))
                     quantise(wc_codes[1][:], wc_sc[1], wc_rounded[1])
                 if step < last_step:
                     if (step + 1, t) != (2, 0):
@@ -324,15 +336,16 @@ def tile_list_order_lane_cost_kernel(
             round_on_gpsimd(step, BANK // 2, BANK)
         round_on_gpsimd(2, 0, Y_ON_GPSIMD)
         round_on_scalar(2, Y_ON_GPSIMD, BANK)
-        round_on_scalar(last_step, 0, BANK - LAST_PART)
-        round_on_scalar(last_step, BANK - LAST_PART, BANK)
+        round_on_scalar(last_step, 0, BANK - Y_ON_VECTOR)
         quantise(y_codes[0][:], y_sc[:, :S], turns[:, : 2 * WIDTH])
         store_words(0, slice(0, S))
-        quantise_lanes(2, 0, BANK)
-        store_words(1, slice(0, BANK))
-        for c0, c1 in ((0, BANK - LAST_PART), (BANK - LAST_PART, BANK)):
-            quantise_lanes(last_step, c0, c1)
-            store_words(1, slice(BANK + c0, BANK + c1))
+        nc.vector.tensor_copy(
+            out=woven_by_runs(y_rounded[last_step][:, PACK * (BANK - Y_ON_VECTOR) :]),
+            in_=by_runs(y[last_step][:, :, BANK - Y_ON_VECTOR :]),
+        )
+        for step in range(2, len(steps)):
+            quantise_lanes(step, 0, BANK)
+            store_words(1, slice((step - 2) * BANK, (step - 1) * BANK))
 
         for q in range(QUADS):
             queue = nc.scalar if q % 2 else nc.sync

@@ -32,7 +32,8 @@ WIDTH = PACK * BANK
 
 W1_ON_VECTOR = (0, 48, 80)
 WC_ON_GPSIMD = 32
-Y_ON_GPSIMD = 160
+Y_ON_GPSIMD = 64
+Y_EARLY = 128
 Y_ON_VECTOR = 128
 CHUNK = BANK // 2
 RAW_BUFS = 4
@@ -177,9 +178,10 @@ def tile_list_order_lane_cost_kernel(
         lap_gpsimd = PACK * WC_ON_GPSIMD
         turns = keep.tile([P, 2 * WIDTH], BF16, name="turns", align_bytes=64)
         wc_first = keep.tile([P, WIDTH], BF16, name="wc_first", align_bytes=64)
-        wc_rounded = [wc_first[:], turns[:, :WIDTH]]
+        wc_start = PACK * Y_EARLY
+        wc_rounded = [wc_first[:], turns[:, wc_start : wc_start + WIDTH]]
         h_middle = keep.tile([P, 2, PACK * CHUNK], BF16, name="h_middle", align_bytes=64)
-        h_last = WIDTH - lap_gpsimd
+        h_last = wc_start + WIDTH - lap_gpsimd
         h_rounded = [
             stock_picked[:, PACK - 1, BANK:].bitcast(BF16),
             h_middle[:, 0, :],
@@ -196,7 +198,8 @@ def tile_list_order_lane_cost_kernel(
         pieces = load_weight(wc[:, :K_PASS], WC_PIECES)
         for i in range(WC_PIECES):
             nc.scalar.copy(out=dealt(wc_rounded[0])[:, i * m_piece : (i + 1) * m_piece], in_=undealt(pieces[i]))
-        wc_last = load_weight(wc[:, K_PASS:], 1)[0]
+        pieces = load_weight(wc[:, K_PASS:], WC_PIECES)
+        nc.scalar.copy(out=dealt(wc_rounded[1])[:, :m_piece], in_=undealt(pieces[0]))
 
         def by_runs(planes):
             return planes.rearrange("p t (c i) -> p c t i", i=RUN)
@@ -267,7 +270,7 @@ def tile_list_order_lane_cost_kernel(
             g, half = steps[step]
             share = handed_on(("demand%d" if g else "share%d") % half, [P, PACK, BANK], F32)
             cells.append([share[:, t, :] for t in range(PACK)])
-        cells[0][PACK - 2] = handed_on("wc_codes1", [P, BANK], F32)[:]
+        cells[1][0] = handed_on("wc_codes1", [P, BANK], F32)[:]
         cells[last_step][-1] = handed_on("y_sc", [P, BANK], F32)[:]
         y = [raw_tile([P, PACK, BANK]) for step in range(len(steps))]
 
@@ -275,9 +278,14 @@ def tile_list_order_lane_cost_kernel(
             share_plane(0, t)
         costs = [cost_plane(0, t) for t in range(PACK)]
 
-        m_scalar = P - WC_ON_GPSIMD
-        nc.scalar.copy(out=dealt(wc_rounded[1])[:, :m_scalar], in_=undealt(wc_last)[:, :m_scalar])
-        share_plane(2, 0)
+        m_scalar = P - WC_ON_GPSIMD - m_piece
+        nc.scalar.copy(
+            out=dealt(wc_rounded[1])[:, m_piece : m_piece + m_scalar], in_=undealt(pieces[1])[:, :m_scalar]
+        )
+        early = [(2, 0), (2, 1)]
+        for step, t in early:
+            share_plane(step, t)
+        waiting = []
         for step in range(len(steps)):
             next_costs = []
             for t in range(PACK):
@@ -285,20 +293,23 @@ def tile_list_order_lane_cost_kernel(
                 if (step, t) == (0, 0):
                     quantise_h(3)
                     nc.gpsimd.tensor_scalar(
-                        out=wc_rounded[1].rearrange("p (t m j) -> p m t j", t=PACK, j=PACK)[:, m_scalar:],
-                        in0=wc_last.rearrange("p j (m t) -> p m t j", t=PACK)[:, m_scalar:],
+                        out=wc_rounded[1].rearrange("p (t m j) -> p m t j", t=PACK, j=PACK)[:, m_piece + m_scalar :],
+                        in0=pieces[1].rearrange("p j (m t) -> p m t j", t=PACK)[:, m_scalar:],
                         scalar1=1.0,
                         scalar2=-0.0,
                         op0=ALU.mult,
                         op1=ALU.add,
                     )
-                if (step, t) == (0, PACK - 1):
+                if (step, t) == (1, 1):
                     wc_codes.append(handed_on("wc_codes1", [P, K_PASS], U32))
                     quantise(wc_codes[1][:], wc_sc[1], wc_rounded[1])
                 if step < last_step:
-                    if (step + 1, t) != (2, 0):
+                    if (step + 1, t) not in early:
                         share_plane(step + 1, t)
-                    next_costs.append(cost_plane(step + 1, t))
+                    waiting.append(t)
+                    if steps[step + 1][0] < len(wc_codes):
+                        next_costs += [cost_plane(step + 1, u) for u in waiting]
+                        waiting = []
             costs = next_costs
 
         y_rounded = [turns[:, :WIDTH], turns[:, WIDTH : 2 * WIDTH]]
@@ -331,9 +342,10 @@ def tile_list_order_lane_cost_kernel(
             words = out_1[g].rearrange("p m t -> p (m t)").bitcast(I32)
             nc.sync.dma_start(out=words[:, cols], in_=y_codes[g][:, cols].bitcast(I32))
 
-        for step in range(2):
-            round_on_gpsimd(step, 0, BANK // 2)
-            round_on_gpsimd(step, BANK // 2, BANK)
+        round_on_gpsimd(0, 0, Y_EARLY)
+        round_on_gpsimd(0, Y_EARLY, BANK)
+        round_on_gpsimd(1, 0, BANK // 2)
+        round_on_gpsimd(1, BANK // 2, BANK)
         round_on_gpsimd(2, 0, Y_ON_GPSIMD)
         round_on_scalar(2, Y_ON_GPSIMD, BANK)
         round_on_scalar(last_step, 0, BANK - Y_ON_VECTOR)

@@ -145,10 +145,9 @@ def tile_list_order_lane_cost_kernel(
         first_product(0)
         load_words(2)
         gather_words(2)
-        for q in range(QUADS):
+        for r in range(QUAD_ROWS):
             nc.sync.dma_start(
-                out=w4_sc_raw[32 * q : 32 * q + QUAD_ROWS, :].bitcast(I32),
-                in_=w4_scales[0, QUAD_ROWS * q : QUAD_ROWS * (q + 1), :].bitcast(I32),
+                out=w4_sc_raw[r:P:32, :].bitcast(I32), in_=w4_scales[0, r :: QUAD_ROWS, :].bitcast(I32)
             )
         nc.sync.dma_start(out=bias[:], in_=b1.rearrange("(p t) -> p t", t=PACK))
         nc.vector.tensor_copy(
@@ -359,9 +358,9 @@ def tile_list_order_lane_cost_kernel(
             quantise_lanes(step, 0, BANK)
             store_words(1, slice((step - 2) * BANK, (step - 1) * BANK))
 
-        for q in range(QUADS):
-            queue = nc.scalar if q % 2 else nc.sync
+        for r in range(QUAD_ROWS):
+            queue = nc.scalar if r % 2 else nc.sync
             queue.dma_start(
-                out=out_2[:, QUAD_ROWS * q : QUAD_ROWS * (q + 1), :].bitcast(I32).rearrange("g r m -> r g m"),
-                in_=y_sc[32 * q : 32 * q + QUAD_ROWS, :].bitcast(I32).rearrange("r (g m) -> r g m", g=GROUPS),
+                out=out_2[:, r :: QUAD_ROWS, :].bitcast(I32).rearrange("g q m -> q g m"),
+                in_=y_sc[r:P:32, :].bitcast(I32).rearrange("q (g m) -> q g m", g=GROUPS),
             )

@@ -97,10 +97,6 @@ def tile_list_order_lane_cost_kernel(
         def quantise(codes, scales, rounded):
             nc.vector.quantize_mx(out=codes.bitcast(FP8X4), scales=scales, in_=rounded)
 
-        warm = keep.tile([P, 2], F32, name="warm")
-        nc.vector.memset(warm[:, 0:1], 0.0)
-        nc.scalar.activation(out=warm[:, 1:2], in_=warm[:, 0:1], func=ACT.Sigmoid)
-
         nc.gpsimd.memset(table_sc[:].bitcast(I32), 0)
         nc.gpsimd.memset(w4_sc_raw[:].bitcast(I32), 0)
 
@@ -135,10 +131,15 @@ def tile_list_order_lane_cost_kernel(
         nc.sync.dma_start(offsets[:], offs)
         load_words(1)
         for q in range(QUADS):
-            nc.sync.dma_start(
+            queue = nc.sync if q < QUADS // 2 else nc.scalar
+            queue.dma_start(
                 out=table_sc[32 * q : 32 * q + QUAD_ROWS * PASSES, :].bitcast(I32),
                 in_=tab_scales[:, QUAD_ROWS * q : QUAD_ROWS * (q + 1), :].bitcast(I32),
             )
+        warm = keep.tile([P, 2], F32, name="warm")
+        nc.vector.memset(warm[:, 0:1], 0.0)
+        nc.scalar.activation(out=warm[:, 1:2], in_=warm[:, 0:1], func=ACT.Sigmoid)
+
         gather_words(0)
         gather_words(1)
         nc.vector.tensor_copy(out=picked_sc[:], in_=table_sc[:].indirect(offsets[:]))

@@ -264,6 +264,7 @@ def tile_list_order_lane_cost_kernel(
         quantise(wc_codes[0][:], wc_sc[0], wc_rounded[0])
         minimum(3)
         quantise_h(2)
+        quantise_h(3)
 
         cells = []
         for step in range(len(steps)):
@@ -271,7 +272,7 @@ def tile_list_order_lane_cost_kernel(
             share = handed_on(("demand%d" if g else "share%d") % half, [P, PACK, BANK], F32)
             cells.append([share[:, t, :] for t in range(PACK)])
         cells[1][0] = handed_on("wc_codes1", [P, BANK], F32)[:]
-        cells[last_step][-1] = handed_on("y_sc", [P, BANK], F32)[:]
+        cells[last_step][-2] = handed_on("y_sc", [P, BANK], F32)[:]
         y = [raw_tile([P, PACK, BANK]) for step in range(len(steps))]
 
         for t in range(PACK):
@@ -282,7 +283,15 @@ def tile_list_order_lane_cost_kernel(
         nc.scalar.copy(
             out=dealt(wc_rounded[1])[:, m_piece : m_piece + m_scalar], in_=undealt(pieces[1])[:, :m_scalar]
         )
-        early = [(2, 0), (2, 1)]
+        nc.gpsimd.tensor_scalar(
+            out=wc_rounded[1].rearrange("p (t m j) -> p m t j", t=PACK, j=PACK)[:, m_piece + m_scalar :],
+            in0=pieces[1].rearrange("p j (m t) -> p m t j", t=PACK)[:, m_scalar:],
+            scalar1=1.0,
+            scalar2=-0.0,
+            op0=ALU.mult,
+            op1=ALU.add,
+        )
+        early = [(2, 0)]
         for step, t in early:
             share_plane(step, t)
         waiting = []
@@ -290,16 +299,6 @@ def tile_list_order_lane_cost_kernel(
             next_costs = []
             for t in range(PACK):
                 lanes_plane(step, t, costs[t])
-                if (step, t) == (0, 0):
-                    quantise_h(3)
-                    nc.gpsimd.tensor_scalar(
-                        out=wc_rounded[1].rearrange("p (t m j) -> p m t j", t=PACK, j=PACK)[:, m_piece + m_scalar :],
-                        in0=pieces[1].rearrange("p j (m t) -> p m t j", t=PACK)[:, m_scalar:],
-                        scalar1=1.0,
-                        scalar2=-0.0,
-                        op0=ALU.mult,
-                        op1=ALU.add,
-                    )
                 if (step, t) == (1, 1):
                     wc_codes.append(handed_on("wc_codes1", [P, K_PASS], U32))
                     quantise(wc_codes[1][:], wc_sc[1], wc_rounded[1])

@@ -30,9 +30,10 @@ RUN = 2
 WC_PIECES = 2
 WIDTH = PACK * BANK
 
-W1_ON_VECTOR = (0, 48, 80)
-WC_ON_GPSIMD = 32
-Y_ON_GPSIMD = 64
+W1_ON_VECTOR = (0, 48, 64)
+WC_ON_GPSIMD = 64
+Y_ON_GPSIMD = 160
+Y_MIDDLE = 128
 Y_EARLY = 128
 Y_ON_VECTOR = 128
 CHUNK = BANK // 2
@@ -155,7 +156,17 @@ def tile_list_order_lane_cost_kernel(
             out=w4_sc[:].rearrange("p (g t m) -> p g t m", g=GROUPS, t=PACK),
             in_=w4_sc_raw[:].rearrange("p (g m t) -> p g t m", g=GROUPS, t=PACK),
         )
+        def load_stock(t):
+            nc.sync.dma_start(out=stock[t][:], in_=gT.rearrange("(p t) c -> t p c", t=PACK)[t])
+
+        def gather_stock(t, first, width):
+            nc.vector.tensor_copy(
+                out=stock_picked[:, t, first : first + width], in_=stock[t][:].indirect(entries(first, width))
+            )
+
         first_product(1)
+        load_stock(0)
+        gather_stock(0, 0, S)
         first_product(2)
 
         demand = [handed_on("demand%d" % half, [P, PACK, BANK], F32) for half in range(HALVES)]
@@ -165,13 +176,8 @@ def tile_list_order_lane_cost_kernel(
                     out=demand[half][:, t, :], in_=acc[half][t][:], func=ACT.Relu, bias=bias[:, t : t + 1]
                 )
 
-        def gather_stock(t, first, width):
-            nc.vector.tensor_copy(
-                out=stock_picked[:, t, first : first + width], in_=stock[t][:].indirect(entries(first, width))
-            )
-
-        for t in range(PACK):
-            nc.sync.dma_start(out=stock[t][:], in_=gT.rearrange("(p t) c -> t p c", t=PACK)[t])
+        for t in range(1, PACK):
+            load_stock(t)
             if t < PACK - 1:
                 gather_stock(t, 0, S)
 
@@ -189,15 +195,15 @@ def tile_list_order_lane_cost_kernel(
             turns[:, h_last : h_last + PACK * CHUNK],
         ]
 
+        m_piece = P // WC_PIECES
+        pieces = load_weight(wc[:, :K_PASS], WC_PIECES)
+        for i in range(WC_PIECES):
+            nc.scalar.copy(out=dealt(wc_rounded[0])[:, i * m_piece : (i + 1) * m_piece], in_=undealt(pieces[i]))
         nc.sync.dma_start(out=w4_raw[:].bitcast(I32), in_=w4_words[0].bitcast(I32))
         nc.scalar.copy(
             out=w4_codes[:].bitcast(U16).rearrange("p (g t m) -> p g m t", g=GROUPS, t=PACK),
             in_=w4_raw[:].bitcast(U16).rearrange("p (g m t) -> p g m t", g=GROUPS, t=PACK),
         )
-        m_piece = P // WC_PIECES
-        pieces = load_weight(wc[:, :K_PASS], WC_PIECES)
-        for i in range(WC_PIECES):
-            nc.scalar.copy(out=dealt(wc_rounded[0])[:, i * m_piece : (i + 1) * m_piece], in_=undealt(pieces[i]))
         pieces = load_weight(wc[:, K_PASS:], WC_PIECES)
         nc.scalar.copy(out=dealt(wc_rounded[1])[:, :m_piece], in_=undealt(pieces[0]))
 
@@ -279,13 +285,9 @@ def tile_list_order_lane_cost_kernel(
             share_plane(0, t)
         costs = [cost_plane(0, t) for t in range(PACK)]
 
-        m_scalar = P - WC_ON_GPSIMD - m_piece
-        nc.scalar.copy(
-            out=dealt(wc_rounded[1])[:, m_piece : m_piece + m_scalar], in_=undealt(pieces[1])[:, :m_scalar]
-        )
         nc.gpsimd.tensor_scalar(
-            out=wc_rounded[1].rearrange("p (t m j) -> p m t j", t=PACK, j=PACK)[:, m_piece + m_scalar :],
-            in0=pieces[1].rearrange("p j (m t) -> p m t j", t=PACK)[:, m_scalar:],
+            out=wc_rounded[1].rearrange("p (t m j) -> p m t j", t=PACK, j=PACK)[:, m_piece:],
+            in0=pieces[1].rearrange("p j (m t) -> p m t j", t=PACK),
             scalar1=1.0,
             scalar2=-0.0,
             op0=ALU.mult,
@@ -343,8 +345,8 @@ def tile_list_order_lane_cost_kernel(
 
         round_on_gpsimd(0, 0, Y_EARLY)
         round_on_gpsimd(0, Y_EARLY, BANK)
-        round_on_gpsimd(1, 0, BANK // 2)
-        round_on_gpsimd(1, BANK // 2, BANK)
+        round_on_gpsimd(1, 0, BANK - Y_MIDDLE)
+        round_on_scalar(1, BANK - Y_MIDDLE, BANK)
         round_on_gpsimd(2, 0, Y_ON_GPSIMD)
         round_on_scalar(2, Y_ON_GPSIMD, BANK)
         round_on_scalar(last_step, 0, BANK - Y_ON_VECTOR)

@@ -32,7 +32,7 @@ WIDTH = PACK * BANK
 
 W1_ON_VECTOR = (0, 48, 64)
 WC_ON_GPSIMD = 64
-Y_ON_GPSIMD = 160
+Y_ON_GPSIMD = 96
 Y_MIDDLE = 128
 Y_EARLY = 128
 Y_ON_VECTOR = 128
@@ -186,14 +186,9 @@ def tile_list_order_lane_cost_kernel(
         wc_first = keep.tile([P, WIDTH], BF16, name="wc_first", align_bytes=64)
         wc_start = PACK * Y_EARLY
         wc_rounded = [wc_first[:], turns[:, wc_start : wc_start + WIDTH]]
-        h_middle = keep.tile([P, 2, PACK * CHUNK], BF16, name="h_middle", align_bytes=64)
+        h_middle = keep.tile([P, 3, PACK * CHUNK], BF16, name="h_middle", align_bytes=64)
         h_last = wc_start + WIDTH - lap_gpsimd
-        h_rounded = [
-            stock_picked[:, PACK - 1, BANK:].bitcast(BF16),
-            h_middle[:, 0, :],
-            h_middle[:, 1, :],
-            turns[:, h_last : h_last + PACK * CHUNK],
-        ]
+        h_rounded = [h_middle[:, c, :] for c in range(3)] + [turns[:, h_last : h_last + PACK * CHUNK]]
 
         m_piece = P // WC_PIECES
         pieces = load_weight(wc[:, :K_PASS], WC_PIECES)
@@ -260,11 +255,11 @@ def tile_list_order_lane_cost_kernel(
             nc.vector.tensor_tensor(out=y[step][:, t, :], in0=cells[step][t], in1=cost[:], op=ALU.mult)
             nc.sync.dma_start(out=rows.rearrange("(p t) c -> t p c", t=PACK)[t], in_=y[step][:, t, :])
 
-        for work in (lambda c: gather_stock(PACK - 1, c * CHUNK, CHUNK), minimum, quantise_h):
+        for half in range(HALVES):
+            gather_stock(PACK - 1, half * BANK, BANK)
+        for work in (minimum, quantise_h):
             work(0)
             work(1)
-        gather_stock(PACK - 1, 2 * CHUNK, CHUNK)
-        gather_stock(PACK - 1, 3 * CHUNK, CHUNK)
         minimum(2)
         wc_codes = [keep.tile([P, K_PASS], U32, name="wc_codes0", align_bytes=64)]
         quantise(wc_codes[0][:], wc_sc[0], wc_rounded[0])

@@ -26,7 +26,7 @@ QUAD_ROWS = 4
 LIST_ROWS = 16
 BANK = 512
 HALVES = S // BANK
-RUN = 2
+RUN = 4
 WC_PIECES = 2
 WIDTH = PACK * BANK
 

@@ -137,9 +137,6 @@ def tile_list_order_lane_cost_kernel(
                 out=table_sc[32 * q : 32 * q + QUAD_ROWS * PASSES, :].bitcast(I32),
                 in_=tab_scales[:, QUAD_ROWS * q : QUAD_ROWS * (q + 1), :].bitcast(I32),
             )
-        warm = keep.tile([P, 2], F32, name="warm")
-        nc.vector.memset(warm[:, 0:1], 0.0)
-        nc.scalar.activation(out=warm[:, 1:2], in_=warm[:, 0:1], func=ACT.Sigmoid)
 
         gather_words(0)
         gather_words(1)

@@ -30,7 +30,7 @@ RUN = 4
 WC_PIECES = 2
 WIDTH = PACK * BANK
 
-W1_ON_VECTOR = (0, 48, 64)
+W1_ON_GPSIMD = (0, 48, 48)
 WC_ON_GPSIMD = 64
 Y_ON_GPSIMD = 96
 Y_MIDDLE = 128
@@ -59,7 +59,7 @@ def tile_list_order_lane_cost_kernel(
         bias = keep.tile([P, PACK], F32, name="bias")
         table = [keep.tile([P, T], U32, name="table%d" % a) for a in range(PASSES)]
         table_sc = keep.tile([P, T], U8, name="table_sc")
-        picked = [keep.tile([P, S], U32, name="picked%d" % a, align_bytes=64) for a in range(PASSES)]
+        picked = [keep.tile([P, S], U32, name="picked%d" % a, align_bytes=64) for a in range(PASSES - 1)]
         picked_sc = keep.tile([P, S], U8, name="picked_sc", align_bytes=64)
         stock = [keep.tile([P, T], F32, name="stock%d" % t) for t in range(PACK)]
         stock_picked = keep.tile([P, PACK, S], F32, name="stock_picked", align_bytes=64)
@@ -95,6 +95,16 @@ def tile_list_order_lane_cost_kernel(
         def dealt(rounded):
             return rounded.rearrange("p (t m j) -> p m j t", t=PACK, j=PACK)
 
+        def deal_on_gpsimd(rounded, m, raw):
+            nc.gpsimd.tensor_scalar(
+                out=rounded.rearrange("p (t m j) -> p m t j", t=PACK, j=PACK)[:, m:],
+                in0=raw.rearrange("p j (m t) -> p m t j", t=PACK),
+                scalar1=1.0,
+                scalar2=-0.0,
+                op0=ALU.mult,
+                op1=ALU.add,
+            )
+
         def quantise(codes, scales, rounded):
             nc.vector.quantize_mx(out=codes.bitcast(FP8X4), scales=scales, in_=rounded)
 
@@ -108,11 +118,11 @@ def tile_list_order_lane_cost_kernel(
 
         def first_product(a):
             raw = load_weight(w1[a * K_PASS : (a + 1) * K_PASS, :], 1)[0]
-            rounded = ring.tile([P, WIDTH], BF16, name="w1_rounded", bufs=2, align_bytes=64)
-            m = P - W1_ON_VECTOR[a]
+            rounded = handed_on("w1_rounded%d" % a, [P, WIDTH], BF16)
+            m = P - W1_ON_GPSIMD[a]
             nc.scalar.copy(out=dealt(rounded[:])[:, :m], in_=undealt(raw)[:, :m])
             if m < P:
-                nc.vector.tensor_copy(out=dealt(rounded[:])[:, m:], in_=undealt(raw)[:, m:])
+                deal_on_gpsimd(rounded[:], m, raw[:, :, PACK * m :])
             quantise(w1_codes[a][:], w1_sc[a][:], rounded[:])
             for half in range(HALVES):
                 cols = slice(half * BANK, (half + 1) * BANK)
@@ -143,6 +153,7 @@ def tile_list_order_lane_cost_kernel(
         nc.vector.tensor_copy(out=picked_sc[:], in_=table_sc[:].indirect(offsets[:]))
         first_product(0)
         load_words(2)
+        picked.append(handed_on("w1_rounded0", [P, S], U32))
         gather_words(2)
         for r in range(QUAD_ROWS):
             nc.sync.dma_start(

@@ -30,7 +30,7 @@ RUN = 4
 WC_PIECES = 2
 WIDTH = PACK * BANK
 
-W1_ON_GPSIMD = (0, 48, 48)
+W1_ON_VECTOR = (0, 32, 64)
 WC_ON_GPSIMD = 64
 Y_ON_GPSIMD = 96
 Y_MIDDLE = 128
@@ -59,7 +59,7 @@ def tile_list_order_lane_cost_kernel(
         bias = keep.tile([P, PACK], F32, name="bias")
         table = [keep.tile([P, T], U32, name="table%d" % a) for a in range(PASSES)]
         table_sc = keep.tile([P, T], U8, name="table_sc")
-        picked = [keep.tile([P, S], U32, name="picked%d" % a, align_bytes=64) for a in range(PASSES - 1)]
+        picked = [keep.tile([P, S], U32, name="picked%d" % a, align_bytes=64) for a in range(PASSES)]
         picked_sc = keep.tile([P, S], U8, name="picked_sc", align_bytes=64)
         stock = [keep.tile([P, T], F32, name="stock%d" % t) for t in range(PACK)]
         stock_picked = keep.tile([P, PACK, S], F32, name="stock_picked", align_bytes=64)
@@ -95,21 +95,11 @@ def tile_list_order_lane_cost_kernel(
         def dealt(rounded):
             return rounded.rearrange("p (t m j) -> p m j t", t=PACK, j=PACK)
 
-        def deal_on_gpsimd(rounded, m, raw):
-            nc.gpsimd.tensor_scalar(
-                out=rounded.rearrange("p (t m j) -> p m t j", t=PACK, j=PACK)[:, m:],
-                in0=raw.rearrange("p j (m t) -> p m t j", t=PACK),
-                scalar1=1.0,
-                scalar2=-0.0,
-                op0=ALU.mult,
-                op1=ALU.add,
-            )
-
         def quantise(codes, scales, rounded):
             nc.vector.quantize_mx(out=codes.bitcast(FP8X4), scales=scales, in_=rounded)
 
         nc.gpsimd.memset(table_sc[:].bitcast(I32), 0)
-        nc.gpsimd.memset(w4_sc_raw[:].bitcast(I32), 0)
+        nc.vector.memset(w4_sc_raw[:].bitcast(I32), 0)
 
         acc = [[psum.tile([P, BANK], F32, name=tag) for t in range(PACK)] for tag in ("route", "cost")]
 
@@ -118,11 +108,11 @@ def tile_list_order_lane_cost_kernel(
 
         def first_product(a):
             raw = load_weight(w1[a * K_PASS : (a + 1) * K_PASS, :], 1)[0]
-            rounded = handed_on("w1_rounded%d" % a, [P, WIDTH], BF16)
-            m = P - W1_ON_GPSIMD[a]
+            rounded = ring.tile([P, WIDTH], BF16, name="w1_rounded", bufs=2, align_bytes=64)
+            m = P - W1_ON_VECTOR[a]
             nc.scalar.copy(out=dealt(rounded[:])[:, :m], in_=undealt(raw)[:, :m])
             if m < P:
-                deal_on_gpsimd(rounded[:], m, raw[:, :, PACK * m :])
+                nc.vector.tensor_copy(out=dealt(rounded[:])[:, m:], in_=undealt(raw)[:, m:])
             quantise(w1_codes[a][:], w1_sc[a][:], rounded[:])
             for half in range(HALVES):
                 cols = slice(half * BANK, (half + 1) * BANK)
@@ -142,24 +132,28 @@ def tile_list_order_lane_cost_kernel(
         nc.sync.dma_start(offsets[:], offs)
         load_words(1)
         for q in range(QUADS):
-            queue = nc.sync if q < QUADS // 2 else nc.scalar
+            queue = nc.sync if q < QUADS // 2 else nc.gpsimd
             queue.dma_start(
                 out=table_sc[32 * q : 32 * q + QUAD_ROWS * PASSES, :].bitcast(I32),
                 in_=tab_scales[:, QUAD_ROWS * q : QUAD_ROWS * (q + 1), :].bitcast(I32),
             )
 
+        nc.sync.dma_start(out=bias[:], in_=b1.rearrange("(p t) -> p t", t=PACK))
+
+        def load_w4_scales(rows):
+            for r in rows:
+                nc.sync.dma_start(
+                    out=w4_sc_raw[r:P:32, :].bitcast(I32), in_=w4_scales[0, r :: QUAD_ROWS, :].bitcast(I32)
+                )
+
         gather_words(0)
         gather_words(1)
         nc.vector.tensor_copy(out=picked_sc[:], in_=table_sc[:].indirect(offsets[:]))
         first_product(0)
+        load_w4_scales(range(1))
         load_words(2)
-        picked.append(handed_on("w1_rounded0", [P, S], U32))
         gather_words(2)
-        for r in range(QUAD_ROWS):
-            nc.sync.dma_start(
-                out=w4_sc_raw[r:P:32, :].bitcast(I32), in_=w4_scales[0, r :: QUAD_ROWS, :].bitcast(I32)
-            )
-        nc.sync.dma_start(out=bias[:], in_=b1.rearrange("(p t) -> p t", t=PACK))
+        load_w4_scales(range(1, QUAD_ROWS))
         nc.vector.tensor_copy(
             out=w4_sc[:].rearrange("p (g t m) -> p g t m", g=GROUPS, t=PACK),
             in_=w4_sc_raw[:].rearrange("p (g m t) -> p g t m", g=GROUPS, t=PACK),

from contextlib import ExitStack

import concourse.mybir as mybir

K, T, S, H, N = 1536, 2048, 1024, 512, 1024
FLOPS = 2 * K * H * S + 2 * 2 * H * N * S

F32 = mybir.dt.float32
BF16 = mybir.dt.bfloat16
I32 = mybir.dt.int32
U32 = mybir.dt.uint32
U16 = mybir.dt.uint16
U8 = mybir.dt.uint8
FP8X4 = mybir.dt.float8_e4m3fn_x4
FP4X4 = mybir.dt.float4_e2m1fn_x4
ACT = mybir.ActivationFunctionType
ALU = mybir.AluOpType

P = 128
PACK = 4
K_PASS = P * PACK
PASSES = K // K_PASS
GROUPS = N // K_PASS
QUADS = 4
QUAD_ROWS = 4
LIST_ROWS = 16
BANK = 512
HALVES = S // BANK
RUN = 4
WC_PIECES = 2
WIDTH = PACK * BANK

W1_ON_VECTOR = (0, 32, 64)
WC_ON_GPSIMD = 64
Y_ON_GPSIMD = 96
Y_MIDDLE = 128
Y_EARLY = 128
Y_ON_VECTOR = 128
CHUNK = BANK // 2
RAW_BUFS = 4


def tile_list_order_lane_cost_kernel(
    tc, tab_words, tab_scales, offs, w1, b1, gT, w4_words, w4_scales, wc, out_0, out_1, out_2
):
    nc = tc.nc
    with ExitStack() as ctx:
        keep = ctx.enter_context(tc.tile_pool(name="keep", bufs=1))
        ring = ctx.enter_context(tc.tile_pool(name="ring", bufs=1))
        psum = ctx.enter_context(tc.psum_pool(name="psum", bufs=PACK))

        def handed_on(tag, shape, dtype):
            return ring.tile(shape, dtype, name=tag, bufs=1, align_bytes=64)

        def raw_tile(shape):
            return ring.tile(shape, F32, name="raw", bufs=RAW_BUFS)

        offsets = keep.tile([P, S // LIST_ROWS], U16, name="offsets")
        bias = keep.tile([P, PACK], F32, name="bias")
        table = [keep.tile([P, T], U32, name="table%d" % a) for a in range(PASSES)]
        table_sc = keep.tile([P, T], U8, name="table_sc")
        picked = [keep.tile([P, S], U32, name="picked%d" % a, align_bytes=64) for a in range(PASSES)]
        picked_sc = keep.tile([P, S], U8, name="picked_sc", align_bytes=64)
        stock = [keep.tile([P, T], F32, name="stock%d" % t) for t in range(PACK)]
        stock_picked = keep.tile([P, PACK, S], F32, name="stock_picked", align_bytes=64)
        w4_raw = keep.tile([P, 2 * N], U8, name="w4_raw")
        w4_sc_raw = keep.tile([P, N], U8, name="w4_sc_raw")
        w4_codes = keep.tile([P, 2 * N], U8, name="w4_codes", align_bytes=64)
        w4_sc = keep.tile([P, N], U8, name="w4_sc", align_bytes=64)
        w1_codes = [keep.tile([P, K_PASS], U32, name="w1_codes%d" % a, align_bytes=64) for a in range(PASSES)]
        w1_sc = [keep.tile([P, K_PASS], U8, name="w1_sc%d" % a, align_bytes=64) for a in range(PASSES)]
        h_codes = [keep.tile([P, BANK], U32, name="h_codes%d" % half, align_bytes=64) for half in range(HALVES)]
        h_sc = [keep.tile([P, BANK], U8, name="h_sc%d" % half, align_bytes=64)[:] for half in range(HALVES)]
        wc_sc = [keep.tile([P, K_PASS], U8, name="wc_sc%d" % g, align_bytes=64)[:] for g in range(GROUPS)]
        y_codes = [keep.tile([P, S], U32, name="y_codes%d" % g, align_bytes=64) for g in range(GROUPS)]

        def load_words(a):
            src = tab_words[a].rearrange("p n i -> p (n i)").bitcast(I32)
            nc.sync.dma_start(out=table[a][:].bitcast(I32), in_=src)

        def entries(first, width):
            return offsets[:, first // LIST_ROWS : (first + width) // LIST_ROWS]

        def load_weight(rows, pieces):
            width = K_PASS // pieces
            raw = raw_tile([P, pieces, PACK, width])
            for i in range(pieces):
                src = rows[:, i * width : (i + 1) * width]
                nc.sync.dma_start(out=raw[:, i], in_=src.rearrange("(p j) c -> p j c", j=PACK))
            return [raw[:, i] for i in range(pieces)]

        def undealt(raw):
            return raw.rearrange("p j (m t) -> p m j t", t=PACK)

        def dealt(rounded):
            return rounded.rearrange("p (t m j) -> p m j t", t=PACK, j=PACK)

        def quantise(codes, scales, rounded):
            nc.vector.quantize_mx(out=codes.bitcast(FP8X4), scales=scales, in_=rounded)

        nc.gpsimd.memset(table_sc[:].bitcast(I32), 0)
        nc.vector.memset(w4_sc_raw[:].bitcast(I32), 0)

        acc = [[psum.tile([P, BANK], F32, name=tag) for t in range(PACK)] for tag in ("route", "cost")]

        def gather_words(a):
            nc.vector.tensor_copy(out=picked[a][:], in_=table[a][:].indirect(offsets[:]))

        def first_product(a):
            raw = load_weight(w1[a * K_PASS : (a + 1) * K_PASS, :], 1)[0]
            rounded = ring.tile([P, WIDTH], BF16, name="w1_rounded", bufs=2, align_bytes=64)
            m = P - W1_ON_VECTOR[a]
            nc.scalar.copy(out=dealt(rounded[:])[:, :m], in_=undealt(raw)[:, :m])
            if m < P:
                nc.vector.tensor_copy(out=dealt(rounded[:])[:, m:], in_=undealt(raw)[:, m:])
            quantise(w1_codes[a][:], w1_sc[a][:], rounded[:])
            for half in range(HALVES):
                cols = slice(half * BANK, (half + 1) * BANK)
                for t in range(PACK):
                    places = slice(t * P, (t + 1) * P)
                    nc.tensor.matmul_mx(
                        out=acc[half][t][:],
                        lhsT=w1_codes[a][:, places].bitcast(FP8X4),
                        lhsT_scale=w1_sc[a][:, places],
                        rhs=picked[a][:, cols].bitcast(FP8X4),
                        rhs_scale=picked_sc[QUAD_ROWS * a :, cols],
                        start=(a == 0),
                        stop=(a == PASSES - 1),
                    )

        load_words(0)
        nc.sync.dma_start(offsets[:], offs)
        load_words(1)
        for q in range(QUADS):
            queue = nc.sync if q < QUADS // 2 else nc.gpsimd
            queue.dma_start(
                out=table_sc[32 * q : 32 * q + QUAD_ROWS * PASSES, :].bitcast(I32),
                in_=tab_scales[:, QUAD_ROWS * q : QUAD_ROWS * (q + 1), :].bitcast(I32),
            )

        nc.sync.dma_start(out=bias[:], in_=b1.rearrange("(p t) -> p t", t=PACK))

        def load_w4_scales(rows):
            for r in rows:
                nc.sync.dma_start(
                    out=w4_sc_raw[r:P:32, :].bitcast(I32), in_=w4_scales[0, r :: QUAD_ROWS, :].bitcast(I32)
                )

        gather_words(0)
        gather_words(1)
        nc.vector.tensor_copy(out=picked_sc[:], in_=table_sc[:].indirect(offsets[:]))
        first_product(0)
        load_w4_scales(range(1))
        load_words(2)
        gather_words(2)
        load_w4_scales(range(1, QUAD_ROWS))
        nc.vector.tensor_copy(
            out=w4_sc[:].rearrange("p (g t m) -> p g t m", g=GROUPS, t=PACK),
            in_=w4_sc_raw[:].rearrange("p (g m t) -> p g t m", g=GROUPS, t=PACK),
        )
        def load_stock(t):
            nc.sync.dma_start(out=stock[t][:], in_=gT.rearrange("(p t) c -> t p c", t=PACK)[t])

        def gather_stock(t, first, width):
            nc.vector.tensor_copy(
                out=stock_picked[:, t, first : first + width], in_=stock[t][:].indirect(entries(first, width))
            )

        first_product(1)
        load_stock(0)
        gather_stock(0, 0, S)
        first_product(2)

        demand = [handed_on("demand%d" % half, [P, PACK, BANK], F32) for half in range(HALVES)]
        for half in range(HALVES):
            for t in range(PACK):
                nc.scalar.activation(
                    out=demand[half][:, t, :], in_=acc[half][t][:], func=ACT.Relu, bias=bias[:, t : t + 1]
                )

        for t in range(1, PACK):
            load_stock(t)
            if t < PACK - 1:
                gather_stock(t, 0, S)

        lap_gpsimd = PACK * WC_ON_GPSIMD
        turns = keep.tile([P, 2 * WIDTH], BF16, name="turns", align_bytes=64)
        wc_first = keep.tile([P, WIDTH], BF16, name="wc_first", align_bytes=64)
        wc_start = PACK * Y_EARLY
        wc_rounded = [wc_first[:], turns[:, wc_start : wc_start + WIDTH]]
        h_middle = keep.tile([P, 3, PACK * CHUNK], BF16, name="h_middle", align_bytes=64)
        h_last = wc_start + WIDTH - lap_gpsimd
        h_rounded = [h_middle[:, c, :] for c in range(3)] + [turns[:, h_last : h_last + PACK * CHUNK]]

        m_piece = P // WC_PIECES
        pieces = load_weight(wc[:, :K_PASS], WC_PIECES)
        for i in range(WC_PIECES):
            nc.scalar.copy(out=dealt(wc_rounded[0])[:, i * m_piece : (i + 1) * m_piece], in_=undealt(pieces[i]))
        nc.sync.dma_start(out=w4_raw[:].bitcast(I32), in_=w4_words[0].bitcast(I32))
        nc.scalar.copy(
            out=w4_codes[:].bitcast(U16).rearrange("p (g t m) -> p g m t", g=GROUPS, t=PACK),
            in_=w4_raw[:].bitcast(U16).rearrange("p (g m t) -> p g m t", g=GROUPS, t=PACK),
        )
        pieces = load_weight(wc[:, K_PASS:], WC_PIECES)
        nc.scalar.copy(out=dealt(wc_rounded[1])[:, :m_piece], in_=undealt(pieces[0]))

        def by_runs(planes):
            return planes.rearrange("p t (c i) -> p c t i", i=RUN)

        def woven_by_runs(rounded):
            return rounded.rearrange("p (c i t) -> p c t i", i=RUN, t=PACK)

        def minimum(c):
            half, c0 = divmod(c * CHUNK, BANK)
            nc.vector.tensor_tensor(
                out=woven_by_runs(h_rounded[c]),
                in0=by_runs(demand[half][:, :, c0 : c0 + CHUNK]),
                in1=by_runs(stock_picked[:, :, c * CHUNK : (c + 1) * CHUNK]),
                op=ALU.min,
            )

        def quantise_h(c):
            half, c0 = divmod(c * CHUNK, BANK)
            quantise(h_codes[half][:, c0 : c0 + CHUNK], h_sc[half][:, c0 : c0 + CHUNK], h_rounded[c])

        steps = [(g, half) for g in range(GROUPS) for half in range(HALVES)]
        last_step = len(steps) - 1

        def second_product(tag, codes, scales, half):
            bank = psum.tile([P, BANK], F32, name=tag)
            nc.tensor.matmul_mx(
                out=bank[:],
                lhsT=codes,
                lhsT_scale=scales,
                rhs=h_codes[half][:].bitcast(FP8X4),
                rhs_scale=h_sc[half],
                start=True,
                stop=True,
            )
            return bank

        def share_plane(step, t):
            g, half = steps[step]
            first = g * K_PASS + t * P
            codes = w4_codes[:, 2 * first : 2 * (first + P)].bitcast(FP4X4)
            route = second_product("route", codes, w4_sc[:, first : first + P], half)
            nc.scalar.activation(out=cells[step][t], in_=route[:], func=ACT.Sigmoid)

        def cost_plane(step, t):
            g, half = steps[step]
            places = slice(t * P, (t + 1) * P)
            return second_product("cost", wc_codes[g][:, places].bitcast(FP8X4), wc_sc[g][:, places], half)

        def lanes_plane(step, t, cost):
            g, half = steps[step]
            rows = out_0[g * K_PASS : (g + 1) * K_PASS, half * BANK : (half + 1) * BANK]
            nc.vector.tensor_tensor(out=y[step][:, t, :], in0=cells[step][t], in1=cost[:], op=ALU.mult)
            nc.sync.dma_start(out=rows.rearrange("(p t) c -> t p c", t=PACK)[t], in_=y[step][:, t, :])

        for half in range(HALVES):
            gather_stock(PACK - 1, half * BANK, BANK)
        for work in (minimum, quantise_h):
            work(0)
            work(1)
        minimum(2)
        wc_codes = [keep.tile([P, K_PASS], U32, name="wc_codes0", align_bytes=64)]
        quantise(wc_codes[0][:], wc_sc[0], wc_rounded[0])
        minimum(3)
        quantise_h(2)
        quantise_h(3)

        cells = []
        for step in range(len(steps)):
            g, half = steps[step]
            share = handed_on(("demand%d" if g else "share%d") % half, [P, PACK, BANK], F32)
            cells.append([share[:, t, :] for t in range(PACK)])
        cells[1][0] = handed_on("wc_codes1", [P, BANK], F32)[:]
        cells[last_step][-2] = handed_on("y_sc", [P, BANK], F32)[:]
        y = [raw_tile([P, PACK, BANK]) for step in range(len(steps))]

        for t in range(PACK):
            share_plane(0, t)
        costs = [cost_plane(0, t) for t in range(PACK)]

        nc.gpsimd.tensor_scalar(
            out=wc_rounded[1].rearrange("p (t m j) -> p m t j", t=PACK, j=PACK)[:, m_piece:],
            in0=pieces[1].rearrange("p j (m t) -> p m t j", t=PACK),
            scalar1=1.0,
            scalar2=-0.0,
            op0=ALU.mult,
            op1=ALU.add,
        )
        early = [(2, 0)]
        for step, t in early:
            share_plane(step, t)
        waiting = []
        for step in range(len(steps)):
            next_costs = []
            for t in range(PACK):
                lanes_plane(step, t, costs[t])
                if (step, t) == (1, 1):
                    wc_codes.append(handed_on("wc_codes1", [P, K_PASS], U32))
                    quantise(wc_codes[1][:], wc_sc[1], wc_rounded[1])
                if step < last_step:
                    if (step + 1, t) not in early:
                        share_plane(step + 1, t)
                    waiting.append(t)
                    if steps[step + 1][0] < len(wc_codes):
                        next_costs += [cost_plane(step + 1, u) for u in waiting]
                        waiting = []
            costs = next_costs

        y_rounded = [turns[:, :WIDTH], turns[:, WIDTH : 2 * WIDTH]]
        for step in range(2, len(steps)):
            y_rounded.append(keep.tile([P, WIDTH], BF16, name="y_rounded%d" % step, align_bytes=64))
        y_sc = handed_on("y_sc", [P, GROUPS * S], U8)

        def round_on_gpsimd(step, c0, c1):
            nc.gpsimd.tensor_scalar(
                out=y_rounded[step][:, PACK * c0 : PACK * c1].rearrange("p (c t) -> p c t", t=PACK),
                in0=y[step][:, :, c0:c1].rearrange("p t c -> p c t"),
                scalar1=1.0,
                scalar2=-0.0,
                op0=ALU.mult,
                op1=ALU.add,
            )

        def round_on_scalar(step, c0, c1):
            out = woven_by_runs(y_rounded[step][:, PACK * c0 : PACK * c1])
            nc.scalar.copy(out=out, in_=by_runs(y[step][:, :, c0:c1]))

        def quantise_lanes(step, c0, c1):
            g, half = steps[step]
            first, end = half * BANK + c0, half * BANK + c1
            quantise(
                y_codes[g][:, first:end], y_sc[:, g * S + first : g * S + end], y_rounded[step][:, PACK * c0 : PACK * c1]
            )

        def store_words(g, cols):
            words = out_1[g].rearrange("p m t -> p (m t)").bitcast(I32)
            nc.sync.dma_start(out=words[:, cols], in_=y_codes[g][:, cols].bitcast(I32))

        round_on_gpsimd(0, 0, Y_EARLY)
        round_on_gpsimd(0, Y_EARLY, BANK)
        round_on_gpsimd(1, 0, BANK - Y_MIDDLE)
        round_on_scalar(1, BANK - Y_MIDDLE, BANK)
        round_on_gpsimd(2, 0, Y_ON_GPSIMD)
        round_on_scalar(2, Y_ON_GPSIMD, BANK)
        round_on_scalar(last_step, 0, BANK - Y_ON_VECTOR)
        quantise(y_codes[0][:], y_sc[:, :S], turns[:, : 2 * WIDTH])
        store_words(0, slice(0, S))
        nc.vector.tensor_copy(
            out=woven_by_runs(y_rounded[last_step][:, PACK * (BANK - Y_ON_VECTOR) :]),
            in_=by_runs(y[last_step][:, :, BANK - Y_ON_VECTOR :]),
        )
        for step in range(2, len(steps)):
            quantise_lanes(step, 0, BANK)
            store_words(1, slice((step - 2) * BANK, (step - 1) * BANK))

        for r in range(QUAD_ROWS):
            queue = nc.scalar if r % 2 else nc.sync
            queue.dma_start(
                out=out_2[:, r :: QUAD_ROWS, :].bitcast(I32).rearrange("g q m -> q g m"),
                in_=y_sc[r:P:32, :].bitcast(I32).rearrange("q (g m) -> q g m", g=GROUPS),
            )
